import numpy as np
import ml_dtypes


def mxq(x, axis, fmt="e4m3"):
    dtype, down = {"e4m3": (ml_dtypes.float8_e4m3fn, 7), "e5m2": (ml_dtypes.float8_e5m2, 14)}[fmt]
    v = np.moveaxis(np.asarray(x, np.float32).astype(ml_dtypes.bfloat16).astype(np.float64), axis, -1)
    blocks = v.reshape(v.shape[:-1] + (-1, 32))
    amax = np.abs(blocks).max(-1, keepdims=True)
    byte = np.maximum(np.where(amax > 0, np.frexp(amax)[1] - 1 + 127, 0) - down, 1)
    scale = np.exp2(byte - 127.0)
    codes = (blocks / scale).astype(np.float32).astype(dtype).astype(np.float64)
    return np.moveaxis((codes * scale).reshape(v.shape), -1, axis)


WIDE = False


def mx_kscale(k):
    if not WIDE:
        return np.ones(k)
    levels = np.array([10, -10, 5, -5, 0])
    if k % 512:
        return np.exp2(np.random.permutation(np.resize(levels, k // 32))).repeat(32)
    a = np.empty((k // 512, 16))
    for p in range(k // 512):
        a[p, :8] = np.random.permutation(np.resize(levels, 8))
        for g in range(8):
            far = levels[np.abs(levels - a[p, g]) >= 10]
            a[p, g + 8] = far[np.random.randint(len(far))]
    return np.exp2(a.ravel()).repeat(32)


def f64(x):
    return np.asarray(x).astype(np.float64)


def striped(idx):
    return np.tile(idx.reshape(-1, 16).T, (8, 1)).astype(np.uint16)


def unstriped(offs):
    return offs[:16].T.reshape(-1).astype(np.int64)


E2M1 = np.array([0.0, 0.5, 1.0, 1.5, 2.0, 3.0, 4.0, 6.0, -0.0, -0.5, -1.0, -1.5, -2.0, -3.0, -4.0, -6.0])


def pack_weight(w, fmt):
    k, n = w.shape
    w = f64(np.asarray(w, np.float32).astype(ml_dtypes.bfloat16)).reshape(k // 32, 32, n)
    amax = np.abs(w).max(1)
    if fmt == "e4m3":
        byte = np.frexp(amax)[1] - 1 + 127 - 7
    else:
        mant, ex = np.frexp(amax / 6.0)
        byte = np.where(mant > 0.5, ex, ex - 1) + 127
    byte = np.clip(np.where(amax > 0, byte, 1), 1, 254)
    scaled = (w * np.exp2(127.0 - byte)[:, None, :]).reshape(k, n).astype(np.float32)
    by_word = np.ascontiguousarray(scaled.reshape(k // 512, 128, 4, n).transpose(0, 1, 3, 2))
    if fmt == "e4m3":
        words = by_word.astype(ml_dtypes.float8_e4m3fn).view(np.uint8)
    else:
        c = by_word.astype(ml_dtypes.float4_e2m1fn).view(np.uint8) & 0xF
        words = (c[..., 0::2] | (c[..., 1::2] << 4)).reshape(k // 512, 128, 2 * n)
    return np.ascontiguousarray(words), np.ascontiguousarray(byte.astype(np.uint8).reshape(k // 512, 16, n))


def unpack_weight(words, scales, fmt):
    g, _, n = scales.shape
    words = np.ascontiguousarray(words).reshape(g, 128, n, -1)
    if fmt == "e4m3":
        vals = words.view(ml_dtypes.float8_e4m3fn).astype(np.float64)
    else:
        nib = np.empty((g, 128, n, 4), np.uint8)
        nib[..., 0::2] = words & 0xF
        nib[..., 1::2] = words >> 4
        vals = E2M1[nib]
    vals = vals * np.repeat(np.exp2(scales.astype(np.float64) - 127.0), 8, axis=1)[..., None]
    return vals.transpose(0, 1, 3, 2).reshape(g * 512, n)


def gelu(v):
    return 0.5 * v * (1.0 + np.tanh(np.sqrt(2.0 / np.pi) * (v + 0.044715 * v**3)))


K, T, S, N = 1536, 2048, 1024, 1024

def setup_inputs():
    n = np.random.standard_normal
    s = mx_kscale(K)[:, None]
    w = mx_kscale(S)[:, None]
    tab_words, tab_scales = pack_weight(n((K, T)) * s, "e4m3")
    wr_words, wr_scales = pack_weight(1.5 * n((S, S)) / np.sqrt(S) / w, "e2m1")
    return {
        "tab_words": tab_words,
        "tab_scales": tab_scales,
        "offs": striped(np.random.permutation(T)[:S]),
        "gT": n((N, T)).astype(np.float32),
        "contact": (n((K, N)) / np.sqrt(K) / s).astype(np.float32),
        "bias": (0.5 * n(S)).astype(np.float32),
        "gain": (np.exp(0.3 * n(S)) * w[:, 0]).astype(np.float32),
        "wr_words": wr_words,
        "wr_scales": wr_scales,
    }

def reference(tab_words, tab_scales, offs, gT, contact, bias, gain, wr_words, wr_scales):
    v = unpack_weight(tab_words, tab_scales, "e4m3")[:, unstriped(offs)]
    e = v.T @ mxq(f64(contact), 0, "e4m3")
    h = np.tanh(e + f64(bias)[:, None]) * f64(gain)[:, None]
    wr = unpack_weight(wr_words, wr_scales, "e2m1")
    y = mxq(h, 0, "e4m3").T @ wr
    g = f64(gT)[:, unstriped(offs)]
    new = g + 0.5 * (y - g)
    out = f64(gT).copy()
    out[:, unstriped(offs)] = new
    return out

@@ -1,0 +1,217 @@
+from contextlib import ExitStack
+
+import concourse.mybir as mybir
+
+K, T, S, N = 1536, 2048, 1024, 1024
+FLOPS = 2 * K * S * N + 2 * S * S * N
+
+F32 = mybir.dt.float32
+BF16 = mybir.dt.bfloat16
+I32 = mybir.dt.int32
+U32 = mybir.dt.uint32
+U16 = mybir.dt.uint16
+U8 = mybir.dt.uint8
+FP8X4 = mybir.dt.float8_e4m3fn_x4
+FP4X4 = mybir.dt.float4_e2m1fn_x4
+ACT = mybir.ActivationFunctionType
+ALU = mybir.AluOpType
+
+P = 128
+PACK = 4
+PASS = P * PACK
+K_PASSES = K // PASS
+M_PASSES = S // PASS
+TILES = N // P
+BANK = 512
+CONTACT_WIDTH = 256
+
+
+def tile_list_vowel_shift_kernel(tc, tab_words, tab_scales, offs, gT, contact, bias, gain, wr_words, wr_scales, out):
+    nc = tc.nc
+    with ExitStack() as ctx:
+        held = ctx.enter_context(tc.tile_pool(name="held", bufs=1))
+        ring = ctx.enter_context(tc.tile_pool(name="ring", bufs=2))
+        psum = ctx.enter_context(tc.psum_pool(name="psum", bufs=2))
+
+        offsets = held.tile([P, S // 16], U16, name="offsets")
+        table_scales = held.tile([P, T], U8, name="table_scales", align_bytes=64)
+        wr_planes = held.tile([P, M_PASSES, S], U8, name="wr_planes", align_bytes=64)
+        nc.vector.memset(table_scales[:].bitcast(I32), 0)
+        nc.vector.memset(wr_planes[:].rearrange("p a c -> p (a c)").bitcast(I32), 0)
+
+        nc.sync.dma_start(offsets[:], offs)
+        table_words = []
+        for a in range(K_PASSES):
+            words = held.tile([P, T], U32, name="table_words%d" % a, align_bytes=64)
+            nc.sync.dma_start(words[:].bitcast(I32), tab_words[a].rearrange("p n t -> p (n t)").bitcast(I32))
+            table_words.append(words)
+        for q in range(4):
+            nc.sync.dma_start(
+                table_scales[32 * q : 32 * q + 4 * K_PASSES, :].bitcast(I32),
+                tab_scales[:, 4 * q : 4 * q + 4, :].bitcast(I32),
+            )
+
+        contact_raw = {}
+        state = {}
+
+        def load_contact(c):
+            width = CONTACT_WIDTH
+            n0 = c * width
+            raw = held.tile([P, K_PASSES, PACK, width], F32, name="contact_raw%d" % c)
+            for a in range(K_PASSES):
+                rows = contact[a * PASS : (a + 1) * PASS, n0 : n0 + width]
+                nc.sync.dma_start(raw[:, a], rows.rearrange("(p j) n -> p j n", j=PACK))
+            for i in range(width // P):
+                contact_raw[n0 // P + i] = raw[:, :, :, i * P : (i + 1) * P]
+
+        def load_state(i):
+            rows = held.tile([P, T], F32, name="state%d" % i)
+            nc.sync.dma_start(rows[:], gT[i * P : (i + 1) * P, :])
+            state[i] = rows
+
+        load_contact(0)
+        load_state(0)
+        bias_sb = held.tile([P, M_PASSES, PACK], F32, name="bias_sb")
+        gain_sb = held.tile([P, M_PASSES, PACK], F32, name="gain_sb")
+        nc.sync.dma_start(bias_sb[:], bias.rearrange("(b p t) -> p b t", p=P, t=PACK))
+        nc.sync.dma_start(gain_sb[:], gain.rearrange("(b p t) -> p b t", p=P, t=PACK))
+        load_state(1)
+        load_state(2)
+        wr_codes = held.tile([P, M_PASSES, 2 * S], U8, name="wr_codes", align_bytes=64)
+        nc.sync.dma_start(wr_codes[:].bitcast(I32), wr_words.rearrange("a p c -> p a c").bitcast(I32))
+        for q in range(4):
+            nc.sync.dma_start(
+                wr_planes[32 * q : 32 * q + 4].bitcast(I32),
+                wr_scales[:, 4 * q : 4 * q + 4, :].rearrange("a r c -> r a c").bitcast(I32),
+            )
+        load_state(3)
+        load_contact(1)
+        load_contact(2)
+        load_state(4)
+        load_state(5)
+        load_contact(3)
+        load_state(6)
+        load_state(7)
+
+        picked_words = []
+        picked_scales = held.tile([P, S], U8, name="picked_scales", align_bytes=64)
+        ordered_scales = held.tile([P, S], U8, name="ordered_scales", align_bytes=64)
+        for a in range(K_PASSES):
+            picked = held.tile([P, S], U32, name="picked_words%d" % a, align_bytes=64)
+            nc.vector.tensor_copy(
+                picked[:].rearrange("p (b t q) -> p b q t", b=M_PASSES, t=PACK),
+                table_words[a][:].indirect(offsets[:]),
+            )
+            picked_words.append(picked)
+            if a == 0:
+                nc.vector.tensor_copy(picked_scales[:], table_scales[:].indirect(offsets[:]))
+        nc.vector.tensor_copy(
+            ordered_scales[:].rearrange("p (b t q) -> p b t q", b=M_PASSES, t=PACK),
+            picked_scales[:].rearrange("p (b q t) -> p b t q", b=M_PASSES, t=PACK),
+        )
+
+        contact_mx = {}
+        h_mx = {}
+        half_state = [held.tile([P, S], F32, name="half_state%d" % i, align_bytes=64) for i in range(TILES)]
+        contact_home = {0: 0, 1: 1, 2: 4, 3: 5, 4: 6, 5: 7}
+        staging = {}
+
+        def quantise_contact(i):
+            if i in contact_home:
+                grouped = half_state[contact_home[i]][:, : K_PASSES * PASS // 2].bitcast(BF16)
+            else:
+                grouped = ring.tile([P, K_PASSES * PASS], BF16, name="contact_grouped", align_bytes=64)[:]
+            nc.scalar.copy(
+                grouped.rearrange("p (a c i t) -> p a c t i", a=K_PASSES, i=4, t=PACK),
+                contact_raw[i].rearrange("p a t (c i) -> p a c t i", i=4),
+            )
+            codes = ring.tile([P, K_PASSES * P], U32, name="contact_codes", bufs=5, align_bytes=64)
+            scales = ring.tile([P, K_PASSES * P], U8, name="contact_scales", bufs=5, align_bytes=64)
+            for w0, w1 in ((0, 2 * P), (2 * P, 3 * P)):
+                nc.vector.quantize_mx(codes[:, w0:w1].bitcast(FP8X4), scales[:, w0:w1], grouped[:, PACK * w0 : PACK * w1])
+            contact_mx[i] = (codes, scales)
+
+        def first_product(i):
+            codes, scales = contact_mx[i]
+            staging[i] = ring.tile([P, S], F32, name="staging", bufs=4)
+            scaled = staging[i][:, S // 4 : 3 * S // 4].bitcast(BF16).rearrange("p (b t n) -> p b t n", b=M_PASSES, t=PACK)
+            for b in range(M_PASSES):
+                e = psum.tile([P, PACK, P], F32, name="e%d" % b)
+                for t in range(PACK):
+                    cols = slice(b * PASS + t * P, b * PASS + (t + 1) * P)
+                    for a in range(K_PASSES):
+                        nc.tensor.matmul_mx(
+                            e[:, t, :],
+                            lhsT=picked_words[a][:, cols].bitcast(FP8X4),
+                            lhsT_scale=ordered_scales[4 * a : P, cols],
+                            rhs=codes[:, a * P : (a + 1) * P].bitcast(FP8X4),
+                            rhs_scale=scales[:, a * P : (a + 1) * P],
+                            start=(a == 0),
+                            stop=(a == K_PASSES - 1),
+                        )
+                saturated = ring.tile([P, PACK, P], F32, name="saturated")
+                for t in range(PACK):
+                    nc.scalar.activation(saturated[:, t, :], e[:, t, :], ACT.Tanh, bias=bias_sb[:, b, t : t + 1])
+                for t in range(PACK):
+                    nc.scalar.activation(scaled[:, b, t, :], saturated[:, t, :], ACT.Copy, scale=gain_sb[:, b, t : t + 1])
+            if i == 0:
+                grouped = half_state[3][:, S // 4 : 3 * S // 4].bitcast(BF16)
+            else:
+                grouped = ring.tile([P, S], BF16, name="h_grouped", align_bytes=64)[:]
+            nc.scalar.copy(
+                grouped.rearrange("p (b c i t) -> p b c t i", b=M_PASSES, i=4, t=PACK),
+                scaled.rearrange("p b t (c i) -> p b c t i", i=4),
+            )
+            h_codes = ring.tile([P, M_PASSES * P], U32, name="h_codes", bufs=3, align_bytes=64)
+            h_scales = ring.tile([P, M_PASSES * P], U8, name="h_scales", bufs=3, align_bytes=64)
+            nc.vector.quantize_mx(h_codes[:].bitcast(FP8X4), h_scales[:], grouped)
+            h_mx[i] = (h_codes, h_scales)
+
+        def pick_state(i):
+            half = half_state[i]
+            for u in range(S // BANK):
+                nc.vector.tensor_scalar(
+                    half[:, u * BANK : (u + 1) * BANK],
+                    state[i][:].indirect(offsets[:, u * 32 : (u + 1) * 32]),
+                    0.5,
+                    0.0,
+                    ALU.mult,
+                    ALU.add,
+                )
+
+        def second_product(i):
+            h_codes, h_scales = h_mx[i]
+            if 0 < i < TILES - 1:
+                half_y = staging[i + 1]
+            else:
+                half_y = ring.tile([P, S], F32, name="staging", bufs=4)
+            for u in range(S // BANK):
+                y = psum.tile([P, BANK], F32, name="y%d" % u)
+                for b in range(M_PASSES):
+                    nc.tensor.matmul_mx(
+                        y[:],
+                        lhsT=h_codes[:, b * P : (b + 1) * P].bitcast(FP8X4),
+                        lhsT_scale=h_scales[:, b * P : (b + 1) * P],
+                        rhs=wr_codes[:, b, 2 * u * BANK : 2 * (u + 1) * BANK].bitcast(FP4X4),
+                        rhs_scale=wr_planes[:, b, u * BANK : (u + 1) * BANK],
+                        start=(b == 0),
+                        stop=(b == M_PASSES - 1),
+                    )
+                nc.scalar.activation(half_y[:, u * BANK : (u + 1) * BANK], y[:], ACT.Copy, scale=0.5)
+            nc.vector.tensor_tensor(state[i][:].indirect(offsets[:]), half_state[i][:], half_y[:], ALU.add)
+            nc.sync.dma_start(out[i * P : (i + 1) * P, :], state[i][:])
+
+        quantise_contact(0)
+        quantise_contact(1)
+        first_product(0)
+        pick_state(0)
+        second_product(0)
+        first_product(1)
+        for i in range(1, TILES):
+            if 2 * i < TILES:
+                quantise_contact(2 * i)
+                quantise_contact(2 * i + 1)
+            if i + 1 < TILES:
+                first_product(i + 1)
+            pick_state(i)
+            second_product(i)

@@ -39,6 +39,10 @@ def tile_list_vowel_shift_kernel(tc, tab_words, tab_scales, offs, gT, contact, b
         nc.vector.memset(table_scales[:].bitcast(I32), 0)
         nc.vector.memset(wr_planes[:].rearrange("p a c -> p (a c)").bitcast(I32), 0)
 
+        warm = held.tile([P, 2], F32, name="warm")
+        nc.gpsimd.memset(warm[:, 0:1], 0.0)
+        nc.scalar.activation(warm[:, 1:2], warm[:, 0:1], ACT.Tanh)
+
         nc.sync.dma_start(offsets[:], offs)
         table_words = []
         for a in range(K_PASSES):
@@ -89,8 +93,8 @@ def tile_list_vowel_shift_kernel(tc, tab_words, tab_scales, offs, gT, contact, b
         load_contact(2)
         load_state(4)
         load_state(5)
-        load_contact(3)
         load_state(6)
+        load_contact(3)
         load_state(7)
 
         picked_words = []
@@ -149,7 +153,10 @@ def tile_list_vowel_shift_kernel(tc, tab_words, tab_scales, offs, gT, contact, b
                             start=(a == 0),
                             stop=(a == K_PASSES - 1),
                         )
-                saturated = ring.tile([P, PACK, P], F32, name="saturated")
+                if i == 2:
+                    saturated = contact_raw[5][:, b]
+                else:
+                    saturated = ring.tile([P, PACK, P], F32, name="saturated")
                 for t in range(PACK):
                     nc.scalar.activation(saturated[:, t, :], e[:, t, :], ACT.Tanh, bias=bias_sb[:, b, t : t + 1])
                 for t in range(PACK):
@@ -207,10 +214,14 @@ def tile_list_vowel_shift_kernel(tc, tab_words, tab_scales, offs, gT, contact, b
         pick_state(0)
         second_product(0)
         first_product(1)
-        for i in range(1, TILES):
-            if 2 * i < TILES:
-                quantise_contact(2 * i)
-                quantise_contact(2 * i + 1)
+        for i in range(2, 6):
+            quantise_contact(i)
+        first_product(2)
+        pick_state(1)
+        second_product(1)
+        for i in range(6, TILES):
+            quantise_contact(i)
+        for i in range(2, TILES):
             if i + 1 < TILES:
                 first_product(i + 1)
             pick_state(i)

@@ -102,9 +102,11 @@ def tile_list_vowel_shift_kernel(tc, tab_words, tab_scales, offs, gT, contact, b
         ordered_scales = held.tile([P, S], U8, name="ordered_scales", align_bytes=64)
         for a in range(K_PASSES):
             picked = held.tile([P, S], U32, name="picked_words%d" % a, align_bytes=64)
+            listed = ring.tile([P, S], U32, name="listed_words", align_bytes=64)
+            nc.vector.tensor_copy(listed[:], table_words[a][:].indirect(offsets[:]))
             nc.vector.tensor_copy(
-                picked[:].rearrange("p (b t q) -> p b q t", b=M_PASSES, t=PACK),
-                table_words[a][:].indirect(offsets[:]),
+                picked[:].bitcast(I32).rearrange("p (b t c i) -> p b c t i", b=M_PASSES, t=PACK, i=4),
+                listed[:].bitcast(I32).rearrange("p (b c i t) -> p b c t i", b=M_PASSES, t=PACK, i=4),
             )
             picked_words.append(picked)
             if a == 0:
@@ -137,7 +139,7 @@ def tile_list_vowel_shift_kernel(tc, tab_words, tab_scales, offs, gT, contact, b
 
         def first_product(i):
             codes, scales = contact_mx[i]
-            staging[i] = ring.tile([P, S], F32, name="staging", bufs=4)
+            staging[i] = ring.tile([P, S], F32, name="staging", bufs=3)
             scaled = staging[i][:, S // 4 : 3 * S // 4].bitcast(BF16).rearrange("p (b t n) -> p b t n", b=M_PASSES, t=PACK)
             for b in range(M_PASSES):
                 e = psum.tile([P, PACK, P], F32, name="e%d" % b)
@@ -191,7 +193,7 @@ def tile_list_vowel_shift_kernel(tc, tab_words, tab_scales, offs, gT, contact, b
             if 0 < i < TILES - 1:
                 half_y = staging[i + 1]
             else:
-                half_y = ring.tile([P, S], F32, name="staging", bufs=4)
+                half_y = ring.tile([P, S], F32, name="staging", bufs=3)
             for u in range(S // BANK):
                 y = psum.tile([P, BANK], F32, name="y%d" % u)
                 for b in range(M_PASSES):

@@ -102,11 +102,9 @@ def tile_list_vowel_shift_kernel(tc, tab_words, tab_scales, offs, gT, contact, b
         ordered_scales = held.tile([P, S], U8, name="ordered_scales", align_bytes=64)
         for a in range(K_PASSES):
             picked = held.tile([P, S], U32, name="picked_words%d" % a, align_bytes=64)
-            listed = ring.tile([P, S], U32, name="listed_words", align_bytes=64)
-            nc.vector.tensor_copy(listed[:], table_words[a][:].indirect(offsets[:]))
             nc.vector.tensor_copy(
-                picked[:].bitcast(I32).rearrange("p (b t c i) -> p b c t i", b=M_PASSES, t=PACK, i=4),
-                listed[:].bitcast(I32).rearrange("p (b c i t) -> p b c t i", b=M_PASSES, t=PACK, i=4),
+                picked[:].rearrange("p (b t q) -> p b q t", b=M_PASSES, t=PACK),
+                table_words[a][:].indirect(offsets[:]),
             )
             picked_words.append(picked)
             if a == 0:
@@ -119,14 +117,15 @@ def tile_list_vowel_shift_kernel(tc, tab_words, tab_scales, offs, gT, contact, b
         contact_mx = {}
         h_mx = {}
         half_state = [held.tile([P, S], F32, name="half_state%d" % i, align_bytes=64) for i in range(TILES)]
-        contact_home = {0: 0, 1: 1, 2: 4, 3: 5, 4: 6, 5: 7}
+        contact_home = {0: 0, 1: 1, 2: 4, 3: 5, 4: 6, 6: 7}
+        spare = held.tile([P, K_PASSES * PASS // 2], F32, name="spare", align_bytes=64)
         staging = {}
 
         def quantise_contact(i):
             if i in contact_home:
                 grouped = half_state[contact_home[i]][:, : K_PASSES * PASS // 2].bitcast(BF16)
             else:
-                grouped = ring.tile([P, K_PASSES * PASS], BF16, name="contact_grouped", align_bytes=64)[:]
+                grouped = spare[:].bitcast(BF16)
             nc.scalar.copy(
                 grouped.rearrange("p (a c i t) -> p a c t i", a=K_PASSES, i=4, t=PACK),
                 contact_raw[i].rearrange("p a t (c i) -> p a c t i", i=4),
@@ -139,7 +138,7 @@ def tile_list_vowel_shift_kernel(tc, tab_words, tab_scales, offs, gT, contact, b
 
         def first_product(i):
             codes, scales = contact_mx[i]
-            staging[i] = ring.tile([P, S], F32, name="staging", bufs=3)
+            staging[i] = ring.tile([P, S], F32, name="staging", bufs=4)
             scaled = staging[i][:, S // 4 : 3 * S // 4].bitcast(BF16).rearrange("p (b t n) -> p b t n", b=M_PASSES, t=PACK)
             for b in range(M_PASSES):
                 e = psum.tile([P, PACK, P], F32, name="e%d" % b)
@@ -165,6 +164,10 @@ def tile_list_vowel_shift_kernel(tc, tab_words, tab_scales, offs, gT, contact, b
                     nc.scalar.activation(scaled[:, b, t, :], saturated[:, t, :], ACT.Copy, scale=gain_sb[:, b, t : t + 1])
             if i == 0:
                 grouped = half_state[3][:, S // 4 : 3 * S // 4].bitcast(BF16)
+            elif i == 2:
+                grouped = half_state[7][:, S // 4 : 3 * S // 4].bitcast(BF16)
+            elif i == 3:
+                grouped = spare[:, : S // 2].bitcast(BF16)
             else:
                 grouped = ring.tile([P, S], BF16, name="h_grouped", align_bytes=64)[:]
             nc.scalar.copy(
@@ -193,7 +196,7 @@ def tile_list_vowel_shift_kernel(tc, tab_words, tab_scales, offs, gT, contact, b
             if 0 < i < TILES - 1:
                 half_y = staging[i + 1]
             else:
-                half_y = ring.tile([P, S], F32, name="staging", bufs=3)
+                half_y = ring.tile([P, S], F32, name="staging", bufs=4)
             for u in range(S // BANK):
                 y = psum.tile([P, BANK], F32, name="y%d" % u)
                 for b in range(M_PASSES):
@@ -215,15 +218,16 @@ def tile_list_vowel_shift_kernel(tc, tab_words, tab_scales, offs, gT, contact, b
         first_product(0)
         pick_state(0)
         second_product(0)
+        quantise_contact(2)
         first_product(1)
-        for i in range(2, 6):
+        for i in range(3, 6):
             quantise_contact(i)
         first_product(2)
         pick_state(1)
         second_product(1)
-        for i in range(6, TILES):
-            quantise_contact(i)
         for i in range(2, TILES):
+            if i + 4 < TILES:
+                quantise_contact(i + 4)
             if i + 1 < TILES:
                 first_product(i + 1)
             pick_state(i)

@@ -39,6 +39,8 @@ def tile_list_vowel_shift_kernel(tc, tab_words, tab_scales, offs, gT, contact, b
         nc.vector.memset(table_scales[:].bitcast(I32), 0)
         nc.vector.memset(wr_planes[:].rearrange("p a c -> p (a c)").bitcast(I32), 0)
 
+        halves = held.tile([P, S], F32, name="halves")
+        nc.vector.memset(halves[:], 0.5)
         warm = held.tile([P, 2], F32, name="warm")
         nc.gpsimd.memset(warm[:, 0:1], 0.0)
         nc.scalar.activation(warm[:, 1:2], warm[:, 0:1], ACT.Tanh)
@@ -81,6 +83,7 @@ def tile_list_vowel_shift_kernel(tc, tab_words, tab_scales, offs, gT, contact, b
         nc.sync.dma_start(gain_sb[:], gain.rearrange("(b p t) -> p b t", p=P, t=PACK))
         load_state(1)
         load_state(2)
+        load_state(3)
         wr_codes = held.tile([P, M_PASSES, 2 * S], U8, name="wr_codes", align_bytes=64)
         nc.sync.dma_start(wr_codes[:].bitcast(I32), wr_words.rearrange("a p c -> p a c").bitcast(I32))
         for q in range(4):
@@ -88,7 +91,6 @@ def tile_list_vowel_shift_kernel(tc, tab_words, tab_scales, offs, gT, contact, b
                 wr_planes[32 * q : 32 * q + 4].bitcast(I32),
                 wr_scales[:, 4 * q : 4 * q + 4, :].rearrange("a r c -> r a c").bitcast(I32),
             )
-        load_state(3)
         load_contact(1)
         load_contact(2)
         load_state(4)
@@ -180,16 +182,7 @@ def tile_list_vowel_shift_kernel(tc, tab_words, tab_scales, offs, gT, contact, b
             h_mx[i] = (h_codes, h_scales)
 
         def pick_state(i):
-            half = half_state[i]
-            for u in range(S // BANK):
-                nc.vector.tensor_scalar(
-                    half[:, u * BANK : (u + 1) * BANK],
-                    state[i][:].indirect(offsets[:, u * 32 : (u + 1) * 32]),
-                    0.5,
-                    0.0,
-                    ALU.mult,
-                    ALU.add,
-                )
+            nc.vector.tensor_tensor(half_state[i][:], state[i][:].indirect(offsets[:]), halves[:], ALU.mult)
 
         def second_product(i):
             h_codes, h_scales = h_mx[i]

@@ -128,10 +128,11 @@ def tile_list_vowel_shift_kernel(tc, tab_words, tab_scales, offs, gT, contact, b
                 grouped = half_state[contact_home[i]][:, : K_PASSES * PASS // 2].bitcast(BF16)
             else:
                 grouped = spare[:].bitcast(BF16)
-            nc.scalar.copy(
-                grouped.rearrange("p (a c i t) -> p a c t i", a=K_PASSES, i=4, t=PACK),
-                contact_raw[i].rearrange("p a t (c i) -> p a c t i", i=4),
-            )
+            for a0, a1 in ((0, 1), (1, 2), (2, 3)) if i == 0 else ((0, 3),):
+                nc.scalar.copy(
+                    grouped.rearrange("p (a c i t) -> p a c t i", a=K_PASSES, i=4, t=PACK)[:, a0:a1],
+                    contact_raw[i].rearrange("p a t (c i) -> p a c t i", i=4)[:, a0:a1],
+                )
             codes = ring.tile([P, K_PASSES * P], U32, name="contact_codes", bufs=5, align_bytes=64)
             scales = ring.tile([P, K_PASSES * P], U8, name="contact_scales", bufs=5, align_bytes=64)
             for w0, w1 in ((0, 2 * P), (2 * P, 3 * P)):
@@ -203,7 +204,12 @@ def tile_list_vowel_shift_kernel(tc, tab_words, tab_scales, offs, gT, contact, b
                         stop=(b == M_PASSES - 1),
                     )
                 nc.scalar.activation(half_y[:, u * BANK : (u + 1) * BANK], y[:], ACT.Copy, scale=0.5)
-            nc.vector.tensor_tensor(state[i][:].indirect(offsets[:]), half_state[i][:], half_y[:], ALU.add)
+            pieces = S // BANK if i == 0 else 1
+            for u in range(pieces):
+                width = S // pieces
+                cols = slice(u * width, (u + 1) * width)
+                listed = offsets[:, u * width // 16 : (u + 1) * width // 16]
+                nc.vector.tensor_tensor(state[i][:].indirect(listed), half_state[i][:, cols], half_y[:, cols], ALU.add)
             nc.sync.dma_start(out[i * P : (i + 1) * P, :], state[i][:])
 
         quantise_contact(0)

@@ -1,6 +1,7 @@
 from contextlib import ExitStack
 
 import concourse.mybir as mybir
+from concourse.masks import make_identity
 
 K, T, S, N = 1536, 2048, 1024, 1024
 FLOPS = 2 * K * S * N + 2 * S * S * N
@@ -33,12 +34,18 @@ def tile_list_vowel_shift_kernel(tc, tab_words, tab_scales, offs, gT, contact, b
         ring = ctx.enter_context(tc.tile_pool(name="ring", bufs=2))
         psum = ctx.enter_context(tc.psum_pool(name="psum", bufs=2))
 
+        identity = held.tile([P, P], F32, name="identity")
+        make_identity(nc, identity[:])
         offsets = held.tile([P, S // 16], U16, name="offsets")
         table_scales = held.tile([P, T], U8, name="table_scales", align_bytes=64)
         wr_planes = held.tile([P, M_PASSES, S], U8, name="wr_planes", align_bytes=64)
         nc.vector.memset(table_scales[:].bitcast(I32), 0)
         nc.vector.memset(wr_planes[:].rearrange("p a c -> p (a c)").bitcast(I32), 0)
 
+        vectors = held.tile([P, PASS], F32, name="vectors")
+        nc.vector.memset(vectors[:], 0.0)
+        nc.scalar.dma_start(vectors[0:M_PASSES, :], bias.rearrange("(b m) -> b m", b=M_PASSES))
+        nc.scalar.dma_start(vectors[M_PASSES : 2 * M_PASSES, :], gain.rearrange("(b m) -> b m", b=M_PASSES))
         halves = held.tile([P, S], F32, name="halves")
         nc.vector.memset(halves[:], 0.5)
         warm = held.tile([P, 2], F32, name="warm")
@@ -52,7 +59,7 @@ def tile_list_vowel_shift_kernel(tc, tab_words, tab_scales, offs, gT, contact, b
             nc.sync.dma_start(words[:].bitcast(I32), tab_words[a].rearrange("p n t -> p (n t)").bitcast(I32))
             table_words.append(words)
         for q in range(4):
-            nc.sync.dma_start(
+            nc.gpsimd.dma_start(
                 table_scales[32 * q : 32 * q + 4 * K_PASSES, :].bitcast(I32),
                 tab_scales[:, 4 * q : 4 * q + 4, :].bitcast(I32),
             )
@@ -77,17 +84,13 @@ def tile_list_vowel_shift_kernel(tc, tab_words, tab_scales, offs, gT, contact, b
 
         load_contact(0)
         load_state(0)
-        bias_sb = held.tile([P, M_PASSES, PACK], F32, name="bias_sb")
-        gain_sb = held.tile([P, M_PASSES, PACK], F32, name="gain_sb")
-        nc.sync.dma_start(bias_sb[:], bias.rearrange("(b p t) -> p b t", p=P, t=PACK))
-        nc.sync.dma_start(gain_sb[:], gain.rearrange("(b p t) -> p b t", p=P, t=PACK))
         load_state(1)
         load_state(2)
         load_state(3)
         wr_codes = held.tile([P, M_PASSES, 2 * S], U8, name="wr_codes", align_bytes=64)
         nc.sync.dma_start(wr_codes[:].bitcast(I32), wr_words.rearrange("a p c -> p a c").bitcast(I32))
         for q in range(4):
-            nc.sync.dma_start(
+            nc.gpsimd.dma_start(
                 wr_planes[32 * q : 32 * q + 4].bitcast(I32),
                 wr_scales[:, 4 * q : 4 * q + 4, :].rearrange("a r c -> r a c").bitcast(I32),
             )
@@ -99,8 +102,13 @@ def tile_list_vowel_shift_kernel(tc, tab_words, tab_scales, offs, gT, contact, b
         load_contact(3)
         load_state(7)
 
+        turned = psum.tile([P, PACK, P], F32, name="y0")
+        for t in range(PACK):
+            nc.tensor.transpose(turned[:, t, :], vectors[:, t:PASS:PACK], identity[:])
+        columns = held.tile([P, PACK, 2 * M_PASSES], F32, name="columns")
+        nc.scalar.copy(columns[:], turned[:, :, : 2 * M_PASSES])
+
         picked_words = []
-        picked_scales = held.tile([P, S], U8, name="picked_scales", align_bytes=64)
         ordered_scales = held.tile([P, S], U8, name="ordered_scales", align_bytes=64)
         for a in range(K_PASSES):
             picked = held.tile([P, S], U32, name="picked_words%d" % a, align_bytes=64)
@@ -109,8 +117,8 @@ def tile_list_vowel_shift_kernel(tc, tab_words, tab_scales, offs, gT, contact, b
                 table_words[a][:].indirect(offsets[:]),
             )
             picked_words.append(picked)
-            if a == 0:
-                nc.vector.tensor_copy(picked_scales[:], table_scales[:].indirect(offsets[:]))
+        picked_scales = held.tile([P, S], U8, name="table_words1", align_bytes=64)
+        nc.vector.tensor_copy(picked_scales[:], table_scales[:].indirect(offsets[:]))
         nc.vector.tensor_copy(
             ordered_scales[:].rearrange("p (b t q) -> p b t q", b=M_PASSES, t=PACK),
             picked_scales[:].rearrange("p (b q t) -> p b t q", b=M_PASSES, t=PACK),
@@ -144,7 +152,7 @@ def tile_list_vowel_shift_kernel(tc, tab_words, tab_scales, offs, gT, contact, b
             staging[i] = ring.tile([P, S], F32, name="staging", bufs=4)
             scaled = staging[i][:, S // 4 : 3 * S // 4].bitcast(BF16).rearrange("p (b t n) -> p b t n", b=M_PASSES, t=PACK)
             for b in range(M_PASSES):
-                e = psum.tile([P, PACK, P], F32, name="e%d" % b)
+                e = psum.tile([P, PACK, P], F32, name="y0" if i == 1 else "e%d" % b)
                 for t in range(PACK):
                     cols = slice(b * PASS + t * P, b * PASS + (t + 1) * P)
                     for a in range(K_PASSES):
@@ -162,9 +170,9 @@ def tile_list_vowel_shift_kernel(tc, tab_words, tab_scales, offs, gT, contact, b
                 else:
                     saturated = ring.tile([P, PACK, P], F32, name="saturated")
                 for t in range(PACK):
-                    nc.scalar.activation(saturated[:, t, :], e[:, t, :], ACT.Tanh, bias=bias_sb[:, b, t : t + 1])
+                    nc.scalar.activation(saturated[:, t, :], e[:, t, :], ACT.Tanh, bias=columns[:, t, b : b + 1])
                 for t in range(PACK):
-                    nc.scalar.activation(scaled[:, b, t, :], saturated[:, t, :], ACT.Copy, scale=gain_sb[:, b, t : t + 1])
+                    nc.scalar.activation(scaled[:, b, t, :], saturated[:, t, :], ACT.Copy, scale=columns[:, t, M_PASSES + b : M_PASSES + b + 1])
             if i == 0:
                 grouped = half_state[3][:, S // 4 : 3 * S // 4].bitcast(BF16)
             elif i == 2:

@@ -32,7 +32,7 @@ def tile_list_vowel_shift_kernel(tc, tab_words, tab_scales, offs, gT, contact, b
     with ExitStack() as ctx:
         held = ctx.enter_context(tc.tile_pool(name="held", bufs=1))
         ring = ctx.enter_context(tc.tile_pool(name="ring", bufs=2))
-        psum = ctx.enter_context(tc.psum_pool(name="psum", bufs=2))
+        psum = ctx.enter_context(tc.psum_pool(name="psum", bufs=1))
 
         identity = held.tile([P, P], F32, name="identity")
         make_identity(nc, identity[:])
@@ -52,14 +52,23 @@ def tile_list_vowel_shift_kernel(tc, tab_words, tab_scales, offs, gT, contact, b
         nc.gpsimd.memset(warm[:, 0:1], 0.0)
         nc.scalar.activation(warm[:, 1:2], warm[:, 0:1], ACT.Tanh)
 
+        own_halves = {}
+        for i in (1, 0):
+            own_halves[i] = held.tile([P, S], F32, name="own_halves%d" % i, align_bytes=64)
+            nc.scalar.copy(own_halves[i][:], halves[:])
+
         nc.sync.dma_start(offsets[:], offs)
         table_words = []
-        for a in range(K_PASSES):
+
+        def load_table(a):
             words = held.tile([P, T], U32, name="table_words%d" % a, align_bytes=64)
             nc.sync.dma_start(words[:].bitcast(I32), tab_words[a].rearrange("p n t -> p (n t)").bitcast(I32))
             table_words.append(words)
+
+        load_table(0)
+        load_table(1)
         for q in range(4):
-            nc.gpsimd.dma_start(
+            nc.sync.dma_start(
                 table_scales[32 * q : 32 * q + 4 * K_PASSES, :].bitcast(I32),
                 tab_scales[:, 4 * q : 4 * q + 4, :].bitcast(I32),
             )
@@ -70,7 +79,7 @@ def tile_list_vowel_shift_kernel(tc, tab_words, tab_scales, offs, gT, contact, b
         def load_contact(c):
             width = CONTACT_WIDTH
             n0 = c * width
-            raw = held.tile([P, K_PASSES, PACK, width], F32, name="contact_raw%d" % c)
+            raw = held.tile([P, K_PASSES, PACK, width], F32, name="contact_raw%d" % c, align_bytes=64)
             for a in range(K_PASSES):
                 rows = contact[a * PASS : (a + 1) * PASS, n0 : n0 + width]
                 nc.sync.dma_start(raw[:, a], rows.rearrange("(p j) n -> p j n", j=PACK))
@@ -83,159 +92,233 @@ def tile_list_vowel_shift_kernel(tc, tab_words, tab_scales, offs, gT, contact, b
             state[i] = rows
 
         load_contact(0)
-        load_state(0)
+        load_table(2)
         load_state(1)
-        load_state(2)
-        load_state(3)
         wr_codes = held.tile([P, M_PASSES, 2 * S], U8, name="wr_codes", align_bytes=64)
         nc.sync.dma_start(wr_codes[:].bitcast(I32), wr_words.rearrange("a p c -> p a c").bitcast(I32))
         for q in range(4):
-            nc.gpsimd.dma_start(
+            nc.sync.dma_start(
                 wr_planes[32 * q : 32 * q + 4].bitcast(I32),
                 wr_scales[:, 4 * q : 4 * q + 4, :].rearrange("a r c -> r a c").bitcast(I32),
             )
+        load_state(0)
         load_contact(1)
+        load_state(2)
         load_contact(2)
+        load_state(3)
         load_state(4)
-        load_state(5)
-        load_state(6)
         load_contact(3)
-        load_state(7)
+        for i in range(5, TILES):
+            load_state(i)
 
-        turned = psum.tile([P, PACK, P], F32, name="y0")
+        turned = psum.tile([P, PACK, P], F32, name="bank1_0")
         for t in range(PACK):
             nc.tensor.transpose(turned[:, t, :], vectors[:, t:PASS:PACK], identity[:])
         columns = held.tile([P, PACK, 2 * M_PASSES], F32, name="columns")
         nc.scalar.copy(columns[:], turned[:, :, : 2 * M_PASSES])
 
-        picked_words = []
+        picked_words = [held.tile([P, S], U32, name="picked_words%d" % a, align_bytes=64) for a in range(K_PASSES - 1)]
         ordered_scales = held.tile([P, S], U8, name="ordered_scales", align_bytes=64)
-        for a in range(K_PASSES):
-            picked = held.tile([P, S], U32, name="picked_words%d" % a, align_bytes=64)
+
+        def pick_words(a, b0, b1):
             nc.vector.tensor_copy(
-                picked[:].rearrange("p (b t q) -> p b q t", b=M_PASSES, t=PACK),
-                table_words[a][:].indirect(offsets[:]),
+                picked_words[a][:, b0 * PASS : b1 * PASS].rearrange("p (b t q) -> p b q t", b=b1 - b0, t=PACK),
+                table_words[a][:].indirect(offsets[:, b0 * PASS // 16 : b1 * PASS // 16]),
             )
-            picked_words.append(picked)
+
+        contact_mx = {}
+        h_mx = {}
+        h_home = {}
+        half_state = {}
+        half_y = {}
+        GROUPED = K_PASSES * PASS // 2
+
+        def cast_contact(i, home, steps):
+            grouped = home.bitcast(BF16)
+            for a0, a1 in steps:
+                nc.scalar.copy(
+                    grouped.rearrange("p (a c i t) -> p a c t i", a=K_PASSES, i=4, t=PACK)[:, a0:a1],
+                    contact_raw[i].rearrange("p a t (c i) -> p a c t i", i=4)[:, a0:a1],
+                )
+            return grouped
+
+        def quantise_contact(i, grouped, codes):
+            scales = ring.tile([P, K_PASSES * P], U8, name="contact_scales", bufs=3, align_bytes=64)
+            for w0, w1 in ((0, 2 * P), (2 * P, 3 * P)):
+                nc.vector.quantize_mx(codes[:, w0:w1].bitcast(FP8X4), scales[:, w0:w1], grouped[:, PACK * w0 : PACK * w1])
+            contact_mx[i] = (codes, scales)
+
+        def first_pass(i, e, a, b, t):
+            codes, scales = contact_mx[i]
+            cols = slice(b * PASS + t * P, b * PASS + (t + 1) * P)
+            nc.tensor.matmul_mx(
+                e,
+                lhsT=picked_words[a][:, cols].bitcast(FP8X4),
+                lhsT_scale=ordered_scales[4 * a : P, cols],
+                rhs=codes[:, a * P : (a + 1) * P].bitcast(FP8X4),
+                rhs_scale=scales[:, a * P : (a + 1) * P],
+                start=(a == 0),
+                stop=(a == K_PASSES - 1),
+            )
+
+        def first_product(i, b):
+            e = psum.tile([P, PACK, P], F32, name="bank%d_%d" % {(1, 1): (0, 0), (2, 0): (1, 0), (2, 1): (1, 1)}.get((i, b), (i % 2, b)))
+            for t in range(PACK):
+                for a in range(K_PASSES):
+                    first_pass(i, e[:, t, :], a, b, t)
+            return [e[:, t, :] for t in range(PACK)]
+
+        def saturate(sums, b, saturated, scaled):
+            for t in range(PACK):
+                nc.scalar.activation(saturated[:, t * P : (t + 1) * P], sums[t], ACT.Tanh, bias=columns[:, t, b : b + 1])
+            for t in range(PACK):
+                nc.scalar.activation(
+                    scaled[:, b, t * P : (t + 1) * P],
+                    saturated[:, t * P : (t + 1) * P],
+                    ACT.Copy,
+                    scale=columns[:, t, M_PASSES + b : M_PASSES + b + 1],
+                )
+
+        def interleave_h(grouped, scaled, b0, b1):
+            nc.scalar.copy(
+                grouped.rearrange("p (b c i t) -> p b c t i", b=M_PASSES, i=4, t=PACK)[:, b0:b1],
+                scaled.rearrange("p b (t c i) -> p b c t i", t=PACK, i=4)[:, b0:b1],
+            )
+
+        def as_halves(home):
+            return home.bitcast(BF16).rearrange("p (b x) -> p b x", b=M_PASSES)[:, :, :PASS]
+
+        def new_h_home(i):
+            h_home[i] = ring.tile([P, GROUPED], F32, name="h_home", bufs=3, align_bytes=64)
+            return h_home[i][:, : S // 2].bitcast(BF16)
+
+        def quantise_h(i, grouped):
+            if i < 2:
+                h_codes = held.tile([P, M_PASSES * P], U32, name="own_halves%d" % (1 - i), align_bytes=64)
+            else:
+                h_codes = ring.tile([P, M_PASSES * P], U32, name="h_codes", bufs=3, align_bytes=64)
+            h_scales = ring.tile([P, M_PASSES * P], U8, name="h_scales", bufs=3, align_bytes=64)
+            nc.vector.quantize_mx(h_codes[:].bitcast(FP8X4), h_scales[:], grouped)
+            h_mx[i] = (h_codes, h_scales)
+
+        def pick_state(i):
+            nc.vector.tensor_tensor(half_state[i][:], state[i][:].indirect(offsets[:]), own_halves.get(i, halves)[:], ALU.mult)
+
+        def second_product(i, u):
+            h_codes, h_scales = h_mx[i]
+            y = psum.tile([P, BANK], F32, name="bank%d_%d" % (i % 2, u))
+            for b in range(M_PASSES):
+                nc.tensor.matmul_mx(
+                    y[:],
+                    lhsT=h_codes[:, b * P : (b + 1) * P].bitcast(FP8X4),
+                    lhsT_scale=h_scales[:, b * P : (b + 1) * P],
+                    rhs=wr_codes[:, b, 2 * u * BANK : 2 * (u + 1) * BANK].bitcast(FP4X4),
+                    rhs_scale=wr_planes[:, b, u * BANK : (u + 1) * BANK],
+                    start=(b == 0),
+                    stop=(b == M_PASSES - 1),
+                )
+            return y
+
+        def halve_y(i, u, y):
+            nc.scalar.activation(half_y[i][:, u * BANK : (u + 1) * BANK], y[:], ACT.Copy, scale=0.5)
+
+        def put_back(i, c0, c1):
+            listed = offsets[:, c0 // 16 : c1 // 16]
+            nc.vector.tensor_tensor(state[i][:].indirect(listed), half_state[i][:, c0:c1], half_y[i][:, c0:c1], ALU.add)
+
+        def store(i):
+            nc.sync.dma_start(out[i * P : (i + 1) * P, :], state[i][:])
+
+        late_homes = {5: "first_home", 6: "table_words2", 7: "contact_raw0"}
+
+        def new_half_state(i):
+            half_state[i] = held.tile([P, S], F32, name=late_homes.get(i, "half_state%d" % i), align_bytes=64)
+
+        pick_words(0, 0, M_PASSES)
+        pick_words(1, 0, M_PASSES)
         picked_scales = held.tile([P, S], U8, name="table_words1", align_bytes=64)
         nc.vector.tensor_copy(picked_scales[:], table_scales[:].indirect(offsets[:]))
         nc.vector.tensor_copy(
             ordered_scales[:].rearrange("p (b t q) -> p b t q", b=M_PASSES, t=PACK),
             picked_scales[:].rearrange("p (b q t) -> p b t q", b=M_PASSES, t=PACK),
         )
-
-        contact_mx = {}
-        h_mx = {}
-        half_state = [held.tile([P, S], F32, name="half_state%d" % i, align_bytes=64) for i in range(TILES)]
-        contact_home = {0: 0, 1: 1, 2: 4, 3: 5, 4: 6, 6: 7}
-        spare = held.tile([P, K_PASSES * PASS // 2], F32, name="spare", align_bytes=64)
-        staging = {}
-
-        def quantise_contact(i):
-            if i in contact_home:
-                grouped = half_state[contact_home[i]][:, : K_PASSES * PASS // 2].bitcast(BF16)
-            else:
-                grouped = spare[:].bitcast(BF16)
-            for a0, a1 in ((0, 1), (1, 2), (2, 3)) if i == 0 else ((0, 3),):
-                nc.scalar.copy(
-                    grouped.rearrange("p (a c i t) -> p a c t i", a=K_PASSES, i=4, t=PACK)[:, a0:a1],
-                    contact_raw[i].rearrange("p a t (c i) -> p a c t i", i=4)[:, a0:a1],
-                )
-            codes = ring.tile([P, K_PASSES * P], U32, name="contact_codes", bufs=5, align_bytes=64)
-            scales = ring.tile([P, K_PASSES * P], U8, name="contact_scales", bufs=5, align_bytes=64)
-            for w0, w1 in ((0, 2 * P), (2 * P, 3 * P)):
-                nc.vector.quantize_mx(codes[:, w0:w1].bitcast(FP8X4), scales[:, w0:w1], grouped[:, PACK * w0 : PACK * w1])
-            contact_mx[i] = (codes, scales)
-
-        def first_product(i):
-            codes, scales = contact_mx[i]
-            staging[i] = ring.tile([P, S], F32, name="staging", bufs=4)
-            scaled = staging[i][:, S // 4 : 3 * S // 4].bitcast(BF16).rearrange("p (b t n) -> p b t n", b=M_PASSES, t=PACK)
-            for b in range(M_PASSES):
-                e = psum.tile([P, PACK, P], F32, name="y0" if i == 1 else "e%d" % b)
-                for t in range(PACK):
-                    cols = slice(b * PASS + t * P, b * PASS + (t + 1) * P)
-                    for a in range(K_PASSES):
-                        nc.tensor.matmul_mx(
-                            e[:, t, :],
-                            lhsT=picked_words[a][:, cols].bitcast(FP8X4),
-                            lhsT_scale=ordered_scales[4 * a : P, cols],
-                            rhs=codes[:, a * P : (a + 1) * P].bitcast(FP8X4),
-                            rhs_scale=scales[:, a * P : (a + 1) * P],
-                            start=(a == 0),
-                            stop=(a == K_PASSES - 1),
-                        )
-                if i == 2:
-                    saturated = contact_raw[5][:, b]
-                else:
-                    saturated = ring.tile([P, PACK, P], F32, name="saturated")
-                for t in range(PACK):
-                    nc.scalar.activation(saturated[:, t, :], e[:, t, :], ACT.Tanh, bias=columns[:, t, b : b + 1])
-                for t in range(PACK):
-                    nc.scalar.activation(scaled[:, b, t, :], saturated[:, t, :], ACT.Copy, scale=columns[:, t, M_PASSES + b : M_PASSES + b + 1])
-            if i == 0:
-                grouped = half_state[3][:, S // 4 : 3 * S // 4].bitcast(BF16)
-            elif i == 2:
-                grouped = half_state[7][:, S // 4 : 3 * S // 4].bitcast(BF16)
-            elif i == 3:
-                grouped = spare[:, : S // 2].bitcast(BF16)
-            else:
-                grouped = ring.tile([P, S], BF16, name="h_grouped", align_bytes=64)[:]
-            nc.scalar.copy(
-                grouped.rearrange("p (b c i t) -> p b c t i", b=M_PASSES, i=4, t=PACK),
-                scaled.rearrange("p b t (c i) -> p b c t i", i=4),
-            )
-            h_codes = ring.tile([P, M_PASSES * P], U32, name="h_codes", bufs=3, align_bytes=64)
-            h_scales = ring.tile([P, M_PASSES * P], U8, name="h_scales", bufs=3, align_bytes=64)
-            nc.vector.quantize_mx(h_codes[:].bitcast(FP8X4), h_scales[:], grouped)
-            h_mx[i] = (h_codes, h_scales)
-
-        def pick_state(i):
-            nc.vector.tensor_tensor(half_state[i][:], state[i][:].indirect(offsets[:]), halves[:], ALU.mult)
-
-        def second_product(i):
-            h_codes, h_scales = h_mx[i]
-            if 0 < i < TILES - 1:
-                half_y = staging[i + 1]
-            else:
-                half_y = ring.tile([P, S], F32, name="staging", bufs=4)
-            for u in range(S // BANK):
-                y = psum.tile([P, BANK], F32, name="y%d" % u)
-                for b in range(M_PASSES):
-                    nc.tensor.matmul_mx(
-                        y[:],
-                        lhsT=h_codes[:, b * P : (b + 1) * P].bitcast(FP8X4),
-                        lhsT_scale=h_scales[:, b * P : (b + 1) * P],
-                        rhs=wr_codes[:, b, 2 * u * BANK : 2 * (u + 1) * BANK].bitcast(FP4X4),
-                        rhs_scale=wr_planes[:, b, u * BANK : (u + 1) * BANK],
-                        start=(b == 0),
-                        stop=(b == M_PASSES - 1),
-                    )
-                nc.scalar.activation(half_y[:, u * BANK : (u + 1) * BANK], y[:], ACT.Copy, scale=0.5)
-            pieces = S // BANK if i == 0 else 1
-            for u in range(pieces):
-                width = S // pieces
-                cols = slice(u * width, (u + 1) * width)
-                listed = offsets[:, u * width // 16 : (u + 1) * width // 16]
-                nc.vector.tensor_tensor(state[i][:].indirect(listed), half_state[i][:, cols], half_y[:, cols], ALU.add)
-            nc.sync.dma_start(out[i * P : (i + 1) * P, :], state[i][:])
-
-        quantise_contact(0)
-        quantise_contact(1)
-        first_product(0)
-        pick_state(0)
-        second_product(0)
-        quantise_contact(2)
-        first_product(1)
-        for i in range(3, 6):
-            quantise_contact(i)
-        first_product(2)
+        first_home = held.tile([P, 2 * GROUPED], F32, name="first_home", align_bytes=64)
+        grouped = cast_contact(0, first_home[:, :GROUPED], ((0, 1), (1, 2), (2, 3)))
+        quantise_contact(0, grouped, held.tile([P, K_PASSES * P], U32, name="table_scales", align_bytes=64))
+        picked_words.append(held.tile([P, S], U32, name="table_words1", align_bytes=64))
+        pick_words(2, 0, 1)
+        pick_words(2, 1, 2)
+        grouped = cast_contact(1, first_home[:, GROUPED:], ((0, 3),))
+        quantise_contact(1, grouped, held.tile([P, K_PASSES * P], U32, name="table_words2", align_bytes=64))
+        new_half_state(1)
         pick_state(1)
-        second_product(1)
+
+        sums = [psum.tile([P, P], F32, name="first%d" % t)[:] for t in range(PACK)]
+        for a in range(K_PASSES):
+            for t in range(PACK):
+                first_pass(0, sums[t], a, 0, t)
+        new_half_state(0)
+        scaled = as_halves(half_state[0][:, : S // 2])
+        grouped = new_h_home(0)
+        for b in range(M_PASSES):
+            if b == 1:
+                sums = first_product(0, b)
+            saturate(sums, b, ring.tile([P, PASS], F32, name="saturated")[:], scaled)
+            interleave_h(grouped, scaled, b, b + 1)
+        quantise_h(0, grouped)
+        pick_state(0)
+        shared = held.tile([P, 3 * (S - P)], F32, name="table_words0", align_bytes=64)
+        half_y[0] = shared[:, :S]
+        halve_y(0, 0, second_product(0, 0))
+        y_rest = second_product(0, 1)
+        put_back(0, 0, BANK)
+
+        scaled = as_halves(shared[:, S - P :])
+        for b in range(M_PASSES):
+            saturate(first_product(1, b), b, ring.tile([P, PASS], F32, name="saturated")[:], scaled)
+        grouped = new_h_home(1)
+        interleave_h(grouped, scaled, 0, M_PASSES)
+        quantise_h(1, grouped)
+        halve_y(0, 1, y_rest)
+        put_back(0, BANK, S)
+        store(0)
+        for i in (2, 3):
+            grouped = cast_contact(i, shared[:, S + (i - 2) * GROUPED : S + (i - 1) * GROUPED], ((0, 3),))
+            quantise_contact(i, grouped, ring.tile([P, K_PASSES * P], U32, name="contact_codes", bufs=3, align_bytes=64))
+        shared = held.tile([P, S + GROUPED], F32, name="contact_raw1", align_bytes=64)
+        half_y[1] = shared[:, :S]
+        for u in range(S // BANK):
+            halve_y(1, u, second_product(1, u))
+        put_back(1, 0, S)
+        store(1)
+        grouped = cast_contact(4, shared[:, S:], ((0, 3),))
+        quantise_contact(4, grouped, ring.tile([P, K_PASSES * P], U32, name="contact_codes", bufs=3, align_bytes=64))
+        new_half_state(2)
+        scaled = as_halves(half_state[2][:, : S // 2])
+        for b in range(M_PASSES):
+            saturate(first_product(2, b), b, ring.tile([P, PASS], F32, name="saturated")[:], scaled)
+        grouped = new_h_home(2)
+        interleave_h(grouped, scaled, 0, M_PASSES)
+        quantise_h(2, grouped)
+        pick_state(2)
+
         for i in range(2, TILES):
-            if i + 4 < TILES:
-                quantise_contact(i + 4)
+            ys = [second_product(i, u) for u in range(S // BANK)]
+            staging = ring.tile([P, S], F32, name="staging", bufs=3)
+            half_y[i] = staging[:]
+            if 4 < i + 2 < TILES:
+                grouped = cast_contact(i + 2, h_home[i][:], ((0, 3),))
+                quantise_contact(i + 2, grouped, ring.tile([P, K_PASSES * P], U32, name="contact_codes", bufs=3, align_bytes=64))
             if i + 1 < TILES:
-                first_product(i + 1)
-            pick_state(i)
-            second_product(i)
+                new_half_state(i + 1)
+                scaled = as_halves(staging[:, S // 4 : 3 * S // 4])
+                saturate(first_product(i + 1, 0), 0, half_state[i + 1][:, :PASS], scaled)
+                saturate(first_product(i + 1, 1), 1, ring.tile([P, PASS], F32, name="saturated")[:], scaled)
+                pick_state(i + 1)
+                grouped = new_h_home(i + 1)
+                interleave_h(grouped, scaled, 0, M_PASSES)
+                quantise_h(i + 1, grouped)
+            for u in range(S // BANK):
+                halve_y(i, u, ys[u])
+            put_back(i, 0, S)
+            store(i)

@@ -23,6 +23,7 @@ PASS = P * PACK
 K_PASSES = K // PASS
 M_PASSES = S // PASS
 TILES = N // P
+CHUNKS = S // P
 BANK = 512
 CONTACT_WIDTH = 256
 
@@ -42,18 +43,20 @@ def tile_list_vowel_shift_kernel(tc, tab_words, tab_scales, offs, gT, contact, b
         nc.vector.memset(table_scales[:].bitcast(I32), 0)
         nc.vector.memset(wr_planes[:].rearrange("p a c -> p (a c)").bitcast(I32), 0)
 
-        vectors = held.tile([P, PASS], F32, name="vectors")
+        vectors = held.tile([P, P], F32, name="vectors")
         nc.vector.memset(vectors[:], 0.0)
-        nc.scalar.dma_start(vectors[0:M_PASSES, :], bias.rearrange("(b m) -> b m", b=M_PASSES))
-        nc.scalar.dma_start(vectors[M_PASSES : 2 * M_PASSES, :], gain.rearrange("(b m) -> b m", b=M_PASSES))
+        nc.gpsimd.dma_start(vectors[0:CHUNKS, :], bias.rearrange("(c m) -> c m", c=CHUNKS))
+        nc.gpsimd.dma_start(vectors[CHUNKS : 2 * CHUNKS, :], gain.rearrange("(c m) -> c m", c=CHUNKS))
         halves = held.tile([P, S], F32, name="halves")
         nc.vector.memset(halves[:], 0.5)
         warm = held.tile([P, 2], F32, name="warm")
         nc.gpsimd.memset(warm[:, 0:1], 0.0)
         nc.scalar.activation(warm[:, 1:2], warm[:, 0:1], ACT.Tanh)
+        identity_bf16 = held.tile([P, P], BF16, name="identity_bf16")
+        nc.scalar.copy(identity_bf16[:], identity[:])
 
         own_halves = {}
-        for i in (1, 0):
+        for i in (3, 0):
             own_halves[i] = held.tile([P, S], F32, name="own_halves%d" % i, align_bytes=64)
             nc.scalar.copy(own_halves[i][:], halves[:])
 
@@ -93,7 +96,8 @@ def tile_list_vowel_shift_kernel(tc, tab_words, tab_scales, offs, gT, contact, b
 
         load_contact(0)
         load_table(2)
-        load_state(1)
+        for i in (1, 2, 3):
+            load_state(i)
         wr_codes = held.tile([P, M_PASSES, 2 * S], U8, name="wr_codes", align_bytes=64)
         nc.sync.dma_start(wr_codes[:].bitcast(I32), wr_words.rearrange("a p c -> p a c").bitcast(I32))
         for q in range(4):
@@ -103,26 +107,23 @@ def tile_list_vowel_shift_kernel(tc, tab_words, tab_scales, offs, gT, contact, b
             )
         load_state(0)
         load_contact(1)
-        load_state(2)
         load_contact(2)
-        load_state(3)
-        load_state(4)
-        load_contact(3)
-        for i in range(5, TILES):
+        for i in (4, 5, 6):
             load_state(i)
+        load_contact(3)
+        load_state(7)
 
-        turned = psum.tile([P, PACK, P], F32, name="bank1_0")
-        for t in range(PACK):
-            nc.tensor.transpose(turned[:, t, :], vectors[:, t:PASS:PACK], identity[:])
-        columns = held.tile([P, PACK, 2 * M_PASSES], F32, name="columns")
-        nc.scalar.copy(columns[:], turned[:, :, : 2 * M_PASSES])
+        turned = psum.tile([P, P], F32, name="y1")
+        nc.tensor.transpose(turned[:], vectors[:], identity[:])
+        columns = held.tile([P, 2 * CHUNKS], F32, name="columns")
+        nc.scalar.copy(columns[:], turned[:, : 2 * CHUNKS])
 
         picked_words = [held.tile([P, S], U32, name="picked_words%d" % a, align_bytes=64) for a in range(K_PASSES - 1)]
-        ordered_scales = held.tile([P, S], U8, name="ordered_scales", align_bytes=64)
+        picked_scales = held.tile([P, S], U8, name="picked_scales", align_bytes=64)
 
         def pick_words(a, b0, b1):
             nc.vector.tensor_copy(
-                picked_words[a][:, b0 * PASS : b1 * PASS].rearrange("p (b t q) -> p b q t", b=b1 - b0, t=PACK),
+                picked_words[a][:, b0 * PASS : b1 * PASS],
                 table_words[a][:].indirect(offsets[:, b0 * PASS // 16 : b1 * PASS // 16]),
             )
 
@@ -154,7 +155,7 @@ def tile_list_vowel_shift_kernel(tc, tab_words, tab_scales, offs, gT, contact, b
             nc.tensor.matmul_mx(
                 e,
                 lhsT=picked_words[a][:, cols].bitcast(FP8X4),
-                lhsT_scale=ordered_scales[4 * a : P, cols],
+                lhsT_scale=picked_scales[4 * a : P, cols],
                 rhs=codes[:, a * P : (a + 1) * P].bitcast(FP8X4),
                 rhs_scale=scales[:, a * P : (a + 1) * P],
                 start=(a == 0),
@@ -162,31 +163,50 @@ def tile_list_vowel_shift_kernel(tc, tab_words, tab_scales, offs, gT, contact, b
             )
 
         def first_product(i, b):
-            e = psum.tile([P, PACK, P], F32, name="bank%d_%d" % {(1, 1): (0, 0), (2, 0): (1, 0), (2, 1): (1, 1)}.get((i, b), (i % 2, b)))
+            e = psum.tile([P, PACK, P], F32, name=("y%d" if i == 2 else "e%d") % b)
             for t in range(PACK):
                 for a in range(K_PASSES):
                     first_pass(i, e[:, t, :], a, b, t)
             return [e[:, t, :] for t in range(PACK)]
 
-        def saturate(sums, b, saturated, scaled):
+        def saturate(sums, b, saturated, scaled, rows):
             for t in range(PACK):
-                nc.scalar.activation(saturated[:, t * P : (t + 1) * P], sums[t], ACT.Tanh, bias=columns[:, t, b : b + 1])
+                c = PACK * b + t
+                nc.scalar.activation(saturated[t], sums[t], ACT.Tanh, bias=columns[:, c : c + 1])
             for t in range(PACK):
-                nc.scalar.activation(
-                    scaled[:, b, t * P : (t + 1) * P],
-                    saturated[:, t * P : (t + 1) * P],
-                    ACT.Copy,
-                    scale=columns[:, t, M_PASSES + b : M_PASSES + b + 1],
-                )
+                c = CHUNKS + PACK * b + t
+                cols = slice(t * P, (t + 1) * P)
+                nc.scalar.activation(scaled[:, b, cols], saturated[t], ACT.Copy, scale=columns[:, c : c + 1])
+                nc.tensor.transpose(rows[:, cols], scaled[:, b, cols], identity_bf16[:])
 
-        def interleave_h(grouped, scaled, b0, b1):
+        def quarters(*homes):
+            return [homes[t * len(homes) // PACK][:, t * P : (t + 1) * P] for t in range(PACK)]
+
+        def free_quarters():
+            return quarters(ring.tile([P, PASS], F32, name="saturated"))
+
+        def new_rows(bank, halves_of_list):
+            return psum.tile([P, halves_of_list, PASS], BF16, name="first%d" % bank)
+
+        def turn_back(grouped, pairs, rows, bank, b0, b1):
             nc.scalar.copy(
-                grouped.rearrange("p (b c i t) -> p b c t i", b=M_PASSES, i=4, t=PACK)[:, b0:b1],
-                scaled.rearrange("p b (t c i) -> p b c t i", t=PACK, i=4)[:, b0:b1],
+                pairs[:, b0:b1].rearrange("p b (u q) -> p b u q", u=2),
+                rows[:].bitcast(F32).rearrange("p b (q u) -> p b u q", u=2),
+            )
+            back = psum.tile([P, b1 - b0, 2, P], F32, name=bank)
+            for b in range(b0, b1):
+                for u in range(2):
+                    nc.tensor.transpose(back[:, b - b0, u, :], pairs[:, b, u * P : (u + 1) * P], identity[:])
+            nc.scalar.copy(
+                grouped.bitcast(F32).rearrange("p (b n u) -> p b n u", b=M_PASSES, u=2)[:, b0:b1],
+                back[:].rearrange("p b u n -> p b n u"),
             )
 
         def as_halves(home):
-            return home.bitcast(BF16).rearrange("p (b x) -> p b x", b=M_PASSES)[:, :, :PASS]
+            return home.bitcast(BF16).rearrange("p (b x) -> p b x", b=M_PASSES)
+
+        def as_pairs(home):
+            return home.rearrange("p (b x) -> p b x", b=M_PASSES)[:, :, : PASS // 2]
 
         def new_h_home(i):
             h_home[i] = ring.tile([P, GROUPED], F32, name="h_home", bufs=3, align_bytes=64)
@@ -194,7 +214,7 @@ def tile_list_vowel_shift_kernel(tc, tab_words, tab_scales, offs, gT, contact, b
 
         def quantise_h(i, grouped):
             if i < 2:
-                h_codes = held.tile([P, M_PASSES * P], U32, name="own_halves%d" % (1 - i), align_bytes=64)
+                h_codes = held.tile([P, M_PASSES * P], U32, name="own_halves%d" % (3, 0)[i], align_bytes=64)
             else:
                 h_codes = ring.tile([P, M_PASSES * P], U32, name="h_codes", bufs=3, align_bytes=64)
             h_scales = ring.tile([P, M_PASSES * P], U8, name="h_scales", bufs=3, align_bytes=64)
@@ -206,7 +226,7 @@ def tile_list_vowel_shift_kernel(tc, tab_words, tab_scales, offs, gT, contact, b
 
         def second_product(i, u):
             h_codes, h_scales = h_mx[i]
-            y = psum.tile([P, BANK], F32, name="bank%d_%d" % (i % 2, u))
+            y = psum.tile([P, BANK], F32, name="y%d" % u)
             for b in range(M_PASSES):
                 nc.tensor.matmul_mx(
                     y[:],
@@ -236,12 +256,7 @@ def tile_list_vowel_shift_kernel(tc, tab_words, tab_scales, offs, gT, contact, b
 
         pick_words(0, 0, M_PASSES)
         pick_words(1, 0, M_PASSES)
-        picked_scales = held.tile([P, S], U8, name="table_words1", align_bytes=64)
         nc.vector.tensor_copy(picked_scales[:], table_scales[:].indirect(offsets[:]))
-        nc.vector.tensor_copy(
-            ordered_scales[:].rearrange("p (b t q) -> p b t q", b=M_PASSES, t=PACK),
-            picked_scales[:].rearrange("p (b q t) -> p b t q", b=M_PASSES, t=PACK),
-        )
         first_home = held.tile([P, 2 * GROUPED], F32, name="first_home", align_bytes=64)
         grouped = cast_contact(0, first_home[:, :GROUPED], ((0, 1), (1, 2), (2, 3)))
         quantise_contact(0, grouped, held.tile([P, K_PASSES * P], U32, name="table_scales", align_bytes=64))
@@ -250,8 +265,9 @@ def tile_list_vowel_shift_kernel(tc, tab_words, tab_scales, offs, gT, contact, b
         pick_words(2, 1, 2)
         grouped = cast_contact(1, first_home[:, GROUPED:], ((0, 3),))
         quantise_contact(1, grouped, held.tile([P, K_PASSES * P], U32, name="table_words2", align_bytes=64))
-        new_half_state(1)
-        pick_state(1)
+        for i in (1, 2, 3):
+            new_half_state(i)
+            pick_state(i)
 
         sums = [psum.tile([P, P], F32, name="first%d" % t)[:] for t in range(PACK)]
         for a in range(K_PASSES):
@@ -259,12 +275,14 @@ def tile_list_vowel_shift_kernel(tc, tab_words, tab_scales, offs, gT, contact, b
                 first_pass(0, sums[t], a, 0, t)
         new_half_state(0)
         scaled = as_halves(half_state[0][:, : S // 2])
-        grouped = new_h_home(0)
+        grouped = half_state[0][:, S // 2 :].bitcast(BF16)
+        between = held.tile([P, S // 2], F32, name="between")
         for b in range(M_PASSES):
             if b == 1:
                 sums = first_product(0, b)
-            saturate(sums, b, ring.tile([P, PASS], F32, name="saturated")[:], scaled)
-            interleave_h(grouped, scaled, b, b + 1)
+            rows = new_rows(2 * b, 1)
+            saturate(sums, b, free_quarters(), scaled, rows[:, 0])
+            turn_back(grouped, as_pairs(between[:]), rows, "first%d" % (2 * b + 1), b, b + 1)
         quantise_h(0, grouped)
         pick_state(0)
         shared = held.tile([P, 3 * (S - P)], F32, name="table_words0", align_bytes=64)
@@ -273,11 +291,12 @@ def tile_list_vowel_shift_kernel(tc, tab_words, tab_scales, offs, gT, contact, b
         y_rest = second_product(0, 1)
         put_back(0, 0, BANK)
 
-        scaled = as_halves(shared[:, S - P :])
+        scaled = as_halves(between[:])
+        rows = new_rows(0, M_PASSES)
         for b in range(M_PASSES):
-            saturate(first_product(1, b), b, ring.tile([P, PASS], F32, name="saturated")[:], scaled)
+            saturate(first_product(1, b), b, free_quarters(), scaled, rows[:, b])
         grouped = new_h_home(1)
-        interleave_h(grouped, scaled, 0, M_PASSES)
+        turn_back(grouped, as_pairs(shared[:, S - P :]), rows, "y0", 0, M_PASSES)
         quantise_h(1, grouped)
         halve_y(0, 1, y_rest)
         put_back(0, BANK, S)
@@ -293,31 +312,38 @@ def tile_list_vowel_shift_kernel(tc, tab_words, tab_scales, offs, gT, contact, b
         store(1)
         grouped = cast_contact(4, shared[:, S:], ((0, 3),))
         quantise_contact(4, grouped, ring.tile([P, K_PASSES * P], U32, name="contact_codes", bufs=3, align_bytes=64))
-        new_half_state(2)
-        scaled = as_halves(half_state[2][:, : S // 2])
-        for b in range(M_PASSES):
-            saturate(first_product(2, b), b, ring.tile([P, PASS], F32, name="saturated")[:], scaled)
+        new_half_state(4)
+        staging = ring.tile([P, S], F32, name="staging", bufs=3)
+        scaled = as_halves(staging[:, : S // 2])
+        rows = new_rows(2, M_PASSES)
+        saturate(first_product(2, 0), 0, quarters(half_state[4]), scaled, rows[:, 0])
+        saturate(first_product(2, 1), 1, free_quarters(), scaled, rows[:, 1])
+        pick_state(4)
         grouped = new_h_home(2)
-        interleave_h(grouped, scaled, 0, M_PASSES)
+        turn_back(grouped, as_pairs(staging[:, S // 2 :]), rows, "first3", 0, M_PASSES)
         quantise_h(2, grouped)
-        pick_state(2)
 
         for i in range(2, TILES):
-            ys = [second_product(i, u) for u in range(S // BANK)]
             staging = ring.tile([P, S], F32, name="staging", bufs=3)
             half_y[i] = staging[:]
-            if 4 < i + 2 < TILES:
-                grouped = cast_contact(i + 2, h_home[i][:], ((0, 3),))
-                quantise_contact(i + 2, grouped, ring.tile([P, K_PASSES * P], U32, name="contact_codes", bufs=3, align_bytes=64))
             if i + 1 < TILES:
-                new_half_state(i + 1)
-                scaled = as_halves(staging[:, S // 4 : 3 * S // 4])
-                saturate(first_product(i + 1, 0), 0, half_state[i + 1][:, :PASS], scaled)
-                saturate(first_product(i + 1, 1), 1, ring.tile([P, PASS], F32, name="saturated")[:], scaled)
-                pick_state(i + 1)
+                picks = {2: (5, 6), 3: (7,)}.get(i, ())
+                for j in picks:
+                    new_half_state(j)
+                scaled = as_halves(staging[:, : S // 2])
+                rows = new_rows(2 * (i % 2), M_PASSES)
+                saturate(first_product(i + 1, 0), 0, free_quarters(), scaled, rows[:, 0])
+                second = quarters(*[half_state[j] for j in picks]) if picks else free_quarters()
+                saturate(first_product(i + 1, 1), 1, second, scaled, rows[:, 1])
+                for j in picks:
+                    pick_state(j)
                 grouped = new_h_home(i + 1)
-                interleave_h(grouped, scaled, 0, M_PASSES)
+                turn_back(grouped, as_pairs(staging[:, S // 2 :]), rows, "first%d" % (2 * (i % 2) + 1), 0, M_PASSES)
                 quantise_h(i + 1, grouped)
+            if i + 3 < TILES:
+                grouped = cast_contact(i + 3, h_home[i][:], ((0, 3),))
+                quantise_contact(i + 3, grouped, ring.tile([P, K_PASSES * P], U32, name="contact_codes", bufs=3, align_bytes=64))
+            ys = [second_product(i, u) for u in range(S // BANK)]
             for u in range(S // BANK):
                 halve_y(i, u, ys[u])
             put_back(i, 0, S)

@@ -1,7 +1,6 @@
 from contextlib import ExitStack
 
 import concourse.mybir as mybir
-from concourse.masks import make_identity
 
 K, T, S, N = 1536, 2048, 1024, 1024
 FLOPS = 2 * K * S * N + 2 * S * S * N
@@ -25,7 +24,6 @@ M_PASSES = S // PASS
 TILES = N // P
 CHUNKS = S // P
 BANK = 512
-CONTACT_WIDTH = 256
 
 
 def tile_list_vowel_shift_kernel(tc, tab_words, tab_scales, offs, gT, contact, bias, gain, wr_words, wr_scales, out):
@@ -35,69 +33,52 @@ def tile_list_vowel_shift_kernel(tc, tab_words, tab_scales, offs, gT, contact, b
         ring = ctx.enter_context(tc.tile_pool(name="ring", bufs=2))
         psum = ctx.enter_context(tc.psum_pool(name="psum", bufs=1))
 
-        identity = held.tile([P, P], F32, name="identity")
-        make_identity(nc, identity[:])
         offsets = held.tile([P, S // 16], U16, name="offsets")
         table_scales = held.tile([P, T], U8, name="table_scales", align_bytes=64)
         wr_planes = held.tile([P, M_PASSES, S], U8, name="wr_planes", align_bytes=64)
+        halves = held.tile([P, S], F32, name="halves")
         nc.vector.memset(table_scales[:].bitcast(I32), 0)
         nc.vector.memset(wr_planes[:].rearrange("p a c -> p (a c)").bitcast(I32), 0)
-
-        vectors = held.tile([P, P], F32, name="vectors")
-        nc.vector.memset(vectors[:], 0.0)
-        nc.gpsimd.dma_start(vectors[0:CHUNKS, :], bias.rearrange("(c m) -> c m", c=CHUNKS))
-        nc.gpsimd.dma_start(vectors[CHUNKS : 2 * CHUNKS, :], gain.rearrange("(c m) -> c m", c=CHUNKS))
-        halves = held.tile([P, S], F32, name="halves")
         nc.vector.memset(halves[:], 0.5)
-        warm = held.tile([P, 2], F32, name="warm")
-        nc.gpsimd.memset(warm[:, 0:1], 0.0)
-        nc.scalar.activation(warm[:, 1:2], warm[:, 0:1], ACT.Tanh)
-        identity_bf16 = held.tile([P, P], BF16, name="identity_bf16")
-        nc.scalar.copy(identity_bf16[:], identity[:])
 
-        own_halves = {}
-        for i in (3, 0):
-            own_halves[i] = held.tile([P, S], F32, name="own_halves%d" % i, align_bytes=64)
-            nc.scalar.copy(own_halves[i][:], halves[:])
+        bias_cols = held.tile([P, M_PASSES, PACK], F32, name="bias_cols")
+        gain_cols = held.tile([P, M_PASSES, PACK], F32, name="gain_cols")
+        nc.gpsimd.dma_start(bias_cols[:], bias.rearrange("(b p t) -> p b t", b=M_PASSES, t=PACK))
+        nc.gpsimd.dma_start(gain_cols[:], gain.rearrange("(b p t) -> p b t", b=M_PASSES, t=PACK))
 
-        nc.sync.dma_start(offsets[:], offs)
         table_words = []
+        contact_raw = {}
+        state = {}
 
         def load_table(a):
             words = held.tile([P, T], U32, name="table_words%d" % a, align_bytes=64)
             nc.sync.dma_start(words[:].bitcast(I32), tab_words[a].rearrange("p n t -> p (n t)").bitcast(I32))
             table_words.append(words)
 
-        load_table(0)
-        load_table(1)
-        for q in range(4):
-            nc.sync.dma_start(
-                table_scales[32 * q : 32 * q + 4 * K_PASSES, :].bitcast(I32),
-                tab_scales[:, 4 * q : 4 * q + 4, :].bitcast(I32),
-            )
-
-        contact_raw = {}
-        state = {}
-
-        def load_contact(c):
-            width = CONTACT_WIDTH
-            n0 = c * width
-            raw = held.tile([P, K_PASSES, PACK, width], F32, name="contact_raw%d" % c, align_bytes=64)
+        def load_contact(i):
+            raw = held.tile([P, K_PASSES, PACK, P], F32, name="contact_raw%d" % i, align_bytes=64)
             for a in range(K_PASSES):
-                rows = contact[a * PASS : (a + 1) * PASS, n0 : n0 + width]
+                rows = contact[a * PASS : (a + 1) * PASS, i * P : (i + 1) * P]
                 nc.sync.dma_start(raw[:, a], rows.rearrange("(p j) n -> p j n", j=PACK))
-            for i in range(width // P):
-                contact_raw[n0 // P + i] = raw[:, :, :, i * P : (i + 1) * P]
+            contact_raw[i] = raw
 
         def load_state(i):
             rows = held.tile([P, T], F32, name="state%d" % i)
             nc.sync.dma_start(rows[:], gT[i * P : (i + 1) * P, :])
             state[i] = rows
 
+        load_table(0)
+        nc.sync.dma_start(offsets[:], offs)
+        for q in range(4):
+            nc.scalar.dma_start(
+                table_scales[32 * q : 32 * q + 4 * K_PASSES, :].bitcast(I32),
+                tab_scales[:, 4 * q : 4 * q + 4, :].bitcast(I32),
+            )
+        load_table(1)
         load_contact(0)
         load_table(2)
-        for i in (1, 2, 3):
-            load_state(i)
+        load_state(0)
+        load_state(7)
         wr_codes = held.tile([P, M_PASSES, 2 * S], U8, name="wr_codes", align_bytes=64)
         nc.sync.dma_start(wr_codes[:].bitcast(I32), wr_words.rearrange("a p c -> p a c").bitcast(I32))
         for q in range(4):
@@ -105,31 +86,27 @@ def tile_list_vowel_shift_kernel(tc, tab_words, tab_scales, offs, gT, contact, b
                 wr_planes[32 * q : 32 * q + 4].bitcast(I32),
                 wr_scales[:, 4 * q : 4 * q + 4, :].rearrange("a r c -> r a c").bitcast(I32),
             )
-        load_state(0)
         load_contact(1)
         load_contact(2)
-        for i in (4, 5, 6):
-            load_state(i)
-        load_contact(3)
-        load_state(7)
+        load_state(6)
+        for i in range(3, TILES):
+            load_contact(i)
+            load_state(i - 2)
 
-        turned = psum.tile([P, P], F32, name="y1")
-        nc.tensor.transpose(turned[:], vectors[:], identity[:])
-        columns = held.tile([P, 2 * CHUNKS], F32, name="columns")
-        nc.scalar.copy(columns[:], turned[:, : 2 * CHUNKS])
-
-        picked_words = [held.tile([P, S], U32, name="picked_words%d" % a, align_bytes=64) for a in range(K_PASSES - 1)]
+        picked_words = [held.tile([P, S], U32, name="picked_words%d" % a, align_bytes=64) for a in range(K_PASSES)]
         picked_scales = held.tile([P, S], U8, name="picked_scales", align_bytes=64)
 
+        def dealt(tile):
+            return tile[:].rearrange("p (b t q) -> p b q t", b=M_PASSES, t=PACK)
+
+        def listed(c0, c1):
+            return offsets[:, c0 // 16 : c1 // 16]
+
         def pick_words(a, b0, b1):
-            nc.vector.tensor_copy(
-                picked_words[a][:, b0 * PASS : b1 * PASS],
-                table_words[a][:].indirect(offsets[:, b0 * PASS // 16 : b1 * PASS // 16]),
-            )
+            nc.vector.tensor_copy(dealt(picked_words[a])[:, b0:b1], table_words[a][:].indirect(listed(b0 * PASS, b1 * PASS)))
 
         contact_mx = {}
         h_mx = {}
-        h_home = {}
         half_state = {}
         half_y = {}
         GROUPED = K_PASSES * PASS // 2
@@ -139,212 +116,182 @@ def tile_list_vowel_shift_kernel(tc, tab_words, tab_scales, offs, gT, contact, b
             for a0, a1 in steps:
                 nc.scalar.copy(
                     grouped.rearrange("p (a c i t) -> p a c t i", a=K_PASSES, i=4, t=PACK)[:, a0:a1],
-                    contact_raw[i].rearrange("p a t (c i) -> p a c t i", i=4)[:, a0:a1],
+                    contact_raw[i][:].rearrange("p a t (c i) -> p a c t i", i=4)[:, a0:a1],
                 )
             return grouped
 
-        def quantise_contact(i, grouped, codes):
+        def quantise_contact(i, grouped, steps):
+            codes = ring.tile([P, K_PASSES * P], U32, name="contact_codes", bufs=3, align_bytes=64)
             scales = ring.tile([P, K_PASSES * P], U8, name="contact_scales", bufs=3, align_bytes=64)
-            for w0, w1 in ((0, 2 * P), (2 * P, 3 * P)):
-                nc.vector.quantize_mx(codes[:, w0:w1].bitcast(FP8X4), scales[:, w0:w1], grouped[:, PACK * w0 : PACK * w1])
+            for a0, a1 in steps:
+                nc.vector.quantize_mx(
+                    codes[:, a0 * P : a1 * P].bitcast(FP8X4), scales[:, a0 * P : a1 * P], grouped[:, a0 * PASS : a1 * PASS]
+                )
             contact_mx[i] = (codes, scales)
 
-        def first_pass(i, e, a, b, t):
+        def first_pass(i, e, a, b, t, start, stop):
             codes, scales = contact_mx[i]
             cols = slice(b * PASS + t * P, b * PASS + (t + 1) * P)
             nc.tensor.matmul_mx(
-                e,
+                e[:, t, :],
                 lhsT=picked_words[a][:, cols].bitcast(FP8X4),
                 lhsT_scale=picked_scales[4 * a : P, cols],
                 rhs=codes[:, a * P : (a + 1) * P].bitcast(FP8X4),
                 rhs_scale=scales[:, a * P : (a + 1) * P],
-                start=(a == 0),
-                stop=(a == K_PASSES - 1),
+                start=start,
+                stop=stop,
             )
 
-        def first_product(i, b):
-            e = psum.tile([P, PACK, P], F32, name=("y%d" if i == 2 else "e%d") % b)
+        def new_sums(i, b):
+            return psum.tile([P, PACK, P], F32, name="e%d" % (2 * (i % 2) + b))
+
+        def first_product(i):
+            sums = []
+            for b in range(M_PASSES):
+                e = new_sums(i, b)
+                for t in range(PACK):
+                    for a in range(K_PASSES):
+                        first_pass(i, e, a, b, t, a == 0, a == K_PASSES - 1)
+                sums.append(e)
+            return sums
+
+        def make_h(e, b, scaled, grouped):
+            saturated = ring.tile([P, PACK, P], F32, name="saturated")
+            scaled = scaled.bitcast(BF16)
             for t in range(PACK):
-                for a in range(K_PASSES):
-                    first_pass(i, e[:, t, :], a, b, t)
-            return [e[:, t, :] for t in range(PACK)]
-
-        def saturate(sums, b, saturated, scaled, rows):
+                nc.scalar.activation(saturated[:, t, :], e[:, t, :], ACT.Tanh, bias=bias_cols[:, b, t : t + 1])
             for t in range(PACK):
-                c = PACK * b + t
-                nc.scalar.activation(saturated[t], sums[t], ACT.Tanh, bias=columns[:, c : c + 1])
-            for t in range(PACK):
-                c = CHUNKS + PACK * b + t
-                cols = slice(t * P, (t + 1) * P)
-                nc.scalar.activation(scaled[:, b, cols], saturated[t], ACT.Copy, scale=columns[:, c : c + 1])
-                nc.tensor.transpose(rows[:, cols], scaled[:, b, cols], identity_bf16[:])
-
-        def quarters(*homes):
-            return [homes[t * len(homes) // PACK][:, t * P : (t + 1) * P] for t in range(PACK)]
-
-        def free_quarters():
-            return quarters(ring.tile([P, PASS], F32, name="saturated"))
-
-        def new_rows(bank, halves_of_list):
-            return psum.tile([P, halves_of_list, PASS], BF16, name="first%d" % bank)
-
-        def turn_back(grouped, pairs, rows, bank, b0, b1):
+                nc.scalar.activation(scaled[:, t * P : (t + 1) * P], saturated[:, t, :], ACT.Copy, scale=gain_cols[:, b, t : t + 1])
             nc.scalar.copy(
-                pairs[:, b0:b1].rearrange("p b (u q) -> p b u q", u=2),
-                rows[:].bitcast(F32).rearrange("p b (q u) -> p b u q", u=2),
-            )
-            back = psum.tile([P, b1 - b0, 2, P], F32, name=bank)
-            for b in range(b0, b1):
-                for u in range(2):
-                    nc.tensor.transpose(back[:, b - b0, u, :], pairs[:, b, u * P : (u + 1) * P], identity[:])
-            nc.scalar.copy(
-                grouped.bitcast(F32).rearrange("p (b n u) -> p b n u", b=M_PASSES, u=2)[:, b0:b1],
-                back[:].rearrange("p b u n -> p b n u"),
+                grouped[:, b * PASS : (b + 1) * PASS].rearrange("p (c i t) -> p c t i", i=4, t=PACK),
+                scaled.rearrange("p (t c i) -> p c t i", i=4, t=PACK),
             )
 
-        def as_halves(home):
-            return home.bitcast(BF16).rearrange("p (b x) -> p b x", b=M_PASSES)
+        def new_grouped():
+            return ring.tile([P, S], BF16, name="h_grouped", align_bytes=64)
 
-        def as_pairs(home):
-            return home.rearrange("p (b x) -> p b x", b=M_PASSES)[:, :, : PASS // 2]
+        def quantise_h(i, grouped, b0, b1):
+            h_codes, h_scales = h_mx[i]
+            nc.vector.quantize_mx(h_codes[:, b0 * P : b1 * P].bitcast(FP8X4), h_scales[:, b0 * P : b1 * P], grouped[:, b0 * PASS : b1 * PASS])
 
-        def new_h_home(i):
-            h_home[i] = ring.tile([P, GROUPED], F32, name="h_home", bufs=3, align_bytes=64)
-            return h_home[i][:, : S // 2].bitcast(BF16)
-
-        def quantise_h(i, grouped):
-            if i < 2:
-                h_codes = held.tile([P, M_PASSES * P], U32, name="own_halves%d" % (3, 0)[i], align_bytes=64)
+        def new_h_mx(i):
+            if i == 0:
+                h_codes = held.tile([P, M_PASSES * P], U32, name="second_home", align_bytes=64)
             else:
-                h_codes = ring.tile([P, M_PASSES * P], U32, name="h_codes", bufs=3, align_bytes=64)
-            h_scales = ring.tile([P, M_PASSES * P], U8, name="h_scales", bufs=3, align_bytes=64)
-            nc.vector.quantize_mx(h_codes[:].bitcast(FP8X4), h_scales[:], grouped)
+                h_codes = ring.tile([P, M_PASSES * P], U32, name="h_codes", align_bytes=64)
+            h_scales = ring.tile([P, M_PASSES * P], U8, name="h_scales", align_bytes=64)
             h_mx[i] = (h_codes, h_scales)
 
-        def pick_state(i):
-            nc.vector.tensor_tensor(half_state[i][:], state[i][:].indirect(offsets[:]), own_halves.get(i, halves)[:], ALU.mult)
+        def pick_state(i, c0, c1):
+            nc.vector.tensor_tensor(half_state[i][:, c0:c1], state[i][:].indirect(listed(c0, c1)), halves[:, c0:c1], ALU.mult)
 
-        def second_product(i, u):
+        def second_pass(i, y, u, b):
             h_codes, h_scales = h_mx[i]
-            y = psum.tile([P, BANK], F32, name="y%d" % u)
-            for b in range(M_PASSES):
-                nc.tensor.matmul_mx(
-                    y[:],
-                    lhsT=h_codes[:, b * P : (b + 1) * P].bitcast(FP8X4),
-                    lhsT_scale=h_scales[:, b * P : (b + 1) * P],
-                    rhs=wr_codes[:, b, 2 * u * BANK : 2 * (u + 1) * BANK].bitcast(FP4X4),
-                    rhs_scale=wr_planes[:, b, u * BANK : (u + 1) * BANK],
-                    start=(b == 0),
-                    stop=(b == M_PASSES - 1),
-                )
-            return y
+            nc.tensor.matmul_mx(
+                y[:],
+                lhsT=h_codes[:, b * P : (b + 1) * P].bitcast(FP8X4),
+                lhsT_scale=h_scales[:, b * P : (b + 1) * P],
+                rhs=wr_codes[:, b, 2 * u * BANK : 2 * (u + 1) * BANK].bitcast(FP4X4),
+                rhs_scale=wr_planes[:, b, u * BANK : (u + 1) * BANK],
+                start=(b == 0),
+                stop=(b == M_PASSES - 1),
+            )
 
-        def halve_y(i, u, y):
-            nc.scalar.activation(half_y[i][:, u * BANK : (u + 1) * BANK], y[:], ACT.Copy, scale=0.5)
+        def new_y(u):
+            return psum.tile([P, BANK], F32, name="y%d" % u)
 
-        def put_back(i, c0, c1):
-            listed = offsets[:, c0 // 16 : c1 // 16]
-            nc.vector.tensor_tensor(state[i][:].indirect(listed), half_state[i][:, c0:c1], half_y[i][:, c0:c1], ALU.add)
+        def second_product(i):
+            ys = [new_y(u) for u in range(S // BANK)]
+            for u in range(S // BANK):
+                for b in range(M_PASSES):
+                    second_pass(i, ys[u], u, b)
+            return ys
+
+        def halve_y(home, y):
+            nc.scalar.activation(home, y[:], ACT.Copy, scale=0.5)
+            return home
+
+        def put_back(i, c0, c1, half_y):
+            nc.vector.tensor_tensor(state[i][:].indirect(listed(c0, c1)), half_state[i][:, c0:c1], half_y, ALU.add)
 
         def store(i):
             nc.sync.dma_start(out[i * P : (i + 1) * P, :], state[i][:])
 
-        late_homes = {5: "first_home", 6: "table_words2", 7: "contact_raw0"}
+        def first_half_home():
+            return ring.tile([P, BANK], F32, name="first_half_y")[:]
 
-        def new_half_state(i):
-            half_state[i] = held.tile([P, S], F32, name=late_homes.get(i, "half_state%d" % i), align_bytes=64)
+        QUARTER = PASS // 2
+        WHOLE = ((0, K_PASSES),)
 
         pick_words(0, 0, M_PASSES)
+        nc.vector.tensor_copy(dealt(picked_scales), table_scales[:].indirect(offsets[:]))
         pick_words(1, 0, M_PASSES)
-        nc.vector.tensor_copy(picked_scales[:], table_scales[:].indirect(offsets[:]))
-        first_home = held.tile([P, 2 * GROUPED], F32, name="first_home", align_bytes=64)
-        grouped = cast_contact(0, first_home[:, :GROUPED], ((0, 1), (1, 2), (2, 3)))
-        quantise_contact(0, grouped, held.tile([P, K_PASSES * P], U32, name="table_scales", align_bytes=64))
-        picked_words.append(held.tile([P, S], U32, name="table_words1", align_bytes=64))
-        pick_words(2, 0, 1)
-        pick_words(2, 1, 2)
-        grouped = cast_contact(1, first_home[:, GROUPED:], ((0, 3),))
-        quantise_contact(1, grouped, held.tile([P, K_PASSES * P], U32, name="table_words2", align_bytes=64))
-        for i in (1, 2, 3):
-            new_half_state(i)
-            pick_state(i)
-
-        sums = [psum.tile([P, P], F32, name="first%d" % t)[:] for t in range(PACK)]
-        for a in range(K_PASSES):
+        first_home = held.tile([P, GROUPED], F32, name="first_home", align_bytes=64)
+        grouped = cast_contact(0, first_home[:], ((0, 1), (1, 2), (2, 3)))
+        quantise_contact(0, grouped, ((0, 2), (2, 3)))
+        sums = [new_sums(0, b) for b in range(M_PASSES)]
+        for b in range(M_PASSES):
+            for a in range(K_PASSES - 1):
+                for t in range(PACK):
+                    first_pass(0, sums[b], a, b, t, a == 0 and t == 0, False)
+        for b in range(M_PASSES):
+            pick_words(2, b, b + 1)
             for t in range(PACK):
-                first_pass(0, sums[t], a, 0, t)
-        new_half_state(0)
-        scaled = as_halves(half_state[0][:, : S // 2])
-        grouped = half_state[0][:, S // 2 :].bitcast(BF16)
-        between = held.tile([P, S // 2], F32, name="between")
+                first_pass(0, sums[b], K_PASSES - 1, b, t, False, t == PACK - 1)
+        half_state[0] = held.tile([P, S], F32, name="half_state0")
+        pick_state(0, 0, S)
+        half_state[7] = held.tile([P, S], F32, name="half_state7", align_bytes=64)
+        grouped = new_grouped()
+        new_h_mx(0)
+        ys = [new_y(u) for u in range(S // BANK)]
         for b in range(M_PASSES):
-            if b == 1:
-                sums = first_product(0, b)
-            rows = new_rows(2 * b, 1)
-            saturate(sums, b, free_quarters(), scaled, rows[:, 0])
-            turn_back(grouped, as_pairs(between[:]), rows, "first%d" % (2 * b + 1), b, b + 1)
-        quantise_h(0, grouped)
-        pick_state(0)
-        shared = held.tile([P, 3 * (S - P)], F32, name="table_words0", align_bytes=64)
-        half_y[0] = shared[:, :S]
-        halve_y(0, 0, second_product(0, 0))
-        y_rest = second_product(0, 1)
-        put_back(0, 0, BANK)
-
-        scaled = as_halves(between[:])
-        rows = new_rows(0, M_PASSES)
-        for b in range(M_PASSES):
-            saturate(first_product(1, b), b, free_quarters(), scaled, rows[:, b])
-        grouped = new_h_home(1)
-        turn_back(grouped, as_pairs(shared[:, S - P :]), rows, "y0", 0, M_PASSES)
-        quantise_h(1, grouped)
-        halve_y(0, 1, y_rest)
-        put_back(0, BANK, S)
-        store(0)
-        for i in (2, 3):
-            grouped = cast_contact(i, shared[:, S + (i - 2) * GROUPED : S + (i - 1) * GROUPED], ((0, 3),))
-            quantise_contact(i, grouped, ring.tile([P, K_PASSES * P], U32, name="contact_codes", bufs=3, align_bytes=64))
-        shared = held.tile([P, S + GROUPED], F32, name="contact_raw1", align_bytes=64)
-        half_y[1] = shared[:, :S]
-        for u in range(S // BANK):
-            halve_y(1, u, second_product(1, u))
-        put_back(1, 0, S)
-        store(1)
-        grouped = cast_contact(4, shared[:, S:], ((0, 3),))
-        quantise_contact(4, grouped, ring.tile([P, K_PASSES * P], U32, name="contact_codes", bufs=3, align_bytes=64))
-        new_half_state(4)
-        staging = ring.tile([P, S], F32, name="staging", bufs=3)
-        scaled = as_halves(staging[:, : S // 2])
-        rows = new_rows(2, M_PASSES)
-        saturate(first_product(2, 0), 0, quarters(half_state[4]), scaled, rows[:, 0])
-        saturate(first_product(2, 1), 1, free_quarters(), scaled, rows[:, 1])
-        pick_state(4)
-        grouped = new_h_home(2)
-        turn_back(grouped, as_pairs(staging[:, S // 2 :]), rows, "first3", 0, M_PASSES)
-        quantise_h(2, grouped)
-
-        for i in range(2, TILES):
-            staging = ring.tile([P, S], F32, name="staging", bufs=3)
-            half_y[i] = staging[:]
-            if i + 1 < TILES:
-                picks = {2: (5, 6), 3: (7,)}.get(i, ())
-                for j in picks:
-                    new_half_state(j)
-                scaled = as_halves(staging[:, : S // 2])
-                rows = new_rows(2 * (i % 2), M_PASSES)
-                saturate(first_product(i + 1, 0), 0, free_quarters(), scaled, rows[:, 0])
-                second = quarters(*[half_state[j] for j in picks]) if picks else free_quarters()
-                saturate(first_product(i + 1, 1), 1, second, scaled, rows[:, 1])
-                for j in picks:
-                    pick_state(j)
-                grouped = new_h_home(i + 1)
-                turn_back(grouped, as_pairs(staging[:, S // 2 :]), rows, "first%d" % (2 * (i % 2) + 1), 0, M_PASSES)
-                quantise_h(i + 1, grouped)
-            if i + 3 < TILES:
-                grouped = cast_contact(i + 3, h_home[i][:], ((0, 3),))
-                quantise_contact(i + 3, grouped, ring.tile([P, K_PASSES * P], U32, name="contact_codes", bufs=3, align_bytes=64))
-            ys = [second_product(i, u) for u in range(S // BANK)]
+            make_h(sums[b], b, half_state[7][:, b * PASS : b * PASS + QUARTER], grouped)
+            quantise_h(0, grouped, b, b + 1)
+            pick_state(7, b * PASS, (b + 1) * PASS)
             for u in range(S // BANK):
-                halve_y(i, u, ys[u])
-            put_back(i, 0, S)
-            store(i)
+                second_pass(0, ys[u], u, b)
+        put_back(0, 0, BANK, halve_y(first_half_home(), ys[0]))
+        home = held.tile([P, GROUPED], F32, name="second_home", align_bytes=64)
+        quantise_contact(1, cast_contact(1, home[:], WHOLE), WHOLE)
+        sums = first_product(1)
+        home = held.tile([P, BANK], F32, name="contact_raw1", align_bytes=64)
+        put_back(0, BANK, S, halve_y(home[:], ys[1]))
+        store(0)
+        home = held.tile([P, GROUPED], F32, name="first_home", align_bytes=64)
+        quantise_contact(2, cast_contact(2, home[:], WHOLE), WHOLE)
+        half_state[6] = held.tile([P, S], F32, name="contact_raw2", align_bytes=64)
+        pick_state(6, 0, S)
+
+        for j in range(1, TILES):
+            if j == 1:
+                stage = held.tile([P, GROUPED + S], F32, name="first_stage", align_bytes=64)
+            else:
+                stage = ring.tile([P, GROUPED + BANK], F32, name="stage", bufs=3, align_bytes=64)
+            grouped = new_grouped()
+            make_h(sums[0], 0, stage[:, :QUARTER], grouped)
+            make_h(sums[1], 1, stage[:, GROUPED - P : GROUPED + P], grouped)
+            new_h_mx(j)
+            quantise_h(j, grouped, 0, M_PASSES)
+            if j == 1:
+                half_state[1] = stage[:, GROUPED:]
+                pick_state(1, 0, S)
+            else:
+                put_back(j - 1, BANK, S, halve_y(stage[:, GROUPED:], ys[1]))
+                store(j - 1)
+            ys = second_product(j)
+            if j + 1 < TILES:
+                sums = first_product(j + 1)
+            if j + 2 < TILES:
+                grouped = cast_contact(j + 2, stage[:, :GROUPED], WHOLE)
+                if j > 1:
+                    half_state[j] = held.tile([P, S], F32, name="contact_raw%d" % (j + 2), align_bytes=64)
+                    pick_state(j, 0, S)
+                quantise_contact(j + 2, grouped, WHOLE)
+            if j + 1 < TILES:
+                put_back(j, 0, BANK, halve_y(first_half_home(), ys[0]))
+            else:
+                both = held.tile([P, S], F32, name="half_state0")
+                for u in range(S // BANK):
+                    halve_y(both[:, u * BANK : (u + 1) * BANK], ys[u])
+                put_back(j, 0, S, both[:])
+                store(j)

@@ -1,6 +1,7 @@
 from contextlib import ExitStack
 
 import concourse.mybir as mybir
+from concourse.masks import make_identity
 
 K, T, S, N = 1536, 2048, 1024, 1024
 FLOPS = 2 * K * S * N + 2 * S * S * N
@@ -41,14 +42,23 @@ def tile_list_vowel_shift_kernel(tc, tab_words, tab_scales, offs, gT, contact, b
         nc.vector.memset(wr_planes[:].rearrange("p a c -> p (a c)").bitcast(I32), 0)
         nc.vector.memset(halves[:], 0.5)
 
-        bias_cols = held.tile([P, M_PASSES, PACK], F32, name="bias_cols")
-        gain_cols = held.tile([P, M_PASSES, PACK], F32, name="gain_cols")
-        nc.gpsimd.dma_start(bias_cols[:], bias.rearrange("(b p t) -> p b t", b=M_PASSES, t=PACK))
-        nc.gpsimd.dma_start(gain_cols[:], gain.rearrange("(b p t) -> p b t", b=M_PASSES, t=PACK))
+        identity = held.tile([P, P], F32, name="identity")
+        make_identity(nc, identity[:])
+        vectors = held.tile([P, P], F32, name="vectors")
+        nc.vector.memset(vectors[:], 0.0)
+        nc.gpsimd.dma_start(vectors[0:CHUNKS, :], bias.rearrange("(c m) -> c m", c=CHUNKS))
+        nc.gpsimd.dma_start(vectors[CHUNKS : 2 * CHUNKS, :], gain.rearrange("(c m) -> c m", c=CHUNKS))
+        identity_bf16 = held.tile([P, P], BF16, name="identity_bf16")
+        nc.scalar.copy(identity_bf16[:], identity[:])
+        turned = psum.tile([P, P], F32, name="y1")
+        nc.tensor.transpose(turned[:], vectors[:], identity[:])
+        columns = held.tile([P, 2 * CHUNKS], F32, name="columns")
+        nc.scalar.copy(columns[:], turned[:, : 2 * CHUNKS])
 
         table_words = []
         contact_raw = {}
         state = {}
+        homes = {}
 
         def load_table(a):
             words = held.tile([P, T], U32, name="table_words%d" % a, align_bytes=64)
@@ -56,7 +66,11 @@ def tile_list_vowel_shift_kernel(tc, tab_words, tab_scales, offs, gT, contact, b
             table_words.append(words)
 
         def load_contact(i):
-            raw = held.tile([P, K_PASSES, PACK, P], F32, name="contact_raw%d" % i, align_bytes=64)
+            if i == 1:
+                homes["first_y"] = held.tile([P, BANK + K_PASSES * PASS], F32, name="first_y", align_bytes=64)
+                raw = homes["first_y"][:, BANK:].rearrange("p (a j n) -> p a j n", a=K_PASSES, j=PACK)
+            else:
+                raw = held.tile([P, K_PASSES, PACK, P], F32, name="contact_raw%d" % i, align_bytes=64)[:]
             for a in range(K_PASSES):
                 rows = contact[a * PASS : (a + 1) * PASS, i * P : (i + 1) * P]
                 nc.sync.dma_start(raw[:, a], rows.rearrange("(p j) n -> p j n", j=PACK))
@@ -69,16 +83,17 @@ def tile_list_vowel_shift_kernel(tc, tab_words, tab_scales, offs, gT, contact, b
 
         load_table(0)
         nc.sync.dma_start(offsets[:], offs)
+        load_table(1)
         for q in range(4):
-            nc.scalar.dma_start(
+            nc.sync.dma_start(
                 table_scales[32 * q : 32 * q + 4 * K_PASSES, :].bitcast(I32),
                 tab_scales[:, 4 * q : 4 * q + 4, :].bitcast(I32),
             )
-        load_table(1)
         load_contact(0)
         load_table(2)
         load_state(0)
         load_state(7)
+        load_state(6)
         wr_codes = held.tile([P, M_PASSES, 2 * S], U8, name="wr_codes", align_bytes=64)
         nc.sync.dma_start(wr_codes[:].bitcast(I32), wr_words.rearrange("a p c -> p a c").bitcast(I32))
         for q in range(4):
@@ -88,22 +103,25 @@ def tile_list_vowel_shift_kernel(tc, tab_words, tab_scales, offs, gT, contact, b
             )
         load_contact(1)
         load_contact(2)
-        load_state(6)
-        for i in range(3, TILES):
-            load_contact(i)
-            load_state(i - 2)
+        load_state(5)
+        load_state(1)
+        load_contact(3)
+        load_contact(4)
+        load_state(2)
+        load_contact(5)
+        load_state(3)
+        load_contact(6)
+        load_state(4)
+        load_contact(7)
 
         picked_words = [held.tile([P, S], U32, name="picked_words%d" % a, align_bytes=64) for a in range(K_PASSES)]
         picked_scales = held.tile([P, S], U8, name="picked_scales", align_bytes=64)
-
-        def dealt(tile):
-            return tile[:].rearrange("p (b t q) -> p b q t", b=M_PASSES, t=PACK)
 
         def listed(c0, c1):
             return offsets[:, c0 // 16 : c1 // 16]
 
         def pick_words(a, b0, b1):
-            nc.vector.tensor_copy(dealt(picked_words[a])[:, b0:b1], table_words[a][:].indirect(listed(b0 * PASS, b1 * PASS)))
+            nc.vector.tensor_copy(picked_words[a][:, b0 * PASS : b1 * PASS], table_words[a][:].indirect(listed(b0 * PASS, b1 * PASS)))
 
         contact_mx = {}
         h_mx = {}
@@ -116,7 +134,7 @@ def tile_list_vowel_shift_kernel(tc, tab_words, tab_scales, offs, gT, contact, b
             for a0, a1 in steps:
                 nc.scalar.copy(
                     grouped.rearrange("p (a c i t) -> p a c t i", a=K_PASSES, i=4, t=PACK)[:, a0:a1],
-                    contact_raw[i][:].rearrange("p a t (c i) -> p a c t i", i=4)[:, a0:a1],
+                    contact_raw[i].rearrange("p a t (c i) -> p a c t i", i=4)[:, a0:a1],
                 )
             return grouped
 
@@ -143,7 +161,7 @@ def tile_list_vowel_shift_kernel(tc, tab_words, tab_scales, offs, gT, contact, b
             )
 
         def new_sums(i, b):
-            return psum.tile([P, PACK, P], F32, name="e%d" % (2 * (i % 2) + b))
+            return psum.tile([P, PACK, P], F32, name="e%d" % b)
 
         def first_product(i):
             sums = []
@@ -155,16 +173,28 @@ def tile_list_vowel_shift_kernel(tc, tab_words, tab_scales, offs, gT, contact, b
                 sums.append(e)
             return sums
 
-        def make_h(e, b, scaled, grouped):
+        def make_h(e, b, scaled, pairs, grouped):
             saturated = ring.tile([P, PACK, P], F32, name="saturated")
             scaled = scaled.bitcast(BF16)
+            rows = psum.tile([P, PASS], BF16, name="rows%d" % b)
             for t in range(PACK):
-                nc.scalar.activation(saturated[:, t, :], e[:, t, :], ACT.Tanh, bias=bias_cols[:, b, t : t + 1])
+                c = PACK * b + t
+                nc.scalar.activation(saturated[:, t, :], e[:, t, :], ACT.Tanh, bias=columns[:, c : c + 1])
             for t in range(PACK):
-                nc.scalar.activation(scaled[:, t * P : (t + 1) * P], saturated[:, t, :], ACT.Copy, scale=gain_cols[:, b, t : t + 1])
+                c = CHUNKS + PACK * b + t
+                cols = slice(t * P, (t + 1) * P)
+                nc.scalar.activation(scaled[:, cols], saturated[:, t, :], ACT.Copy, scale=columns[:, c : c + 1])
+                nc.tensor.transpose(rows[:, cols], scaled[:, cols], identity_bf16[:])
             nc.scalar.copy(
-                grouped[:, b * PASS : (b + 1) * PASS].rearrange("p (c i t) -> p c t i", i=4, t=PACK),
-                scaled.rearrange("p (t c i) -> p c t i", i=4, t=PACK),
+                pairs.rearrange("p (u q) -> p u q", u=2),
+                rows[:].bitcast(F32).rearrange("p (q u) -> p u q", u=2),
+            )
+            back = psum.tile([P, 2, P], F32, name="e%d" % b)
+            for u in range(2):
+                nc.tensor.transpose(back[:, u, :], pairs[:, u * P : (u + 1) * P], identity[:])
+            nc.scalar.copy(
+                grouped[:, b * PASS : (b + 1) * PASS].bitcast(F32).rearrange("p (n u) -> p n u", u=2),
+                back[:].rearrange("p u n -> p n u"),
             )
 
         def new_grouped():
@@ -175,8 +205,8 @@ def tile_list_vowel_shift_kernel(tc, tab_words, tab_scales, offs, gT, contact, b
             nc.vector.quantize_mx(h_codes[:, b0 * P : b1 * P].bitcast(FP8X4), h_scales[:, b0 * P : b1 * P], grouped[:, b0 * PASS : b1 * PASS])
 
         def new_h_mx(i):
-            if i == 0:
-                h_codes = held.tile([P, M_PASSES * P], U32, name="second_home", align_bytes=64)
+            if i in (0, 4):
+                h_codes = held.tile([P, M_PASSES * P], U32, name="h4_codes" if i else "second_home", align_bytes=64)
             else:
                 h_codes = ring.tile([P, M_PASSES * P], U32, name="h_codes", align_bytes=64)
             h_scales = ring.tile([P, M_PASSES * P], U8, name="h_scales", align_bytes=64)
@@ -208,7 +238,7 @@ def tile_list_vowel_shift_kernel(tc, tab_words, tab_scales, offs, gT, contact, b
             return ys
 
         def halve_y(home, y):
-            nc.scalar.activation(home, y[:], ACT.Copy, scale=0.5)
+            nc.scalar.activation(home, y, ACT.Copy, scale=0.5)
             return home
 
         def put_back(i, c0, c1, half_y):
@@ -222,10 +252,12 @@ def tile_list_vowel_shift_kernel(tc, tab_words, tab_scales, offs, gT, contact, b
 
         QUARTER = PASS // 2
         WHOLE = ((0, K_PASSES),)
+        FIRST_PIECE = 384
+        HELD = P // 2
 
         pick_words(0, 0, M_PASSES)
-        nc.vector.tensor_copy(dealt(picked_scales), table_scales[:].indirect(offsets[:]))
         pick_words(1, 0, M_PASSES)
+        nc.vector.tensor_copy(picked_scales[:], table_scales[:].indirect(offsets[:]))
         first_home = held.tile([P, GROUPED], F32, name="first_home", align_bytes=64)
         grouped = cast_contact(0, first_home[:], ((0, 1), (1, 2), (2, 3)))
         quantise_contact(0, grouped, ((0, 2), (2, 3)))
@@ -240,58 +272,83 @@ def tile_list_vowel_shift_kernel(tc, tab_words, tab_scales, offs, gT, contact, b
                 first_pass(0, sums[b], K_PASSES - 1, b, t, False, t == PACK - 1)
         half_state[0] = held.tile([P, S], F32, name="half_state0")
         pick_state(0, 0, S)
-        half_state[7] = held.tile([P, S], F32, name="half_state7", align_bytes=64)
-        grouped = new_grouped()
+        half_state[7] = held.tile([P, S], F32, name="half_state7")
+        pick_state(7, 0, S)
+        half_state[6] = held.tile([P, S], F32, name="half_state6", align_bytes=64)
+        grouped = half_state[6][:, :PASS].bitcast(BF16)
+        stage = ring.tile([P, GROUPED + BANK], F32, name="stage", bufs=3, align_bytes=64)
         new_h_mx(0)
-        ys = [new_y(u) for u in range(S // BANK)]
         for b in range(M_PASSES):
-            make_h(sums[b], b, half_state[7][:, b * PASS : b * PASS + QUARTER], grouped)
-            quantise_h(0, grouped, b, b + 1)
-            pick_state(7, b * PASS, (b + 1) * PASS)
-            for u in range(S // BANK):
-                second_pass(0, ys[u], u, b)
-        put_back(0, 0, BANK, halve_y(first_half_home(), ys[0]))
+            make_h(sums[b], b, stage[:, 2 * b * QUARTER : (2 * b + 1) * QUARTER], stage[:, (2 * b + 1) * QUARTER : (2 * b + 2) * QUARTER], grouped)
+        quantise_h(0, grouped, 0, M_PASSES)
+        pick_state(6, 0, S)
+        ys = second_product(0)
+        both = homes["first_y"]
+        halve_y(both[:, :BANK], ys[0][:])
+        put_back(0, 0, FIRST_PIECE, both[:, :FIRST_PIECE])
         home = held.tile([P, GROUPED], F32, name="second_home", align_bytes=64)
         quantise_contact(1, cast_contact(1, home[:], WHOLE), WHOLE)
         sums = first_product(1)
-        home = held.tile([P, BANK], F32, name="contact_raw1", align_bytes=64)
-        put_back(0, BANK, S, halve_y(home[:], ys[1]))
+        halve_y(both[:, BANK:S], ys[1][:])
+        put_back(0, FIRST_PIECE, S, both[:, FIRST_PIECE:S])
         store(0)
         home = held.tile([P, GROUPED], F32, name="first_home", align_bytes=64)
         quantise_contact(2, cast_contact(2, home[:], WHOLE), WHOLE)
-        half_state[6] = held.tile([P, S], F32, name="contact_raw2", align_bytes=64)
-        pick_state(6, 0, S)
+        half_state[5] = held.tile([P, S], F32, name="contact_raw2", align_bytes=64)
+        pick_state(5, 0, S)
 
-        for j in range(1, TILES):
-            if j == 1:
-                stage = held.tile([P, GROUPED + S], F32, name="first_stage", align_bytes=64)
-            else:
-                stage = ring.tile([P, GROUPED + BANK], F32, name="stage", bufs=3, align_bytes=64)
-            grouped = new_grouped()
-            make_h(sums[0], 0, stage[:, :QUARTER], grouped)
-            make_h(sums[1], 1, stage[:, GROUPED - P : GROUPED + P], grouped)
+        def h_round(j, sums, stage, grouped):
+            make_h(sums[0], 0, stage[:, :QUARTER], stage[:, GROUPED + P : GROUPED + P + QUARTER], grouped)
+            make_h(sums[1], 1, stage[:, QUARTER : 2 * QUARTER], stage[:, GROUPED - 3 * P // 2 : GROUPED + P // 2], grouped)
             new_h_mx(j)
             quantise_h(j, grouped, 0, M_PASSES)
-            if j == 1:
-                half_state[1] = stage[:, GROUPED:]
-                pick_state(1, 0, S)
-            else:
-                put_back(j - 1, BANK, S, halve_y(stage[:, GROUPED:], ys[1]))
-                store(j - 1)
+
+        stage = ring.tile([P, GROUPED + BANK], F32, name="stage", bufs=3, align_bytes=64)
+        half_state[1] = held.tile([P, S], F32, name="half_state1", align_bytes=64)
+        h_round(1, sums, stage, half_state[1][:, :PASS].bitcast(BF16))
+        pick_state(1, 0, S)
+        ys = second_product(1)
+        sums = first_product(2)
+        put_back(1, 0, BANK, halve_y(first_half_home(), ys[0][:]))
+
+        stage = held.tile([P, GROUPED + BANK], F32, name="second_stage", align_bytes=64)
+        h_round(2, sums, stage, new_grouped()[:])
+        put_back(1, BANK, BANK + QUARTER, halve_y(stage[:, GROUPED : GROUPED + QUARTER], ys[1][:, :QUARTER]))
+        quantise_contact(3, cast_contact(3, stage[:, :GROUPED], WHOLE), WHOLE)
+        home = held.tile([P, QUARTER + GROUPED], F32, name="contact_raw3", align_bytes=64)
+        put_back(1, BANK + QUARTER, S, halve_y(home[:, :QUARTER], ys[1][:, QUARTER:]))
+        store(1)
+        ys = second_product(2)
+        sums = first_product(3)
+        half_state[2] = held.tile([P, S], F32, name="second_stage", align_bytes=64)
+        pick_state(2, 0, S)
+        quantise_contact(4, cast_contact(4, home[:, QUARTER:], WHOLE), WHOLE)
+        home = held.tile([P, BANK], F32, name="contact_raw4", align_bytes=64)
+        put_back(2, 0, BANK, halve_y(home[:], ys[0][:]))
+
+        for j in range(3, TILES):
+            stage = ring.tile([P, GROUPED + BANK], F32, name="stage", bufs=3, align_bytes=64)
+            h_round(j, sums, stage, new_grouped()[:])
+            halve_y(stage[:, GROUPED + HELD :], ys[1][:, HELD:])
+            halve_y(stage[:, GROUPED : GROUPED + HELD], ys[1][:, :HELD])
+            put_back(j - 1, BANK, S, stage[:, GROUPED:])
+            store(j - 1)
             ys = second_product(j)
             if j + 1 < TILES:
                 sums = first_product(j + 1)
-            if j + 2 < TILES:
+            if j not in half_state:
                 grouped = cast_contact(j + 2, stage[:, :GROUPED], WHOLE)
-                if j > 1:
-                    half_state[j] = held.tile([P, S], F32, name="contact_raw%d" % (j + 2), align_bytes=64)
-                    pick_state(j, 0, S)
+                half_state[j] = held.tile([P, S], F32, name="contact_raw%d" % (j + 2), align_bytes=64)
+                pick_state(j, 0, S)
                 quantise_contact(j + 2, grouped, WHOLE)
             if j + 1 < TILES:
-                put_back(j, 0, BANK, halve_y(first_half_home(), ys[0]))
+                put_back(j, 0, BANK, halve_y(first_half_home(), ys[0][:]))
+                if j == 4:
+                    home = held.tile([P, GROUPED], F32, name="h4_codes", align_bytes=64)
+                    quantise_contact(7, cast_contact(7, home[:], WHOLE), WHOLE)
             else:
                 both = held.tile([P, S], F32, name="half_state0")
                 for u in range(S // BANK):
-                    halve_y(both[:, u * BANK : (u + 1) * BANK], ys[u])
+                    halve_y(both[:, u * BANK : (u + 1) * BANK], ys[u][:])
                 put_back(j, 0, S, both[:])
                 store(j)

@@ -25,6 +25,7 @@ M_PASSES = S // PASS
 TILES = N // P
 CHUNKS = S // P
 BANK = 512
+SPARE = M_PASSES * P // 4
 
 
 def tile_list_vowel_shift_kernel(tc, tab_words, tab_scales, offs, gT, contact, bias, gain, wr_words, wr_scales, out):
@@ -37,17 +38,17 @@ def tile_list_vowel_shift_kernel(tc, tab_words, tab_scales, offs, gT, contact, b
         offsets = held.tile([P, S // 16], U16, name="offsets")
         table_scales = held.tile([P, T], U8, name="table_scales", align_bytes=64)
         wr_planes = held.tile([P, M_PASSES, S], U8, name="wr_planes", align_bytes=64)
-        halves = held.tile([P, S], F32, name="halves")
+        halves = held.tile([P, S + SPARE], F32, name="halves", align_bytes=64)
+        vectors = held.tile([P, P], F32, name="vectors")
+        nc.vector.memset(vectors[:], 0.0)
         nc.vector.memset(table_scales[:].bitcast(I32), 0)
         nc.vector.memset(wr_planes[:].rearrange("p a c -> p (a c)").bitcast(I32), 0)
         nc.vector.memset(halves[:], 0.5)
 
         identity = held.tile([P, P], F32, name="identity")
         make_identity(nc, identity[:])
-        vectors = held.tile([P, P], F32, name="vectors")
-        nc.vector.memset(vectors[:], 0.0)
-        nc.gpsimd.dma_start(vectors[0:CHUNKS, :], bias.rearrange("(c m) -> c m", c=CHUNKS))
-        nc.gpsimd.dma_start(vectors[CHUNKS : 2 * CHUNKS, :], gain.rearrange("(c m) -> c m", c=CHUNKS))
+        nc.scalar.dma_start(vectors[0:CHUNKS, :], bias.rearrange("(c m) -> c m", c=CHUNKS))
+        nc.scalar.dma_start(vectors[CHUNKS : 2 * CHUNKS, :], gain.rearrange("(c m) -> c m", c=CHUNKS))
         identity_bf16 = held.tile([P, P], BF16, name="identity_bf16")
         nc.scalar.copy(identity_bf16[:], identity[:])
         turned = psum.tile([P, P], F32, name="y1")
@@ -120,8 +121,8 @@ def tile_list_vowel_shift_kernel(tc, tab_words, tab_scales, offs, gT, contact, b
         def listed(c0, c1):
             return offsets[:, c0 // 16 : c1 // 16]
 
-        def pick_words(a, b0, b1):
-            nc.vector.tensor_copy(picked_words[a][:, b0 * PASS : b1 * PASS], table_words[a][:].indirect(listed(b0 * PASS, b1 * PASS)))
+        def pick_words(a, c0, c1):
+            nc.vector.tensor_copy(picked_words[a][:, c0:c1], table_words[a][:].indirect(listed(c0, c1)))
 
         contact_mx = {}
         h_mx = {}
@@ -151,7 +152,7 @@ def tile_list_vowel_shift_kernel(tc, tab_words, tab_scales, offs, gT, contact, b
             codes, scales = contact_mx[i]
             cols = slice(b * PASS + t * P, b * PASS + (t + 1) * P)
             nc.tensor.matmul_mx(
-                e[:, t, :],
+                e,
                 lhsT=picked_words[a][:, cols].bitcast(FP8X4),
                 lhsT_scale=picked_scales[4 * a : P, cols],
                 rhs=codes[:, a * P : (a + 1) * P].bitcast(FP8X4),
@@ -160,17 +161,18 @@ def tile_list_vowel_shift_kernel(tc, tab_words, tab_scales, offs, gT, contact, b
                 stop=stop,
             )
 
-        def new_sums(i, b):
-            return psum.tile([P, PACK, P], F32, name="e%d" % b)
+        def new_sums(banks):
+            per_bank = CHUNKS // len(banks)
+            tiles = [psum.tile([P, per_bank, P], F32, name=bank) for bank in banks]
+            chunks = [tiles[c // per_bank][:, c % per_bank, :] for c in range(CHUNKS)]
+            return [chunks[:PACK], chunks[PACK:]]
 
-        def first_product(i):
-            sums = []
+        def first_product(i, banks=("e0", "e1")):
+            sums = new_sums(banks)
             for b in range(M_PASSES):
-                e = new_sums(i, b)
                 for t in range(PACK):
                     for a in range(K_PASSES):
-                        first_pass(i, e, a, b, t, a == 0, a == K_PASSES - 1)
-                sums.append(e)
+                        first_pass(i, sums[b][t], a, b, t, a == 0, a == K_PASSES - 1)
             return sums
 
         def make_h(e, b, scaled, pairs, grouped):
@@ -179,7 +181,7 @@ def tile_list_vowel_shift_kernel(tc, tab_words, tab_scales, offs, gT, contact, b
             rows = psum.tile([P, PASS], BF16, name="rows%d" % b)
             for t in range(PACK):
                 c = PACK * b + t
-                nc.scalar.activation(saturated[:, t, :], e[:, t, :], ACT.Tanh, bias=columns[:, c : c + 1])
+                nc.scalar.activation(saturated[:, t, :], e[t], ACT.Tanh, bias=columns[:, c : c + 1])
             for t in range(PACK):
                 c = CHUNKS + PACK * b + t
                 cols = slice(t * P, (t + 1) * P)
@@ -209,11 +211,15 @@ def tile_list_vowel_shift_kernel(tc, tab_words, tab_scales, offs, gT, contact, b
                 h_codes = held.tile([P, M_PASSES * P], U32, name="h4_codes" if i else "second_home", align_bytes=64)
             else:
                 h_codes = ring.tile([P, M_PASSES * P], U32, name="h_codes", align_bytes=64)
-            h_scales = ring.tile([P, M_PASSES * P], U8, name="h_scales", align_bytes=64)
+            if i == 0:
+                h_scales = halves[:, S:].bitcast(U8)
+            else:
+                h_scales = ring.tile([P, M_PASSES * P], U8, name="h_scales", align_bytes=64)
             h_mx[i] = (h_codes, h_scales)
 
         def pick_state(i, c0, c1):
-            nc.vector.tensor_tensor(half_state[i][:, c0:c1], state[i][:].indirect(listed(c0, c1)), halves[:, c0:c1], ALU.mult)
+            shift = SPARE if i == 7 else 0
+            nc.vector.tensor_tensor(half_state[i][:, c0:c1], state[i][:].indirect(listed(c0, c1)), halves[:, shift + c0 : shift + c1], ALU.mult)
 
         def second_pass(i, y, u, b):
             h_codes, h_scales = h_mx[i]
@@ -253,23 +259,24 @@ def tile_list_vowel_shift_kernel(tc, tab_words, tab_scales, offs, gT, contact, b
         QUARTER = PASS // 2
         WHOLE = ((0, K_PASSES),)
         FIRST_PIECE = 384
+        FOUR_BANKS = ("e0", "spare0", "e1", "spare1")
         HELD = P // 2
 
-        pick_words(0, 0, M_PASSES)
-        pick_words(1, 0, M_PASSES)
+        pick_words(0, 0, S)
+        pick_words(1, 0, S)
         nc.vector.tensor_copy(picked_scales[:], table_scales[:].indirect(offsets[:]))
         first_home = held.tile([P, GROUPED], F32, name="first_home", align_bytes=64)
         grouped = cast_contact(0, first_home[:], ((0, 1), (1, 2), (2, 3)))
         quantise_contact(0, grouped, ((0, 2), (2, 3)))
-        sums = [new_sums(0, b) for b in range(M_PASSES)]
+        sums = new_sums(FOUR_BANKS)
         for b in range(M_PASSES):
             for a in range(K_PASSES - 1):
                 for t in range(PACK):
-                    first_pass(0, sums[b], a, b, t, a == 0 and t == 0, False)
-        for b in range(M_PASSES):
-            pick_words(2, b, b + 1)
-            for t in range(PACK):
-                first_pass(0, sums[b], K_PASSES - 1, b, t, False, t == PACK - 1)
+                    first_pass(0, sums[b][t], a, b, t, a == 0 and t % 2 == 0, False)
+        for c in range(0, CHUNKS, 2):
+            pick_words(2, c * P, (c + 2) * P)
+            for t in (c % PACK, c % PACK + 1):
+                first_pass(0, sums[c // PACK][t], K_PASSES - 1, c // PACK, t, False, t % 2 == 1)
         half_state[0] = held.tile([P, S], F32, name="half_state0")
         pick_state(0, 0, S)
         half_state[7] = held.tile([P, S], F32, name="half_state7")
@@ -288,12 +295,11 @@ def tile_list_vowel_shift_kernel(tc, tab_words, tab_scales, offs, gT, contact, b
         put_back(0, 0, FIRST_PIECE, both[:, :FIRST_PIECE])
         home = held.tile([P, GROUPED], F32, name="second_home", align_bytes=64)
         quantise_contact(1, cast_contact(1, home[:], WHOLE), WHOLE)
-        sums = first_product(1)
+        sums = first_product(1, FOUR_BANKS)
         halve_y(both[:, BANK:S], ys[1][:])
         put_back(0, FIRST_PIECE, S, both[:, FIRST_PIECE:S])
         store(0)
-        home = held.tile([P, GROUPED], F32, name="first_home", align_bytes=64)
-        quantise_contact(2, cast_contact(2, home[:], WHOLE), WHOLE)
+        quantise_contact(2, cast_contact(2, both[:, S : S + GROUPED], WHOLE), WHOLE)
         half_state[5] = held.tile([P, S], F32, name="contact_raw2", align_bytes=64)
         pick_state(5, 0, S)
 

@@ -25,7 +25,13 @@ M_PASSES = S // PASS
 TILES = N // P
 CHUNKS = S // P
 BANK = 512
-SPARE = M_PASSES * P // 4
+GROUPED = K_PASSES * PASS // 2
+QUARTER = PASS // 2
+LEAD = 128
+RESTORED = 16
+FIRST_PIECE = 384
+HELD = 64
+LAST_CUT = 384
 
 
 def tile_list_vowel_shift_kernel(tc, tab_words, tab_scales, offs, gT, contact, bias, gain, wr_words, wr_scales, out):
@@ -38,12 +44,14 @@ def tile_list_vowel_shift_kernel(tc, tab_words, tab_scales, offs, gT, contact, b
         offsets = held.tile([P, S // 16], U16, name="offsets")
         table_scales = held.tile([P, T], U8, name="table_scales", align_bytes=64)
         wr_planes = held.tile([P, M_PASSES, S], U8, name="wr_planes", align_bytes=64)
-        halves = held.tile([P, S + SPARE], F32, name="halves", align_bytes=64)
+        halves = held.tile([P, QUARTER + S + QUARTER], F32, name="halves", align_bytes=64)
+        lead_halves = held.tile([P, LEAD], F32, name="lead_halves", align_bytes=64)
         vectors = held.tile([P, P], F32, name="vectors")
         nc.vector.memset(vectors[:], 0.0)
         nc.vector.memset(table_scales[:].bitcast(I32), 0)
         nc.vector.memset(wr_planes[:].rearrange("p a c -> p (a c)").bitcast(I32), 0)
-        nc.vector.memset(halves[:], 0.5)
+        nc.vector.memset(halves[:, QUARTER : QUARTER + S], 0.5)
+        nc.vector.memset(lead_halves[:], 0.5)
 
         identity = held.tile([P, P], F32, name="identity")
         make_identity(nc, identity[:])
@@ -60,6 +68,7 @@ def tile_list_vowel_shift_kernel(tc, tab_words, tab_scales, offs, gT, contact, b
         contact_raw = {}
         state = {}
         homes = {}
+        wr_codes = []
 
         def load_table(a):
             words = held.tile([P, T], U32, name="table_words%d" % a, align_bytes=64)
@@ -69,18 +78,25 @@ def tile_list_vowel_shift_kernel(tc, tab_words, tab_scales, offs, gT, contact, b
         def load_contact(i):
             if i == 1:
                 homes["first_y"] = held.tile([P, BANK + K_PASSES * PASS], F32, name="first_y", align_bytes=64)
-                raw = homes["first_y"][:, BANK:].rearrange("p (a j n) -> p a j n", a=K_PASSES, j=PACK)
+                raw = [homes["first_y"][:, BANK + (K_PASSES - 1 - a) * PASS : BANK + (K_PASSES - a) * PASS] for a in range(K_PASSES)]
             else:
-                raw = held.tile([P, K_PASSES, PACK, P], F32, name="contact_raw%d" % i, align_bytes=64)[:]
+                whole = held.tile([P, K_PASSES * PASS], F32, name="contact_raw%d" % i, align_bytes=64)
+                homes[i] = whole
+                raw = [whole[:, a * PASS : (a + 1) * PASS] for a in range(K_PASSES)]
             for a in range(K_PASSES):
                 rows = contact[a * PASS : (a + 1) * PASS, i * P : (i + 1) * P]
-                nc.sync.dma_start(raw[:, a], rows.rearrange("(p j) n -> p j n", j=PACK))
+                nc.sync.dma_start(raw[a].rearrange("p (j n) -> p j n", j=PACK), rows.rearrange("(p j) n -> p j n", j=PACK))
             contact_raw[i] = raw
 
         def load_state(i):
             rows = held.tile([P, T], F32, name="state%d" % i)
             nc.sync.dma_start(rows[:], gT[i * P : (i + 1) * P, :])
             state[i] = rows
+
+        def load_wr(u):
+            codes = held.tile([P, M_PASSES, 2 * BANK], U8, name="wr_codes%d" % u, align_bytes=64)
+            nc.sync.dma_start(codes[:].bitcast(I32), wr_words[:, :, 2 * u * BANK : 2 * (u + 1) * BANK].rearrange("a p c -> p a c").bitcast(I32))
+            wr_codes.append(codes)
 
         load_table(0)
         nc.sync.dma_start(offsets[:], offs)
@@ -93,26 +109,26 @@ def tile_list_vowel_shift_kernel(tc, tab_words, tab_scales, offs, gT, contact, b
         load_contact(0)
         load_table(2)
         load_state(0)
-        load_state(7)
-        load_state(6)
-        wr_codes = held.tile([P, M_PASSES, 2 * S], U8, name="wr_codes", align_bytes=64)
-        nc.sync.dma_start(wr_codes[:].bitcast(I32), wr_words.rearrange("a p c -> p a c").bitcast(I32))
+        load_state(1)
+        load_state(2)
         for q in range(4):
             nc.sync.dma_start(
                 wr_planes[32 * q : 32 * q + 4].bitcast(I32),
                 wr_scales[:, 4 * q : 4 * q + 4, :].rearrange("a r c -> r a c").bitcast(I32),
             )
+        load_wr(0)
+        load_wr(1)
         load_contact(1)
         load_contact(2)
+        load_state(3)
+        load_state(4)
         load_state(5)
-        load_state(1)
         load_contact(3)
         load_contact(4)
-        load_state(2)
+        load_state(6)
         load_contact(5)
-        load_state(3)
+        load_state(7)
         load_contact(6)
-        load_state(4)
         load_contact(7)
 
         picked_words = [held.tile([P, S], U32, name="picked_words%d" % a, align_bytes=64) for a in range(K_PASSES)]
@@ -127,19 +143,21 @@ def tile_list_vowel_shift_kernel(tc, tab_words, tab_scales, offs, gT, contact, b
         contact_mx = {}
         h_mx = {}
         half_state = {}
-        half_y = {}
-        GROUPED = K_PASSES * PASS // 2
 
-        def cast_contact(i, home, steps):
+        def cast_pass(i, home, a):
+            nc.scalar.copy(
+                home.bitcast(BF16)[:, a * PASS : (a + 1) * PASS].rearrange("p (c i t) -> p c t i", i=4, t=PACK),
+                contact_raw[i][a].rearrange("p (t c i) -> p c t i", t=PACK, i=4),
+            )
+
+        def cast_whole(i, home):
+            nc.scalar.copy(
+                home.bitcast(BF16).rearrange("p (a c i t) -> p a c t i", a=K_PASSES, i=4, t=PACK),
+                homes[i][:].rearrange("p (a t c i) -> p a c t i", a=K_PASSES, t=PACK, i=4),
+            )
+
+        def quantise_contact(i, home, steps=((0, K_PASSES),)):
             grouped = home.bitcast(BF16)
-            for a0, a1 in steps:
-                nc.scalar.copy(
-                    grouped.rearrange("p (a c i t) -> p a c t i", a=K_PASSES, i=4, t=PACK)[:, a0:a1],
-                    contact_raw[i].rearrange("p a t (c i) -> p a c t i", i=4)[:, a0:a1],
-                )
-            return grouped
-
-        def quantise_contact(i, grouped, steps):
             codes = ring.tile([P, K_PASSES * P], U32, name="contact_codes", bufs=3, align_bytes=64)
             scales = ring.tile([P, K_PASSES * P], U8, name="contact_scales", bufs=3, align_bytes=64)
             for a0, a1 in steps:
@@ -161,91 +179,101 @@ def tile_list_vowel_shift_kernel(tc, tab_words, tab_scales, offs, gT, contact, b
                 stop=stop,
             )
 
-        def new_sums(banks):
+        def turn_bank(i, k):
+            return "turn%d" % ((k - i) % 3)
+
+        def new_sums(i):
+            banks = [turn_bank(i, 0), turn_bank(i, 1)]
+            if i < 2:
+                banks = [banks[0], "spare0", banks[1], "spare1"]
             per_bank = CHUNKS // len(banks)
             tiles = [psum.tile([P, per_bank, P], F32, name=bank) for bank in banks]
             chunks = [tiles[c // per_bank][:, c % per_bank, :] for c in range(CHUNKS)]
             return [chunks[:PACK], chunks[PACK:]]
 
-        def first_product(i, banks=("e0", "e1")):
-            sums = new_sums(banks)
+        def first_product(i):
+            sums = new_sums(i)
             for b in range(M_PASSES):
                 for t in range(PACK):
                     for a in range(K_PASSES):
                         first_pass(i, sums[b][t], a, b, t, a == 0, a == K_PASSES - 1)
             return sums
 
-        def make_h(e, b, scaled, pairs, grouped):
+        def saturate(e, b):
             saturated = ring.tile([P, PACK, P], F32, name="saturated")
-            scaled = scaled.bitcast(BF16)
-            rows = psum.tile([P, PASS], BF16, name="rows%d" % b)
             for t in range(PACK):
                 c = PACK * b + t
                 nc.scalar.activation(saturated[:, t, :], e[t], ACT.Tanh, bias=columns[:, c : c + 1])
+            return saturated
+
+        def amplify(saturated, b, scaled, bank):
+            scaled = scaled.bitcast(BF16)
+            rows = psum.tile([P, PASS], BF16, name=bank)
             for t in range(PACK):
                 c = CHUNKS + PACK * b + t
                 cols = slice(t * P, (t + 1) * P)
                 nc.scalar.activation(scaled[:, cols], saturated[:, t, :], ACT.Copy, scale=columns[:, c : c + 1])
                 nc.tensor.transpose(rows[:, cols], scaled[:, cols], identity_bf16[:])
+            return rows
+
+        def turn_back(rows, pairs, bank, order=(0, 1)):
             nc.scalar.copy(
                 pairs.rearrange("p (u q) -> p u q", u=2),
                 rows[:].bitcast(F32).rearrange("p (q u) -> p u q", u=2),
             )
-            back = psum.tile([P, 2, P], F32, name="e%d" % b)
-            for u in range(2):
+            back = psum.tile([P, 2, P], F32, name=bank)
+            for u in order:
                 nc.tensor.transpose(back[:, u, :], pairs[:, u * P : (u + 1) * P], identity[:])
+            return back
+
+        def lay_out(back, b, grouped):
             nc.scalar.copy(
                 grouped[:, b * PASS : (b + 1) * PASS].bitcast(F32).rearrange("p (n u) -> p n u", u=2),
                 back[:].rearrange("p u n -> p n u"),
             )
 
-        def new_grouped():
-            return ring.tile([P, S], BF16, name="h_grouped", align_bytes=64)
-
-        def quantise_h(i, grouped, b0, b1):
-            h_codes, h_scales = h_mx[i]
-            nc.vector.quantize_mx(h_codes[:, b0 * P : b1 * P].bitcast(FP8X4), h_scales[:, b0 * P : b1 * P], grouped[:, b0 * PASS : b1 * PASS])
-
-        def new_h_mx(i):
-            if i in (0, 4):
-                h_codes = held.tile([P, M_PASSES * P], U32, name="h4_codes" if i else "second_home", align_bytes=64)
+        def make_h(i, sums, scaled, pairs, early, middle, late, order=(0, 1)):
+            grouped = ring.tile([P, S], BF16, name="h_grouped", align_bytes=64)
+            rows0 = amplify(saturate(sums[0], 0), 0, scaled[0], "fixed")
+            saturated1 = saturate(sums[1], 1)
+            early()
+            back0 = turn_back(rows0, pairs[0], "fixed")
+            rows1 = amplify(saturated1, 1, scaled[1], turn_bank(i, 2))
+            lay_out(back0, 0, grouped)
+            middle()
+            back1 = turn_back(rows1, pairs[1], turn_bank(i, 0), order)
+            late()
+            lay_out(back1, 1, grouped)
+            if i == 0:
+                h_codes = held.tile([P, M_PASSES * P], U32, name="second_home", align_bytes=64)
+                h_scales = lead_halves[:, : M_PASSES * P // 4].bitcast(U8)
             else:
                 h_codes = ring.tile([P, M_PASSES * P], U32, name="h_codes", align_bytes=64)
-            if i == 0:
-                h_scales = halves[:, S:].bitcast(U8)
-            else:
                 h_scales = ring.tile([P, M_PASSES * P], U8, name="h_scales", align_bytes=64)
+            nc.vector.quantize_mx(h_codes[:].bitcast(FP8X4), h_scales[:], grouped[:])
             h_mx[i] = (h_codes, h_scales)
 
-        def pick_state(i, c0, c1):
-            shift = SPARE if i == 7 else 0
-            nc.vector.tensor_tensor(half_state[i][:, c0:c1], state[i][:].indirect(listed(c0, c1)), halves[:, shift + c0 : shift + c1], ALU.mult)
-
-        def second_pass(i, y, u, b):
-            h_codes, h_scales = h_mx[i]
-            nc.tensor.matmul_mx(
-                y[:],
-                lhsT=h_codes[:, b * P : (b + 1) * P].bitcast(FP8X4),
-                lhsT_scale=h_scales[:, b * P : (b + 1) * P],
-                rhs=wr_codes[:, b, 2 * u * BANK : 2 * (u + 1) * BANK].bitcast(FP4X4),
-                rhs_scale=wr_planes[:, b, u * BANK : (u + 1) * BANK],
-                start=(b == 0),
-                stop=(b == M_PASSES - 1),
-            )
-
-        def new_y(u):
-            return psum.tile([P, BANK], F32, name="y%d" % u)
+        def pick_state(i, c0, c1, factor):
+            nc.vector.tensor_tensor(half_state[i][:, c0:c1], state[i][:].indirect(listed(c0, c1)), factor, ALU.mult)
 
         def second_product(i):
-            ys = [new_y(u) for u in range(S // BANK)]
+            h_codes, h_scales = h_mx[i]
+            ys = [psum.tile([P, BANK], F32, name="y%d" % u) for u in range(S // BANK)]
             for u in range(S // BANK):
                 for b in range(M_PASSES):
-                    second_pass(i, ys[u], u, b)
+                    nc.tensor.matmul_mx(
+                        ys[u][:],
+                        lhsT=h_codes[:, b * P : (b + 1) * P].bitcast(FP8X4),
+                        lhsT_scale=h_scales[:, b * P : (b + 1) * P],
+                        rhs=wr_codes[u][:, b, :].bitcast(FP4X4),
+                        rhs_scale=wr_planes[:, b, u * BANK : (u + 1) * BANK],
+                        start=(b == 0),
+                        stop=(b == M_PASSES - 1),
+                    )
             return ys
 
         def halve_y(home, y):
             nc.scalar.activation(home, y, ACT.Copy, scale=0.5)
-            return home
 
         def put_back(i, c0, c1, half_y):
             nc.vector.tensor_tensor(state[i][:].indirect(listed(c0, c1)), half_state[i][:, c0:c1], half_y, ALU.add)
@@ -253,22 +281,22 @@ def tile_list_vowel_shift_kernel(tc, tab_words, tab_scales, offs, gT, contact, b
         def store(i):
             nc.sync.dma_start(out[i * P : (i + 1) * P, :], state[i][:])
 
-        def first_half_home():
-            return ring.tile([P, BANK], F32, name="first_half_y")[:]
+        def new_stage():
+            return ring.tile([P, GROUPED + S - LAST_CUT], F32, name="stage", bufs=3, align_bytes=64)
 
-        QUARTER = PASS // 2
-        WHOLE = ((0, K_PASSES),)
-        FIRST_PIECE = 384
-        FOUR_BANKS = ("e0", "spare0", "e1", "spare1")
-        HELD = P // 2
+        def nothing():
+            return None
+
+        plain_halves = halves[:, QUARTER : QUARTER + S]
 
         pick_words(0, 0, S)
         pick_words(1, 0, S)
         nc.vector.tensor_copy(picked_scales[:], table_scales[:].indirect(offsets[:]))
         first_home = held.tile([P, GROUPED], F32, name="first_home", align_bytes=64)
-        grouped = cast_contact(0, first_home[:], ((0, 1), (1, 2), (2, 3)))
-        quantise_contact(0, grouped, ((0, 2), (2, 3)))
-        sums = new_sums(FOUR_BANKS)
+        for a in range(K_PASSES):
+            cast_pass(0, first_home[:], a)
+        quantise_contact(0, first_home[:], ((0, 2), (2, 3)))
+        sums = new_sums(0)
         for b in range(M_PASSES):
             for a in range(K_PASSES - 1):
                 for t in range(PACK):
@@ -277,84 +305,81 @@ def tile_list_vowel_shift_kernel(tc, tab_words, tab_scales, offs, gT, contact, b
             pick_words(2, c * P, (c + 2) * P)
             for t in (c % PACK, c % PACK + 1):
                 first_pass(0, sums[c // PACK][t], K_PASSES - 1, c // PACK, t, False, t % 2 == 1)
-        half_state[0] = held.tile([P, S], F32, name="half_state0")
-        pick_state(0, 0, S)
-        half_state[7] = held.tile([P, S], F32, name="half_state7")
-        pick_state(7, 0, S)
-        half_state[6] = held.tile([P, S], F32, name="half_state6", align_bytes=64)
-        grouped = half_state[6][:, :PASS].bitcast(BF16)
-        stage = ring.tile([P, GROUPED + BANK], F32, name="stage", bufs=3, align_bytes=64)
-        new_h_mx(0)
-        for b in range(M_PASSES):
-            make_h(sums[b], b, stage[:, 2 * b * QUARTER : (2 * b + 1) * QUARTER], stage[:, (2 * b + 1) * QUARTER : (2 * b + 2) * QUARTER], grouped)
-        quantise_h(0, grouped, 0, M_PASSES)
-        pick_state(6, 0, S)
+        freed = [held.tile([P, T], F32, name="table_words%d" % a, align_bytes=64) for a in range(K_PASSES)]
+        half_state[0] = freed[0][:, :S]
+        half_state[1] = freed[1][:, :S]
+        half_state[2] = freed[2][:, :S]
+        half_state[4] = freed[0][:, S:]
+        half_state[5] = freed[1][:, S:]
+        pick_state(0, 0, S, plain_halves)
+        pick_state(1, 0, LEAD, lead_halves[:])
+        pick_state(1, LEAD, S, plain_halves[:, LEAD:])
+        stage = new_stage()
+        make_h(0, sums, (stage[:, :QUARTER], stage[:, QUARTER:PASS]), (stage[:, PASS : PASS + QUARTER], halves[:, :QUARTER]), nothing, nothing, nothing)
+        nc.scalar.copy(halves[:, QUARTER - RESTORED : QUARTER], plain_halves[:, :RESTORED])
+        pick_state(2, 0, S, halves[:, QUARTER - RESTORED : QUARTER - RESTORED + S])
         ys = second_product(0)
         both = homes["first_y"]
         halve_y(both[:, :BANK], ys[0][:])
         put_back(0, 0, FIRST_PIECE, both[:, :FIRST_PIECE])
         home = held.tile([P, GROUPED], F32, name="second_home", align_bytes=64)
-        quantise_contact(1, cast_contact(1, home[:], WHOLE), WHOLE)
-        sums = first_product(1, FOUR_BANKS)
+        for a in range(K_PASSES):
+            cast_pass(1, home[:], a)
+        quantise_contact(1, home[:])
+        sums = first_product(1)
         halve_y(both[:, BANK:S], ys[1][:])
         put_back(0, FIRST_PIECE, S, both[:, FIRST_PIECE:S])
         store(0)
-        quantise_contact(2, cast_contact(2, both[:, S : S + GROUPED], WHOLE), WHOLE)
-        half_state[5] = held.tile([P, S], F32, name="contact_raw2", align_bytes=64)
-        pick_state(5, 0, S)
+        for a in range(K_PASSES):
+            cast_pass(2, both[:, S : S + GROUPED], a)
+        quantise_contact(2, both[:, S : S + GROUPED])
+        half_state[3] = held.tile([P, S], F32, name="contact_raw2", align_bytes=64)[:]
+        pick_state(3, 0, S, plain_halves)
+        stage = new_stage()
+        make_h(1, sums, (stage[:, :QUARTER], stage[:, QUARTER:PASS]), (stage[:, PASS : PASS + QUARTER], halves[:, QUARTER + S :]), nothing, nothing, nothing, (1, 0))
+        nc.scalar.copy(halves[:, QUARTER + S : QUARTER + S + RESTORED], plain_halves[:, :RESTORED])
+        for i in (4, 5):
+            pick_state(i, 0, S, halves[:, QUARTER + RESTORED : QUARTER + RESTORED + S])
 
-        def h_round(j, sums, stage, grouped):
-            make_h(sums[0], 0, stage[:, :QUARTER], stage[:, GROUPED + P : GROUPED + P + QUARTER], grouped)
-            make_h(sums[1], 1, stage[:, QUARTER : 2 * QUARTER], stage[:, GROUPED - 3 * P // 2 : GROUPED + P // 2], grouped)
-            new_h_mx(j)
-            quantise_h(j, grouped, 0, M_PASSES)
-
-        stage = ring.tile([P, GROUPED + BANK], F32, name="stage", bufs=3, align_bytes=64)
-        half_state[1] = held.tile([P, S], F32, name="half_state1", align_bytes=64)
-        h_round(1, sums, stage, half_state[1][:, :PASS].bitcast(BF16))
-        pick_state(1, 0, S)
-        ys = second_product(1)
-        sums = first_product(2)
-        put_back(1, 0, BANK, halve_y(first_half_home(), ys[0][:]))
-
-        stage = held.tile([P, GROUPED + BANK], F32, name="second_stage", align_bytes=64)
-        h_round(2, sums, stage, new_grouped()[:])
-        put_back(1, BANK, BANK + QUARTER, halve_y(stage[:, GROUPED : GROUPED + QUARTER], ys[1][:, :QUARTER]))
-        quantise_contact(3, cast_contact(3, stage[:, :GROUPED], WHOLE), WHOLE)
-        home = held.tile([P, QUARTER + GROUPED], F32, name="contact_raw3", align_bytes=64)
-        put_back(1, BANK + QUARTER, S, halve_y(home[:, :QUARTER], ys[1][:, QUARTER:]))
-        store(1)
-        ys = second_product(2)
-        sums = first_product(3)
-        half_state[2] = held.tile([P, S], F32, name="second_stage", align_bytes=64)
-        pick_state(2, 0, S)
-        quantise_contact(4, cast_contact(4, home[:, QUARTER:], WHOLE), WHOLE)
-        home = held.tile([P, BANK], F32, name="contact_raw4", align_bytes=64)
-        put_back(2, 0, BANK, halve_y(home[:], ys[0][:]))
-
-        for j in range(3, TILES):
-            stage = ring.tile([P, GROUPED + BANK], F32, name="stage", bufs=3, align_bytes=64)
-            h_round(j, sums, stage, new_grouped()[:])
-            halve_y(stage[:, GROUPED + HELD :], ys[1][:, HELD:])
-            halve_y(stage[:, GROUPED : GROUPED + HELD], ys[1][:, :HELD])
-            put_back(j - 1, BANK, S, stage[:, GROUPED:])
-            store(j - 1)
+        for j in range(1, TILES - 1):
+            sums = first_product(j + 1)
             ys = second_product(j)
-            if j + 1 < TILES:
-                sums = first_product(j + 1)
-            if j not in half_state:
-                grouped = cast_contact(j + 2, stage[:, :GROUPED], WHOLE)
-                half_state[j] = held.tile([P, S], F32, name="contact_raw%d" % (j + 2), align_bytes=64)
-                pick_state(j, 0, S)
-                quantise_contact(j + 2, grouped, WHOLE)
-            if j + 1 < TILES:
-                put_back(j, 0, BANK, halve_y(first_half_home(), ys[0][:]))
-                if j == 4:
-                    home = held.tile([P, GROUPED], F32, name="h4_codes", align_bytes=64)
-                    quantise_contact(7, cast_contact(7, home[:], WHOLE), WHOLE)
-            else:
-                both = held.tile([P, S], F32, name="half_state0")
-                for u in range(S // BANK):
-                    halve_y(both[:, u * BANK : (u + 1) * BANK], ys[u][:])
-                put_back(j, 0, S, both[:])
-                store(j)
+            stage = new_stage()
+            cut = LAST_CUT if j == TILES - 2 else BANK
+            waits = BANK - cut if cut < BANK else HELD
+            rest = stage[:, GROUPED : GROUPED + S - cut]
+            pairs0 = stage[:, GROUPED + P : GROUPED + P + QUARTER]
+            if j == 1:
+                early_home = held.tile([P, GROUPED], F32, name="first_home", align_bytes=64)
+                pairs0 = early_home[:, :QUARTER]
+
+            def first_piece():
+                half_y = ring.tile([P, BANK], F32, name="first_half_y")
+                halve_y(half_y[:, :cut], ys[0][:, :cut])
+                put_back(j, 0, cut, half_y[:, :cut])
+
+            def early_contact():
+                if j == 1:
+                    cast_whole(3, early_home[:])
+                    quantise_contact(3, early_home[:])
+
+            def free_part():
+                halve_y(rest[:, waits:], ys[1][:, waits - (BANK - cut) :])
+
+            make_h(j + 1, sums, (stage[:, :QUARTER], stage[:, QUARTER:PASS]), (pairs0, stage[:, GROUPED + HELD - QUARTER : GROUPED + HELD]), first_piece, early_contact, free_part)
+            halve_y(rest[:, :waits], ys[0][:, cut:] if cut < BANK else ys[1][:, :HELD])
+            put_back(j, cut, S, rest)
+            store(j)
+            if j + 3 < TILES:
+                cast_whole(j + 3, stage[:, :GROUPED])
+                quantise_contact(j + 3, stage[:, :GROUPED])
+                if j in (1, 3):
+                    i = 6 if j == 1 else 7
+                    half_state[i] = held.tile([P, S], F32, name="contact_raw%d" % (j + 3), align_bytes=64)[:]
+                    pick_state(i, 0, S, plain_halves)
+        ys = second_product(TILES - 1)
+        both = freed[2][:, S:]
+        for u in range(S // BANK):
+            halve_y(both[:, u * BANK : (u + 1) * BANK], ys[u][:])
+        put_back(TILES - 1, 0, S, both)
+        store(TILES - 1)

@@ -125,10 +125,10 @@ def tile_list_vowel_shift_kernel(tc, tab_words, tab_scales, offs, gT, contact, b
         load_state(5)
         load_contact(3)
         load_contact(4)
-        load_state(6)
         load_contact(5)
-        load_state(7)
+        load_state(6)
         load_contact(6)
+        load_state(7)
         load_contact(7)
 
         picked_words = [held.tile([P, S], U32, name="picked_words%d" % a, align_bytes=64) for a in range(K_PASSES)]
@@ -143,6 +143,7 @@ def tile_list_vowel_shift_kernel(tc, tab_words, tab_scales, offs, gT, contact, b
         contact_mx = {}
         h_mx = {}
         half_state = {}
+        cast_homes = {}
 
         def cast_pass(i, home, a):
             nc.scalar.copy(
@@ -156,10 +157,11 @@ def tile_list_vowel_shift_kernel(tc, tab_words, tab_scales, offs, gT, contact, b
                 homes[i][:].rearrange("p (a t c i) -> p a c t i", a=K_PASSES, t=PACK, i=4),
             )
 
-        def quantise_contact(i, home, steps=((0, K_PASSES),)):
+        def quantise_contact(i, home, steps=((0, K_PASSES),), codes=None):
             grouped = home.bitcast(BF16)
-            codes = ring.tile([P, K_PASSES * P], U32, name="contact_codes", bufs=3, align_bytes=64)
-            scales = ring.tile([P, K_PASSES * P], U8, name="contact_scales", bufs=3, align_bytes=64)
+            if codes is None:
+                codes = ring.tile([P, K_PASSES * P], U32, name="contact_codes", bufs=3, align_bytes=64)[:]
+            scales = ring.tile([P, K_PASSES * P], U8, name="contact_scales", bufs=4, align_bytes=64)
             for a0, a1 in steps:
                 nc.vector.quantize_mx(
                     codes[:, a0 * P : a1 * P].bitcast(FP8X4), scales[:, a0 * P : a1 * P], grouped[:, a0 * PASS : a1 * PASS]
@@ -352,6 +354,8 @@ def tile_list_vowel_shift_kernel(tc, tab_words, tab_scales, offs, gT, contact, b
             if j == 1:
                 early_home = held.tile([P, GROUPED], F32, name="first_home", align_bytes=64)
                 pairs0 = early_home[:, :QUARTER]
+            if j in (2, 3, 4):
+                pairs0 = held.tile([P, QUARTER], F32, name="pairs%d" % j, align_bytes=64)[:]
 
             def first_piece():
                 half_y = ring.tile([P, BANK], F32, name="first_half_y")
@@ -362,6 +366,13 @@ def tile_list_vowel_shift_kernel(tc, tab_words, tab_scales, offs, gT, contact, b
                 if j == 1:
                     cast_whole(3, early_home[:])
                     quantise_contact(3, early_home[:])
+                if j == 2:
+                    codes = held.tile([P, 2, K_PASSES * P], U32, name="pairs2", align_bytes=64)
+                    quantise_contact(4, cast_homes[4], codes=codes[:, 0, :])
+                    quantise_contact(5, cast_homes[5], codes=codes[:, 1, :])
+                if j in (3, 4):
+                    codes = held.tile([P, K_PASSES * P], U32, name="pairs%d" % j, align_bytes=64)
+                    quantise_contact(j + 3, cast_homes[j + 3], codes=codes[:])
 
             def free_part():
                 halve_y(rest[:, waits:], ys[1][:, waits - (BANK - cut) :])
@@ -370,13 +381,20 @@ def tile_list_vowel_shift_kernel(tc, tab_words, tab_scales, offs, gT, contact, b
             halve_y(rest[:, :waits], ys[0][:, cut:] if cut < BANK else ys[1][:, :HELD])
             put_back(j, cut, S, rest)
             store(j)
-            if j + 3 < TILES:
-                cast_whole(j + 3, stage[:, :GROUPED])
-                quantise_contact(j + 3, stage[:, :GROUPED])
-                if j in (1, 3):
-                    i = 6 if j == 1 else 7
-                    half_state[i] = held.tile([P, S], F32, name="contact_raw%d" % (j + 3), align_bytes=64)[:]
-                    pick_state(i, 0, S, plain_halves)
+            if j == 1:
+                cast_homes[4] = stage[:, :GROUPED]
+                cast_whole(4, cast_homes[4])
+                shared = held.tile([P, S + GROUPED], F32, name="contact_raw4", align_bytes=64)
+                half_state[6] = shared[:, :S]
+                cast_homes[5] = shared[:, S:]
+                pick_state(6, 0, S, plain_halves)
+                cast_whole(5, cast_homes[5])
+            if j in (2, 3):
+                cast_homes[j + 4] = stage[:, :GROUPED]
+                cast_whole(j + 4, cast_homes[j + 4])
+            if j == 2:
+                half_state[7] = held.tile([P, S], F32, name="contact_raw6", align_bytes=64)[:]
+                pick_state(7, 0, S, plain_halves)
         ys = second_product(TILES - 1)
         both = freed[2][:, S:]
         for u in range(S // BANK):

@@ -29,7 +29,7 @@ GROUPED = K_PASSES * PASS // 2
 QUARTER = PASS // 2
 LEAD = 128
 RESTORED = 16
-FIRST_PIECE = 384
+FIRST_PIECE = 256
 HELD = 64
 LAST_CUT = 384
 
@@ -55,8 +55,8 @@ def tile_list_vowel_shift_kernel(tc, tab_words, tab_scales, offs, gT, contact, b
 
         identity = held.tile([P, P], F32, name="identity")
         make_identity(nc, identity[:])
-        nc.scalar.dma_start(vectors[0:CHUNKS, :], bias.rearrange("(c m) -> c m", c=CHUNKS))
-        nc.scalar.dma_start(vectors[CHUNKS : 2 * CHUNKS, :], gain.rearrange("(c m) -> c m", c=CHUNKS))
+        nc.gpsimd.dma_start(vectors[0:CHUNKS, :], bias.rearrange("(c m) -> c m", c=CHUNKS))
+        nc.gpsimd.dma_start(vectors[CHUNKS : 2 * CHUNKS, :], gain.rearrange("(c m) -> c m", c=CHUNKS))
         identity_bf16 = held.tile([P, P], BF16, name="identity_bf16")
         nc.scalar.copy(identity_bf16[:], identity[:])
         turned = psum.tile([P, P], F32, name="y1")
@@ -77,8 +77,8 @@ def tile_list_vowel_shift_kernel(tc, tab_words, tab_scales, offs, gT, contact, b
 
         def load_contact(i):
             if i == 1:
-                homes["first_y"] = held.tile([P, BANK + K_PASSES * PASS], F32, name="first_y", align_bytes=64)
-                raw = [homes["first_y"][:, BANK + (K_PASSES - 1 - a) * PASS : BANK + (K_PASSES - a) * PASS] for a in range(K_PASSES)]
+                homes["first_y"] = held.tile([P, S - HELD + K_PASSES * PASS], F32, name="first_y", align_bytes=64)
+                raw = [homes["first_y"][:, S - HELD + (K_PASSES - 1 - a) * PASS : S - HELD + (K_PASSES - a) * PASS] for a in range(K_PASSES)]
             else:
                 whole = held.tile([P, K_PASSES * PASS], F32, name="contact_raw%d" % i, align_bytes=64)
                 homes[i] = whole
@@ -86,6 +86,10 @@ def tile_list_vowel_shift_kernel(tc, tab_words, tab_scales, offs, gT, contact, b
             for a in range(K_PASSES):
                 rows = contact[a * PASS : (a + 1) * PASS, i * P : (i + 1) * P]
                 nc.sync.dma_start(raw[a].rearrange("p (j n) -> p j n", j=PACK), rows.rearrange("(p j) n -> p j n", j=PACK))
+                if i == 0 and a == 1:
+                    load_table(2)
+                if i == 1 and a == 0:
+                    load_wr(1)
             contact_raw[i] = raw
 
         def load_state(i):
@@ -107,7 +111,6 @@ def tile_list_vowel_shift_kernel(tc, tab_words, tab_scales, offs, gT, contact, b
                 tab_scales[:, 4 * q : 4 * q + 4, :].bitcast(I32),
             )
         load_contact(0)
-        load_table(2)
         load_state(0)
         load_state(1)
         load_state(2)
@@ -117,7 +120,6 @@ def tile_list_vowel_shift_kernel(tc, tab_words, tab_scales, offs, gT, contact, b
                 wr_scales[:, 4 * q : 4 * q + 4, :].rearrange("a r c -> r a c").bitcast(I32),
             )
         load_wr(0)
-        load_wr(1)
         load_contact(1)
         load_contact(2)
         load_state(3)
@@ -131,14 +133,23 @@ def tile_list_vowel_shift_kernel(tc, tab_words, tab_scales, offs, gT, contact, b
         load_state(7)
         load_contact(7)
 
-        picked_words = [held.tile([P, S], U32, name="picked_words%d" % a, align_bytes=64) for a in range(K_PASSES)]
-        picked_scales = held.tile([P, S], U8, name="picked_scales", align_bytes=64)
+        picked_words = {}
+        picked_scales = {}
+        for a in range(K_PASSES - 1):
+            whole = held.tile([P, S], U32, name="picked_words%d" % a, align_bytes=64)
+            picked_words[a] = whole
+            for b in range(M_PASSES):
+                picked_words[a, b] = whole[:, b * PASS : (b + 1) * PASS]
 
         def listed(c0, c1):
             return offsets[:, c0 // 16 : c1 // 16]
 
-        def pick_words(a, c0, c1):
-            nc.vector.tensor_copy(picked_words[a][:, c0:c1], table_words[a][:].indirect(listed(c0, c1)))
+        def pick_words(a, home, c0, c1):
+            nc.vector.tensor_copy(home, table_words[a][:].indirect(listed(c0, c1)))
+
+        def pick_scales(b, name):
+            picked_scales[b] = held.tile([P, PASS], U8, name=name, align_bytes=64)[:]
+            nc.vector.tensor_copy(picked_scales[b], table_scales[:].indirect(listed(b * PASS, (b + 1) * PASS)))
 
         contact_mx = {}
         h_mx = {}
@@ -157,24 +168,26 @@ def tile_list_vowel_shift_kernel(tc, tab_words, tab_scales, offs, gT, contact, b
                 homes[i][:].rearrange("p (a t c i) -> p a c t i", a=K_PASSES, t=PACK, i=4),
             )
 
-        def quantise_contact(i, home, steps=((0, K_PASSES),), codes=None):
-            grouped = home.bitcast(BF16)
+        def quantise_passes(i, home, a0, a1):
+            codes, scales = contact_mx[i]
+            nc.vector.quantize_mx(
+                codes[:, a0 * P : a1 * P].bitcast(FP8X4), scales[:, a0 * P : a1 * P], home.bitcast(BF16)[:, a0 * PASS : a1 * PASS]
+            )
+
+        def quantise_contact(i, home, codes=None):
             if codes is None:
                 codes = ring.tile([P, K_PASSES * P], U32, name="contact_codes", bufs=3, align_bytes=64)[:]
             scales = ring.tile([P, K_PASSES * P], U8, name="contact_scales", bufs=4, align_bytes=64)
-            for a0, a1 in steps:
-                nc.vector.quantize_mx(
-                    codes[:, a0 * P : a1 * P].bitcast(FP8X4), scales[:, a0 * P : a1 * P], grouped[:, a0 * PASS : a1 * PASS]
-                )
             contact_mx[i] = (codes, scales)
+            quantise_passes(i, home, 0, K_PASSES)
 
         def first_pass(i, e, a, b, t, start, stop):
             codes, scales = contact_mx[i]
-            cols = slice(b * PASS + t * P, b * PASS + (t + 1) * P)
+            cols = slice(t * P, (t + 1) * P)
             nc.tensor.matmul_mx(
                 e,
-                lhsT=picked_words[a][:, cols].bitcast(FP8X4),
-                lhsT_scale=picked_scales[4 * a : P, cols],
+                lhsT=picked_words[a, b][:, cols].bitcast(FP8X4),
+                lhsT_scale=picked_scales[b][4 * a : P, cols],
                 rhs=codes[:, a * P : (a + 1) * P].bitcast(FP8X4),
                 rhs_scale=scales[:, a * P : (a + 1) * P],
                 start=start,
@@ -247,7 +260,7 @@ def tile_list_vowel_shift_kernel(tc, tab_words, tab_scales, offs, gT, contact, b
             late()
             lay_out(back1, 1, grouped)
             if i == 0:
-                h_codes = held.tile([P, M_PASSES * P], U32, name="second_home", align_bytes=64)
+                h_codes = held.tile([P, M_PASSES * P], U32, name="first_h_codes", align_bytes=64)
                 h_scales = lead_halves[:, : M_PASSES * P // 4].bitcast(U8)
             else:
                 h_codes = ring.tile([P, M_PASSES * P], U32, name="h_codes", align_bytes=64)
@@ -258,21 +271,24 @@ def tile_list_vowel_shift_kernel(tc, tab_words, tab_scales, offs, gT, contact, b
         def pick_state(i, c0, c1, factor):
             nc.vector.tensor_tensor(half_state[i][:, c0:c1], state[i][:].indirect(listed(c0, c1)), factor, ALU.mult)
 
-        def second_product(i):
+        def second_columns(i, c0, c1, bank):
             h_codes, h_scales = h_mx[i]
-            ys = [psum.tile([P, BANK], F32, name="y%d" % u) for u in range(S // BANK)]
-            for u in range(S // BANK):
-                for b in range(M_PASSES):
-                    nc.tensor.matmul_mx(
-                        ys[u][:],
-                        lhsT=h_codes[:, b * P : (b + 1) * P].bitcast(FP8X4),
-                        lhsT_scale=h_scales[:, b * P : (b + 1) * P],
-                        rhs=wr_codes[u][:, b, :].bitcast(FP4X4),
-                        rhs_scale=wr_planes[:, b, u * BANK : (u + 1) * BANK],
-                        start=(b == 0),
-                        stop=(b == M_PASSES - 1),
-                    )
-            return ys
+            y = psum.tile([P, c1 - c0], F32, name=bank)
+            u, first = divmod(c0, BANK)
+            for b in range(M_PASSES):
+                nc.tensor.matmul_mx(
+                    y[:],
+                    lhsT=h_codes[:, b * P : (b + 1) * P].bitcast(FP8X4),
+                    lhsT_scale=h_scales[:, b * P : (b + 1) * P],
+                    rhs=wr_codes[u][:, b, 2 * first : 2 * (first + c1 - c0)].bitcast(FP4X4),
+                    rhs_scale=wr_planes[:, b, c0:c1],
+                    start=(b == 0),
+                    stop=(b == M_PASSES - 1),
+                )
+            return y
+
+        def second_product(i):
+            return [second_columns(i, u * BANK, (u + 1) * BANK, "y%d" % u) for u in range(S // BANK)]
 
         def halve_y(home, y):
             nc.scalar.activation(home, y, ACT.Copy, scale=0.5)
@@ -291,22 +307,29 @@ def tile_list_vowel_shift_kernel(tc, tab_words, tab_scales, offs, gT, contact, b
 
         plain_halves = halves[:, QUARTER : QUARTER + S]
 
-        pick_words(0, 0, S)
-        pick_words(1, 0, S)
-        nc.vector.tensor_copy(picked_scales[:], table_scales[:].indirect(offsets[:]))
+        pick_words(0, picked_words[0][:], 0, S)
+        pick_words(1, picked_words[1][:], 0, S)
+        pick_scales(0, "picked_scales")
         first_home = held.tile([P, GROUPED], F32, name="first_home", align_bytes=64)
         for a in range(K_PASSES):
             cast_pass(0, first_home[:], a)
-        quantise_contact(0, first_home[:], ((0, 2), (2, 3)))
+        last = K_PASSES - 1
+        picked_words[last, 0] = held.tile([P, PASS], U32, name="picked_words2", align_bytes=64)[:]
+        codes = ring.tile([P, K_PASSES * P], U32, name="contact_codes", bufs=3, align_bytes=64)
+        scales = ring.tile([P, K_PASSES * P], U8, name="contact_scales", bufs=4, align_bytes=64)
+        contact_mx[0] = (codes[:], scales)
+        quantise_passes(0, first_home[:], 0, last)
+        for c0 in range(0, PASS, QUARTER):
+            pick_words(last, picked_words[last, 0][:, c0 : c0 + QUARTER], c0, c0 + QUARTER)
+        quantise_passes(0, first_home[:], last, K_PASSES)
+        pick_scales(1, "contact_raw0")
+        picked_words[last, 1] = held.tile([P, PASS], U32, name="first_home", align_bytes=64)[:]
+        pick_words(last, picked_words[last, 1], PASS, S)
         sums = new_sums(0)
         for b in range(M_PASSES):
-            for a in range(K_PASSES - 1):
+            for a in range(K_PASSES):
                 for t in range(PACK):
-                    first_pass(0, sums[b][t], a, b, t, a == 0 and t % 2 == 0, False)
-        for c in range(0, CHUNKS, 2):
-            pick_words(2, c * P, (c + 2) * P)
-            for t in (c % PACK, c % PACK + 1):
-                first_pass(0, sums[c // PACK][t], K_PASSES - 1, c // PACK, t, False, t % 2 == 1)
+                    first_pass(0, sums[b][t], a, b, t, a == 0 and t % 2 == 0, a == last and t % 2 == 1)
         freed = [held.tile([P, T], F32, name="table_words%d" % a, align_bytes=64) for a in range(K_PASSES)]
         half_state[0] = freed[0][:, :S]
         half_state[1] = freed[1][:, :S]
@@ -320,16 +343,19 @@ def tile_list_vowel_shift_kernel(tc, tab_words, tab_scales, offs, gT, contact, b
         make_h(0, sums, (stage[:, :QUARTER], stage[:, QUARTER:PASS]), (stage[:, PASS : PASS + QUARTER], halves[:, :QUARTER]), nothing, nothing, nothing)
         nc.scalar.copy(halves[:, QUARTER - RESTORED : QUARTER], plain_halves[:, :RESTORED])
         pick_state(2, 0, S, halves[:, QUARTER - RESTORED : QUARTER - RESTORED + S])
-        ys = second_product(0)
+        cuts = (0, FIRST_PIECE, BANK, S)
+        ys = [second_columns(0, cuts[k], cuts[k + 1], bank) for k, bank in enumerate(("spare0", "y0", "y1"))]
         both = homes["first_y"]
-        halve_y(both[:, :BANK], ys[0][:])
+        halve_y(both[:, :FIRST_PIECE], ys[0][:])
         put_back(0, 0, FIRST_PIECE, both[:, :FIRST_PIECE])
         home = held.tile([P, GROUPED], F32, name="second_home", align_bytes=64)
         for a in range(K_PASSES):
             cast_pass(1, home[:], a)
         quantise_contact(1, home[:])
         sums = first_product(1)
-        halve_y(both[:, BANK:S], ys[1][:])
+        halve_y(both[:, FIRST_PIECE:BANK], ys[1][:])
+        halve_y(both[:, BANK : S - HELD], ys[2][:, : BANK - HELD])
+        halve_y(both[:, S - HELD : S], ys[2][:, BANK - HELD :])
         put_back(0, FIRST_PIECE, S, both[:, FIRST_PIECE:S])
         store(0)
         for a in range(K_PASSES):
@@ -352,7 +378,7 @@ def tile_list_vowel_shift_kernel(tc, tab_words, tab_scales, offs, gT, contact, b
             rest = stage[:, GROUPED : GROUPED + S - cut]
             pairs0 = stage[:, GROUPED + P : GROUPED + P + QUARTER]
             if j == 1:
-                early_home = held.tile([P, GROUPED], F32, name="first_home", align_bytes=64)
+                early_home = held.tile([P, GROUPED], F32, name="second_home", align_bytes=64)
                 pairs0 = early_home[:, :QUARTER]
             if j in (2, 3, 4):
                 pairs0 = held.tile([P, QUARTER], F32, name="pairs%d" % j, align_bytes=64)[:]
@@ -366,11 +392,7 @@ def tile_list_vowel_shift_kernel(tc, tab_words, tab_scales, offs, gT, contact, b
                 if j == 1:
                     cast_whole(3, early_home[:])
                     quantise_contact(3, early_home[:])
-                if j == 2:
-                    codes = held.tile([P, 2, K_PASSES * P], U32, name="pairs2", align_bytes=64)
-                    quantise_contact(4, cast_homes[4], codes=codes[:, 0, :])
-                    quantise_contact(5, cast_homes[5], codes=codes[:, 1, :])
-                if j in (3, 4):
+                if j in (2, 3, 4):
                     codes = held.tile([P, K_PASSES * P], U32, name="pairs%d" % j, align_bytes=64)
                     quantise_contact(j + 3, cast_homes[j + 3], codes=codes[:])
 
@@ -382,8 +404,8 @@ def tile_list_vowel_shift_kernel(tc, tab_words, tab_scales, offs, gT, contact, b
             put_back(j, cut, S, rest)
             store(j)
             if j == 1:
-                cast_homes[4] = stage[:, :GROUPED]
-                cast_whole(4, cast_homes[4])
+                cast_whole(4, stage[:, :GROUPED])
+                quantise_contact(4, stage[:, :GROUPED])
                 shared = held.tile([P, S + GROUPED], F32, name="contact_raw4", align_bytes=64)
                 half_state[6] = shared[:, :S]
                 cast_homes[5] = shared[:, S:]

@@ -31,7 +31,7 @@ LEAD = 128
 RESTORED = 16
 FIRST_PIECE = 256
 HELD = 64
-LAST_CUT = 384
+CUTS = (320, 512, 192, 256, 288, 320)
 
 
 def tile_list_vowel_shift_kernel(tc, tab_words, tab_scales, offs, gT, contact, bias, gain, wr_words, wr_scales, out):
@@ -88,8 +88,8 @@ def tile_list_vowel_shift_kernel(tc, tab_words, tab_scales, offs, gT, contact, b
                 nc.sync.dma_start(raw[a].rearrange("p (j n) -> p j n", j=PACK), rows.rearrange("(p j) n -> p j n", j=PACK))
                 if i == 0 and a == 1:
                     load_table(2)
-                if i == 1 and a == 0:
-                    load_wr(1)
+                if i == 1 and a < S // BANK:
+                    load_wr(a)
             contact_raw[i] = raw
 
         def load_state(i):
@@ -113,13 +113,12 @@ def tile_list_vowel_shift_kernel(tc, tab_words, tab_scales, offs, gT, contact, b
         load_contact(0)
         load_state(0)
         load_state(1)
-        load_state(2)
         for q in range(4):
             nc.sync.dma_start(
                 wr_planes[32 * q : 32 * q + 4].bitcast(I32),
                 wr_scales[:, 4 * q : 4 * q + 4, :].rearrange("a r c -> r a c").bitcast(I32),
             )
-        load_wr(0)
+        load_state(2)
         load_contact(1)
         load_contact(2)
         load_state(3)
@@ -155,6 +154,7 @@ def tile_list_vowel_shift_kernel(tc, tab_words, tab_scales, offs, gT, contact, b
         h_mx = {}
         half_state = {}
         cast_homes = {}
+        behind_cast = {}
 
         def cast_pass(i, home, a):
             nc.scalar.copy(
@@ -214,8 +214,11 @@ def tile_list_vowel_shift_kernel(tc, tab_words, tab_scales, offs, gT, contact, b
                         first_pass(i, sums[b][t], a, b, t, a == 0, a == K_PASSES - 1)
             return sums
 
-        def saturate(e, b):
-            saturated = ring.tile([P, PACK, P], F32, name="saturated")
+        def saturate(e, b, home=None):
+            if home is None:
+                saturated = ring.tile([P, PACK, P], F32, name="saturated")
+            else:
+                saturated = home.rearrange("p (t n) -> p t n", t=PACK)
             for t in range(PACK):
                 c = PACK * b + t
                 nc.scalar.activation(saturated[:, t, :], e[t], ACT.Tanh, bias=columns[:, c : c + 1])
@@ -249,7 +252,7 @@ def tile_list_vowel_shift_kernel(tc, tab_words, tab_scales, offs, gT, contact, b
 
         def make_h(i, sums, scaled, pairs, early, middle, late, order=(0, 1)):
             grouped = ring.tile([P, S], BF16, name="h_grouped", align_bytes=64)
-            rows0 = amplify(saturate(sums[0], 0), 0, scaled[0], "fixed")
+            rows0 = amplify(saturate(sums[0], 0, behind_cast.get(i)), 0, scaled[0], "fixed")
             saturated1 = saturate(sums[1], 1)
             early()
             back0 = turn_back(rows0, pairs[0], "fixed")
@@ -300,7 +303,7 @@ def tile_list_vowel_shift_kernel(tc, tab_words, tab_scales, offs, gT, contact, b
             nc.sync.dma_start(out[i * P : (i + 1) * P, :], state[i][:])
 
         def new_stage():
-            return ring.tile([P, GROUPED + S - LAST_CUT], F32, name="stage", bufs=3, align_bytes=64)
+            return ring.tile([P, S + GROUPED], F32, name="stage", bufs=3, align_bytes=64)
 
         def nothing():
             return None
@@ -319,12 +322,12 @@ def tile_list_vowel_shift_kernel(tc, tab_words, tab_scales, offs, gT, contact, b
         scales = ring.tile([P, K_PASSES * P], U8, name="contact_scales", bufs=4, align_bytes=64)
         contact_mx[0] = (codes[:], scales)
         quantise_passes(0, first_home[:], 0, last)
-        for c0 in range(0, PASS, QUARTER):
-            pick_words(last, picked_words[last, 0][:, c0 : c0 + QUARTER], c0, c0 + QUARTER)
+        pick_words(last, picked_words[last, 0], 0, PASS)
         quantise_passes(0, first_home[:], last, K_PASSES)
         pick_scales(1, "contact_raw0")
         picked_words[last, 1] = held.tile([P, PASS], U32, name="first_home", align_bytes=64)[:]
-        pick_words(last, picked_words[last, 1], PASS, S)
+        for c0 in range(0, PASS, QUARTER):
+            pick_words(last, picked_words[last, 1][:, c0 : c0 + QUARTER], PASS + c0, PASS + c0 + QUARTER)
         sums = new_sums(0)
         for b in range(M_PASSES):
             for a in range(K_PASSES):
@@ -373,49 +376,50 @@ def tile_list_vowel_shift_kernel(tc, tab_words, tab_scales, offs, gT, contact, b
             sums = first_product(j + 1)
             ys = second_product(j)
             stage = new_stage()
-            cut = LAST_CUT if j == TILES - 2 else BANK
-            waits = BANK - cut if cut < BANK else HELD
-            rest = stage[:, GROUPED : GROUPED + S - cut]
-            pairs0 = stage[:, GROUPED + P : GROUPED + P + QUARTER]
+            half_y = stage[:, :S]
+            cast_home = stage[:, S:]
+            cut = CUTS[j - 1]
             if j == 1:
                 early_home = held.tile([P, GROUPED], F32, name="second_home", align_bytes=64)
                 pairs0 = early_home[:, :QUARTER]
-            if j in (2, 3, 4):
+            else:
                 pairs0 = held.tile([P, QUARTER], F32, name="pairs%d" % j, align_bytes=64)[:]
 
             def first_piece():
-                half_y = ring.tile([P, BANK], F32, name="first_half_y")
-                halve_y(half_y[:, :cut], ys[0][:, :cut])
+                halve_y(half_y[:, :BANK], ys[0][:])
                 put_back(j, 0, cut, half_y[:, :cut])
 
-            def early_contact():
+            def next_contact():
                 if j == 1:
                     cast_whole(3, early_home[:])
                     quantise_contact(3, early_home[:])
-                if j in (2, 3, 4):
+                elif j + 3 < TILES:
                     codes = held.tile([P, K_PASSES * P], U32, name="pairs%d" % j, align_bytes=64)
                     quantise_contact(j + 3, cast_homes[j + 3], codes=codes[:])
 
             def free_part():
-                halve_y(rest[:, waits:], ys[1][:, waits - (BANK - cut) :])
+                halve_y(half_y[:, BANK : S - HELD], ys[1][:, : BANK - HELD])
 
-            make_h(j + 1, sums, (stage[:, :QUARTER], stage[:, QUARTER:PASS]), (pairs0, stage[:, GROUPED + HELD - QUARTER : GROUPED + HELD]), first_piece, early_contact, free_part)
-            halve_y(rest[:, :waits], ys[0][:, cut:] if cut < BANK else ys[1][:, :HELD])
-            put_back(j, cut, S, rest)
+            make_h(j + 1, sums, (cast_home[:, QUARTER:PASS], cast_home[:, PASS:]), (pairs0, stage[:, S - HELD : S - HELD + QUARTER]), first_piece, next_contact, free_part, (1, 0))
+            halve_y(half_y[:, S - HELD :], ys[1][:, BANK - HELD :])
+            put_back(j, cut, S, half_y[:, cut:])
             store(j)
             if j == 1:
-                cast_whole(4, stage[:, :GROUPED])
-                quantise_contact(4, stage[:, :GROUPED])
+                cast_whole(4, cast_home)
+                quantise_contact(4, cast_home)
                 shared = held.tile([P, S + GROUPED], F32, name="contact_raw4", align_bytes=64)
                 half_state[6] = shared[:, :S]
                 cast_homes[5] = shared[:, S:]
                 pick_state(6, 0, S, plain_halves)
                 cast_whole(5, cast_homes[5])
             if j in (2, 3):
-                cast_homes[j + 4] = stage[:, :GROUPED]
-                cast_whole(j + 4, cast_homes[j + 4])
+                cast_homes[j + 4] = cast_home
+                cast_whole(j + 4, cast_home)
+            if j + 4 < TILES:
+                shared = held.tile([P, S + PASS], F32, name="contact_raw%d" % (j + 4), align_bytes=64)
+                behind_cast[j + 2] = shared[:, S:]
             if j == 2:
-                half_state[7] = held.tile([P, S], F32, name="contact_raw6", align_bytes=64)[:]
+                half_state[7] = shared[:, :S]
                 pick_state(7, 0, S, plain_halves)
         ys = second_product(TILES - 1)
         both = freed[2][:, S:]

from contextlib import ExitStack

import concourse.mybir as mybir
from concourse.masks import make_identity

K, T, S, N = 1536, 2048, 1024, 1024
FLOPS = 2 * K * S * N + 2 * S * S * N

F32 = mybir.dt.float32
BF16 = mybir.dt.bfloat16
I32 = mybir.dt.int32
U32 = mybir.dt.uint32
U16 = mybir.dt.uint16
U8 = mybir.dt.uint8
FP8X4 = mybir.dt.float8_e4m3fn_x4
FP4X4 = mybir.dt.float4_e2m1fn_x4
ACT = mybir.ActivationFunctionType
ALU = mybir.AluOpType

P = 128
PACK = 4
PASS = P * PACK
K_PASSES = K // PASS
M_PASSES = S // PASS
TILES = N // P
CHUNKS = S // P
BANK = 512
GROUPED = K_PASSES * PASS // 2
QUARTER = PASS // 2
LEAD = 128
RESTORED = 16
FIRST_PIECE = 256
HELD = 64
CUTS = (320, 512, 192, 256, 288, 320)


def tile_list_vowel_shift_kernel(tc, tab_words, tab_scales, offs, gT, contact, bias, gain, wr_words, wr_scales, out):
    nc = tc.nc
    with ExitStack() as ctx:
        held = ctx.enter_context(tc.tile_pool(name="held", bufs=1))
        ring = ctx.enter_context(tc.tile_pool(name="ring", bufs=2))
        psum = ctx.enter_context(tc.psum_pool(name="psum", bufs=1))

        offsets = held.tile([P, S // 16], U16, name="offsets")
        table_scales = held.tile([P, T], U8, name="table_scales", align_bytes=64)
        wr_planes = held.tile([P, M_PASSES, S], U8, name="wr_planes", align_bytes=64)
        halves = held.tile([P, QUARTER + S + QUARTER], F32, name="halves", align_bytes=64)
        lead_halves = held.tile([P, LEAD], F32, name="lead_halves", align_bytes=64)
        vectors = held.tile([P, P], F32, name="vectors")
        nc.vector.memset(vectors[:], 0.0)
        nc.vector.memset(table_scales[:].bitcast(I32), 0)
        nc.vector.memset(wr_planes[:].rearrange("p a c -> p (a c)").bitcast(I32), 0)
        nc.vector.memset(halves[:, QUARTER : QUARTER + S], 0.5)
        nc.vector.memset(lead_halves[:], 0.5)

        identity = held.tile([P, P], F32, name="identity")
        make_identity(nc, identity[:])
        nc.gpsimd.dma_start(vectors[0:CHUNKS, :], bias.rearrange("(c m) -> c m", c=CHUNKS))
        nc.gpsimd.dma_start(vectors[CHUNKS : 2 * CHUNKS, :], gain.rearrange("(c m) -> c m", c=CHUNKS))
        identity_bf16 = held.tile([P, P], BF16, name="identity_bf16")
        nc.scalar.copy(identity_bf16[:], identity[:])
        turned = psum.tile([P, P], F32, name="y1")
        nc.tensor.transpose(turned[:], vectors[:], identity[:])
        columns = held.tile([P, 2 * CHUNKS], F32, name="columns")
        nc.scalar.copy(columns[:], turned[:, : 2 * CHUNKS])

        table_words = []
        contact_raw = {}
        state = {}
        homes = {}
        wr_codes = []

        def load_table(a):
            words = held.tile([P, T], U32, name="table_words%d" % a, align_bytes=64)
            nc.sync.dma_start(words[:].bitcast(I32), tab_words[a].rearrange("p n t -> p (n t)").bitcast(I32))
            table_words.append(words)

        def load_contact(i):
            if i == 1:
                homes["first_y"] = held.tile([P, S - HELD + K_PASSES * PASS], F32, name="first_y", align_bytes=64)
                raw = [homes["first_y"][:, S - HELD + (K_PASSES - 1 - a) * PASS : S - HELD + (K_PASSES - a) * PASS] for a in range(K_PASSES)]
            else:
                whole = held.tile([P, K_PASSES * PASS], F32, name="contact_raw%d" % i, align_bytes=64)
                homes[i] = whole
                raw = [whole[:, a * PASS : (a + 1) * PASS] for a in range(K_PASSES)]
            for a in range(K_PASSES):
                rows = contact[a * PASS : (a + 1) * PASS, i * P : (i + 1) * P]
                nc.sync.dma_start(raw[a].rearrange("p (j n) -> p j n", j=PACK), rows.rearrange("(p j) n -> p j n", j=PACK))
                if i == 0 and a == 1:
                    load_table(2)
                if i == 1 and a < S // BANK:
                    load_wr(a)
            contact_raw[i] = raw

        def load_state(i):
            rows = held.tile([P, T], F32, name="state%d" % i)
            nc.sync.dma_start(rows[:], gT[i * P : (i + 1) * P, :])
            state[i] = rows

        def load_wr(u):
            codes = held.tile([P, M_PASSES, 2 * BANK], U8, name="wr_codes%d" % u, align_bytes=64)
            nc.sync.dma_start(codes[:].bitcast(I32), wr_words[:, :, 2 * u * BANK : 2 * (u + 1) * BANK].rearrange("a p c -> p a c").bitcast(I32))
            wr_codes.append(codes)

        load_table(0)
        nc.sync.dma_start(offsets[:], offs)
        load_table(1)
        for q in range(4):
            nc.sync.dma_start(
                table_scales[32 * q : 32 * q + 4 * K_PASSES, :].bitcast(I32),
                tab_scales[:, 4 * q : 4 * q + 4, :].bitcast(I32),
            )
        load_contact(0)
        load_state(0)
        load_state(1)
        for q in range(4):
            nc.sync.dma_start(
                wr_planes[32 * q : 32 * q + 4].bitcast(I32),
                wr_scales[:, 4 * q : 4 * q + 4, :].rearrange("a r c -> r a c").bitcast(I32),
            )
        load_state(2)
        load_contact(1)
        load_contact(2)
        load_state(3)
        load_state(4)
        load_state(5)
        load_contact(3)
        load_contact(4)
        load_contact(5)
        load_state(6)
        load_contact(6)
        load_state(7)
        load_contact(7)

        picked_words = {}
        picked_scales = {}
        for a in range(K_PASSES - 1):
            whole = held.tile([P, S], U32, name="picked_words%d" % a, align_bytes=64)
            picked_words[a] = whole
            for b in range(M_PASSES):
                picked_words[a, b] = whole[:, b * PASS : (b + 1) * PASS]

        def listed(c0, c1):
            return offsets[:, c0 // 16 : c1 // 16]

        def pick_words(a, home, c0, c1):
            nc.vector.tensor_copy(home, table_words[a][:].indirect(listed(c0, c1)))

        def pick_scales(b, name):
            picked_scales[b] = held.tile([P, PASS], U8, name=name, align_bytes=64)[:]
            nc.vector.tensor_copy(picked_scales[b], table_scales[:].indirect(listed(b * PASS, (b + 1) * PASS)))

        contact_mx = {}
        h_mx = {}
        half_state = {}
        cast_homes = {}
        behind_cast = {}

        def cast_pass(i, home, a):
            nc.scalar.copy(
                home.bitcast(BF16)[:, a * PASS : (a + 1) * PASS].rearrange("p (c i t) -> p c t i", i=4, t=PACK),
                contact_raw[i][a].rearrange("p (t c i) -> p c t i", t=PACK, i=4),
            )

        def cast_whole(i, home):
            nc.scalar.copy(
                home.bitcast(BF16).rearrange("p (a c i t) -> p a c t i", a=K_PASSES, i=4, t=PACK),
                homes[i][:].rearrange("p (a t c i) -> p a c t i", a=K_PASSES, t=PACK, i=4),
            )

        def quantise_passes(i, home, a0, a1):
            codes, scales = contact_mx[i]
            nc.vector.quantize_mx(
                codes[:, a0 * P : a1 * P].bitcast(FP8X4), scales[:, a0 * P : a1 * P], home.bitcast(BF16)[:, a0 * PASS : a1 * PASS]
            )

        def quantise_contact(i, home, codes=None):
            if codes is None:
                codes = ring.tile([P, K_PASSES * P], U32, name="contact_codes", bufs=3, align_bytes=64)[:]
            scales = ring.tile([P, K_PASSES * P], U8, name="contact_scales", bufs=4, align_bytes=64)
            contact_mx[i] = (codes, scales)
            quantise_passes(i, home, 0, K_PASSES)

        def first_pass(i, e, a, b, t, start, stop):
            codes, scales = contact_mx[i]
            cols = slice(t * P, (t + 1) * P)
            nc.tensor.matmul_mx(
                e,
                lhsT=picked_words[a, b][:, cols].bitcast(FP8X4),
                lhsT_scale=picked_scales[b][4 * a : P, cols],
                rhs=codes[:, a * P : (a + 1) * P].bitcast(FP8X4),
                rhs_scale=scales[:, a * P : (a + 1) * P],
                start=start,
                stop=stop,
            )

        def turn_bank(i, k):
            return "turn%d" % ((k - i) % 3)

        def new_sums(i):
            banks = [turn_bank(i, 0), turn_bank(i, 1)]
            if i < 2:
                banks = [banks[0], "spare0", banks[1], "spare1"]
            per_bank = CHUNKS // len(banks)
            tiles = [psum.tile([P, per_bank, P], F32, name=bank) for bank in banks]
            chunks = [tiles[c // per_bank][:, c % per_bank, :] for c in range(CHUNKS)]
            return [chunks[:PACK], chunks[PACK:]]

        def first_product(i):
            sums = new_sums(i)
            for b in range(M_PASSES):
                for t in range(PACK):
                    for a in range(K_PASSES):
                        first_pass(i, sums[b][t], a, b, t, a == 0, a == K_PASSES - 1)
            return sums

        def saturate(e, b, home=None):
            if home is None:
                saturated = ring.tile([P, PACK, P], F32, name="saturated")
            else:
                saturated = home.rearrange("p (t n) -> p t n", t=PACK)
            for t in range(PACK):
                c = PACK * b + t
                nc.scalar.activation(saturated[:, t, :], e[t], ACT.Tanh, bias=columns[:, c : c + 1])
            return saturated

        def amplify(saturated, b, scaled, bank):
            scaled = scaled.bitcast(BF16)
            rows = psum.tile([P, PASS], BF16, name=bank)
            for t in range(PACK):
                c = CHUNKS + PACK * b + t
                cols = slice(t * P, (t + 1) * P)
                nc.scalar.activation(scaled[:, cols], saturated[:, t, :], ACT.Copy, scale=columns[:, c : c + 1])
                nc.tensor.transpose(rows[:, cols], scaled[:, cols], identity_bf16[:])
            return rows

        def turn_back(rows, pairs, bank, order=(0, 1)):
            nc.scalar.copy(
                pairs.rearrange("p (u q) -> p u q", u=2),
                rows[:].bitcast(F32).rearrange("p (q u) -> p u q", u=2),
            )
            back = psum.tile([P, 2, P], F32, name=bank)
            for u in order:
                nc.tensor.transpose(back[:, u, :], pairs[:, u * P : (u + 1) * P], identity[:])
            return back

        def lay_out(back, b, grouped):
            nc.scalar.copy(
                grouped[:, b * PASS : (b + 1) * PASS].bitcast(F32).rearrange("p (n u) -> p n u", u=2),
                back[:].rearrange("p u n -> p n u"),
            )

        def make_h(i, sums, scaled, pairs, early, middle, late, order=(0, 1)):
            grouped = ring.tile([P, S], BF16, name="h_grouped", align_bytes=64)
            rows0 = amplify(saturate(sums[0], 0, behind_cast.get(i)), 0, scaled[0], "fixed")
            saturated1 = saturate(sums[1], 1)
            early()
            back0 = turn_back(rows0, pairs[0], "fixed")
            rows1 = amplify(saturated1, 1, scaled[1], turn_bank(i, 2))
            lay_out(back0, 0, grouped)
            middle()
            back1 = turn_back(rows1, pairs[1], turn_bank(i, 0), order)
            late()
            lay_out(back1, 1, grouped)
            if i == 0:
                h_codes = held.tile([P, M_PASSES * P], U32, name="first_h_codes", align_bytes=64)
                h_scales = lead_halves[:, : M_PASSES * P // 4].bitcast(U8)
            else:
                h_codes = ring.tile([P, M_PASSES * P], U32, name="h_codes", align_bytes=64)
                h_scales = ring.tile([P, M_PASSES * P], U8, name="h_scales", align_bytes=64)
            nc.vector.quantize_mx(h_codes[:].bitcast(FP8X4), h_scales[:], grouped[:])
            h_mx[i] = (h_codes, h_scales)

        def pick_state(i, c0, c1, factor):
            nc.vector.tensor_tensor(half_state[i][:, c0:c1], state[i][:].indirect(listed(c0, c1)), factor, ALU.mult)

        def second_columns(i, c0, c1, bank):
            h_codes, h_scales = h_mx[i]
            y = psum.tile([P, c1 - c0], F32, name=bank)
            u, first = divmod(c0, BANK)
            for b in range(M_PASSES):
                nc.tensor.matmul_mx(
                    y[:],
                    lhsT=h_codes[:, b * P : (b + 1) * P].bitcast(FP8X4),
                    lhsT_scale=h_scales[:, b * P : (b + 1) * P],
                    rhs=wr_codes[u][:, b, 2 * first : 2 * (first + c1 - c0)].bitcast(FP4X4),
                    rhs_scale=wr_planes[:, b, c0:c1],
                    start=(b == 0),
                    stop=(b == M_PASSES - 1),
                )
            return y

        def second_product(i):
            return [second_columns(i, u * BANK, (u + 1) * BANK, "y%d" % u) for u in range(S // BANK)]

        def halve_y(home, y):
            nc.scalar.activation(home, y, ACT.Copy, scale=0.5)

        def put_back(i, c0, c1, half_y):
            nc.vector.tensor_tensor(state[i][:].indirect(listed(c0, c1)), half_state[i][:, c0:c1], half_y, ALU.add)

        def store(i):
            nc.sync.dma_start(out[i * P : (i + 1) * P, :], state[i][:])

        def new_stage():
            return ring.tile([P, S + GROUPED], F32, name="stage", bufs=3, align_bytes=64)

        def nothing():
            return None

        plain_halves = halves[:, QUARTER : QUARTER + S]

        pick_words(0, picked_words[0][:], 0, S)
        pick_words(1, picked_words[1][:], 0, S)
        pick_scales(0, "picked_scales")
        first_home = held.tile([P, GROUPED], F32, name="first_home", align_bytes=64)
        for a in range(K_PASSES):
            cast_pass(0, first_home[:], a)
        last = K_PASSES - 1
        picked_words[last, 0] = held.tile([P, PASS], U32, name="picked_words2", align_bytes=64)[:]
        codes = ring.tile([P, K_PASSES * P], U32, name="contact_codes", bufs=3, align_bytes=64)
        scales = ring.tile([P, K_PASSES * P], U8, name="contact_scales", bufs=4, align_bytes=64)
        contact_mx[0] = (codes[:], scales)
        quantise_passes(0, first_home[:], 0, last)
        pick_words(last, picked_words[last, 0], 0, PASS)
        quantise_passes(0, first_home[:], last, K_PASSES)
        pick_scales(1, "contact_raw0")
        picked_words[last, 1] = held.tile([P, PASS], U32, name="first_home", align_bytes=64)[:]
        for c0 in range(0, PASS, QUARTER):
            pick_words(last, picked_words[last, 1][:, c0 : c0 + QUARTER], PASS + c0, PASS + c0 + QUARTER)
        sums = new_sums(0)
        for b in range(M_PASSES):
            for a in range(K_PASSES):
                for t in range(PACK):
                    first_pass(0, sums[b][t], a, b, t, a == 0 and t % 2 == 0, a == last and t % 2 == 1)
        freed = [held.tile([P, T], F32, name="table_words%d" % a, align_bytes=64) for a in range(K_PASSES)]
        half_state[0] = freed[0][:, :S]
        half_state[1] = freed[1][:, :S]
        half_state[2] = freed[2][:, :S]
        half_state[4] = freed[0][:, S:]
        half_state[5] = freed[1][:, S:]
        pick_state(0, 0, S, plain_halves)
        pick_state(1, 0, LEAD, lead_halves[:])
        pick_state(1, LEAD, S, plain_halves[:, LEAD:])
        stage = new_stage()
        make_h(0, sums, (stage[:, :QUARTER], stage[:, QUARTER:PASS]), (stage[:, PASS : PASS + QUARTER], halves[:, :QUARTER]), nothing, nothing, nothing)
        nc.scalar.copy(halves[:, QUARTER - RESTORED : QUARTER], plain_halves[:, :RESTORED])
        pick_state(2, 0, S, halves[:, QUARTER - RESTORED : QUARTER - RESTORED + S])
        cuts = (0, FIRST_PIECE, BANK, S)
        ys = [second_columns(0, cuts[k], cuts[k + 1], bank) for k, bank in enumerate(("spare0", "y0", "y1"))]
        both = homes["first_y"]
        halve_y(both[:, :FIRST_PIECE], ys[0][:])
        put_back(0, 0, FIRST_PIECE, both[:, :FIRST_PIECE])
        home = held.tile([P, GROUPED], F32, name="second_home", align_bytes=64)
        for a in range(K_PASSES):
            cast_pass(1, home[:], a)
        quantise_contact(1, home[:])
        sums = first_product(1)
        halve_y(both[:, FIRST_PIECE:BANK], ys[1][:])
        halve_y(both[:, BANK : S - HELD], ys[2][:, : BANK - HELD])
        halve_y(both[:, S - HELD : S], ys[2][:, BANK - HELD :])
        put_back(0, FIRST_PIECE, S, both[:, FIRST_PIECE:S])
        store(0)
        for a in range(K_PASSES):
            cast_pass(2, both[:, S : S + GROUPED], a)
        quantise_contact(2, both[:, S : S + GROUPED])
        half_state[3] = held.tile([P, S], F32, name="contact_raw2", align_bytes=64)[:]
        pick_state(3, 0, S, plain_halves)
        stage = new_stage()
        make_h(1, sums, (stage[:, :QUARTER], stage[:, QUARTER:PASS]), (stage[:, PASS : PASS + QUARTER], halves[:, QUARTER + S :]), nothing, nothing, nothing, (1, 0))
        nc.scalar.copy(halves[:, QUARTER + S : QUARTER + S + RESTORED], plain_halves[:, :RESTORED])
        for i in (4, 5):
            pick_state(i, 0, S, halves[:, QUARTER + RESTORED : QUARTER + RESTORED + S])

        for j in range(1, TILES - 1):
            sums = first_product(j + 1)
            ys = second_product(j)
            stage = new_stage()
            half_y = stage[:, :S]
            cast_home = stage[:, S:]
            cut = CUTS[j - 1]
            if j == 1:
                early_home = held.tile([P, GROUPED], F32, name="second_home", align_bytes=64)
                pairs0 = early_home[:, :QUARTER]
            else:
                pairs0 = held.tile([P, QUARTER], F32, name="pairs%d" % j, align_bytes=64)[:]

            def first_piece():
                halve_y(half_y[:, :BANK], ys[0][:])
                put_back(j, 0, cut, half_y[:, :cut])

            def next_contact():
                if j == 1:
                    cast_whole(3, early_home[:])
                    quantise_contact(3, early_home[:])
                elif j + 3 < TILES:
                    codes = held.tile([P, K_PASSES * P], U32, name="pairs%d" % j, align_bytes=64)
                    quantise_contact(j + 3, cast_homes[j + 3], codes=codes[:])

            def free_part():
                halve_y(half_y[:, BANK : S - HELD], ys[1][:, : BANK - HELD])

            make_h(j + 1, sums, (cast_home[:, QUARTER:PASS], cast_home[:, PASS:]), (pairs0, stage[:, S - HELD : S - HELD + QUARTER]), first_piece, next_contact, free_part, (1, 0))
            halve_y(half_y[:, S - HELD :], ys[1][:, BANK - HELD :])
            put_back(j, cut, S, half_y[:, cut:])
            store(j)
            if j == 1:
                cast_whole(4, cast_home)
                quantise_contact(4, cast_home)
                shared = held.tile([P, S + GROUPED], F32, name="contact_raw4", align_bytes=64)
                half_state[6] = shared[:, :S]
                cast_homes[5] = shared[:, S:]
                pick_state(6, 0, S, plain_halves)
                cast_whole(5, cast_homes[5])
            if j in (2, 3):
                cast_homes[j + 4] = cast_home
                cast_whole(j + 4, cast_home)
            if j + 4 < TILES:
                shared = held.tile([P, S + PASS], F32, name="contact_raw%d" % (j + 4), align_bytes=64)
                behind_cast[j + 2] = shared[:, S:]
            if j == 2:
                half_state[7] = shared[:, :S]
                pick_state(7, 0, S, plain_halves)
        ys = second_product(TILES - 1)
        both = freed[2][:, S:]
        for u in range(S // BANK):
            halve_y(both[:, u * BANK : (u + 1) * BANK], ys[u][:])
        put_back(TILES - 1, 0, S, both)
        store(TILES - 1)
